import numpy as np, ml_dtypes
CORES = [2,6,10,14,18,22,26,30]
N = 8
import mx_ref
BF = ml_dtypes.bfloat16
def gcols(t, e):
    v = np.concatenate([t.reshape(8, 16, -1, 4), np.zeros((8, 16, 1, 4), BF)], axis=2)
    return np.ascontiguousarray(np.stack([v[g][:, e[g]] for g in range(8)])).reshape(128, -1)
def tile(rs):
    return np.stack(rs, axis=2).reshape(128, -1).astype(BF)
def pick(q, e):
    c = np.concatenate([q[0].reshape(128, -1, 4), np.zeros((128, 1, 4), np.uint8)], axis=1); s = np.concatenate([q[1], np.ones((16, 1), np.uint8)], axis=1)
    return (np.ascontiguousarray(c[:, e].reshape(128, -1)), np.ascontiguousarray(s[:, e]))
def join(*qs):
    return (np.concatenate([q[0] for q in qs], axis=1), np.concatenate([q[1] for q in qs], axis=1))
def put(q, e, v):
    c, s = q[0].reshape(128, -1, 4).copy(), q[1].copy(); c[:, e] = v[0].reshape(128, -1, 4); s[:, e] = v[1]
    return (c.reshape(128, -1), s)
def pk(c, s):
    return (np.ascontiguousarray(c), mx_ref.live(s))
def emit(q):
    return q[0], q[1]
def packed(v, rng):
    q = [mx_ref.quantize(np.ascontiguousarray(v[r])) for r in range(N)]
    return np.stack([a for a, b in q]), np.stack([mx_ref.plane(b, rng) for a, b in q])
def values_of_codes():
    e, c = np.zeros((128, 128, 4), np.float32), np.zeros((128, 2, 4), np.uint8)
    e[np.arange(128), np.arange(128), 0] = 1
    c[:127, :, 0] = np.arange(256).reshape(2, 128).T[:127]
    return mx_ref.matmul(mx_ref.quantize(e.reshape(128, 512).astype(BF)), (c.reshape(128, 8), np.full((16, 2), 127, np.uint8))).T.reshape(-1).astype(np.float64)
CODE_VALUE, SCALE_VALUE = values_of_codes(), 2.0 ** (np.arange(256) - 127.0)
def decode(q):
    return (CODE_VALUE[q[0]].reshape(16, 8, -1, 4) * SCALE_VALUE[q[1]][:, None, :, None] + 0.0).reshape(128, -1).astype(np.float32)
def f(rng, *shape):
    return mx_ref.flush((rng.standard_normal(shape, dtype=np.float32) * np.exp2(rng.integers(-2, 3, shape[:-1] + (1,)))).astype(BF))
def wide(rng, *shape, cols=0):
    v = rng.standard_normal(shape, dtype=np.float32) * np.exp2(rng.integers(-12, 13, shape)).astype(np.float32)
    if cols: v *= np.repeat(np.exp2(rng.integers(-cols, cols + 1, shape[:-2] + (1, shape[-1] // 4))) * (rng.random(shape[:-2] + (1, shape[-1] // 4)) > 0.0625), 4, axis=-1).astype(np.float32)
    return mx_ref.flush(v.astype(BF))
C, K, E, R = 320, 64, 384, 3
def numbers_of(rng):
    return {"x": np.array(f(rng, N, 128, 4 * E)), "u": np.array(f(rng, N, 128, 512)), "v": np.array(f(rng, N, 128, 512))}
def layers(rng, still=[]):
    w = np.array(f(rng, N, 128, 2048)).reshape(N, 8, 16, 4, 8, 16, 4)
    for i in still:
        w[:, :, i] = 0
        w[:, :, :, :, :, i] = 0
    return w
def weights(rng, w):
    c, s = packed(np.ascontiguousarray(w).reshape(N, 128, 2048), rng)
    return {"wc": c, "ws": s}
def setup_inputs(rng):
    return {**numbers_of(rng), **weights(rng, layers(rng))}
def setup_inputs_ties(rng):
    d = numbers_of(rng)
    x = d["x"].reshape(N, 8, 16, E, 4)
    k = rng.integers(0, 4, (N, 8, E))
    k[:, :, C:] = rng.integers(-1, 5, (N, 8, K))
    x[:, :, 0] = 0
    x[:, :, 0, :, 0] = k.astype(np.float32).astype(BF)
    u = d["u"].reshape(N, 128, 128, 4)
    u[:, :, ::16] = 0
    o = rng.permutation(N)
    for r in range(N):
        for h in range(0, 128, 16): u[r, h, h, 0] = 0.0 if r == o[0] else -1.0 if r == o[1] else 1.0
    return {"x": x.reshape(N, 128, 4 * E), "u": u.reshape(N, 128, 512), "v": d["v"], **weights(rng, layers(rng, [0]))}
def close():
    t = np.zeros((128, 40, 4), np.float32)
    t[8, :, 0] = 1.96875
    t[9, :, 0] = (np.arange(8, 16) * np.exp2(-np.arange(14.0, 19.0))[:, None]).reshape(-1)
    once = decode(mx_ref.quantize(t.reshape(128, 160).astype(BF)))
    twice = decode(mx_ref.quantize(once.astype(BF)))[9, ::4]
    return max([np.unique(once[9, ::4][twice == k]) for k in twice], key=len)
def setup_inputs_edges(rng):
    d = numbers_of(rng)
    x = d["x"].astype(np.float32).reshape(N, 8, 16, E, 4)
    k = rng.integers(64, 192, (N, 8, E))
    k[:, :, :K // 2] = 200
    k[:, :, :C] = rng.permuted(k[:, :, :C], axis=2)
    for r in range(N):
        h = rng.permutation(8)
        for i in range(5): k[r, h[i], C:] = [255, 0, 199, 200, 128][i]
        k[r, h[5], C:] = rng.permutation(K) % 2 * 255
    b = np.arange(4)
    x[:, :, 0] = ((k[:, :, :, None] >> b) & 1) * np.exp2(b)
    x[:, :, 1] = ((k[:, :, :, None] >> (b + 4)) & 1) * np.exp2(b + 4)
    a = np.exp2(rng.integers(-14, -7, (N, 4, 8, E, 4))) * (1.0 + (2 * rng.integers(0, 64, (N, 4, 8, E, 4)) + 1) * 2.0 ** -7) * rng.choice([-1.0, 1.0], (N, 4, 8, E, 4))
    a[:, :, 0, :, 0] = 1.96875
    a[:, :, 1] = 0
    a[:, :, 1, :, 0] = rng.choice(close(), (N, 4, E))
    x[:, 4:, 8:] = a
    x[:, 0, 9] = 0
    u = d["u"].reshape(N, 128, 128, 4)
    u[:, :, ::16] = 0
    for h in range(0, 128, 16):
        u[:, h, h] = 1.0
        u[:, h + 1, h] = 1.0
    u[:, 9, 0, 0] = 2.0 ** 8
    w = layers(rng, [0, 1, 9])
    w[:, :, :, :, 4:, 8:] = 0
    return {"x": x.reshape(N, 128, 4 * E).astype(BF), "u": u.reshape(N, 128, 512), "v": d["v"], **weights(rng, w)}
def setup_inputs_near(rng):
    d = numbers_of(rng)
    x = d["x"].astype(np.float32).reshape(N, 8, 16, E, 4)
    x[:, :, 0] = 0
    x[:, :, 8:] = 0
    s = rng.integers(0, 256, (N, 8, E))
    b = np.arange(4)
    u = d["u"].reshape(N, 128, 128, 4)
    u[:, :, ::16] = 0
    o = rng.permutation(N) % 4
    for r in range(N):
        sign = rng.choice([-1.0, 1.0], (8, E))
        if o[r] < 2:
            x[r, :, 0, :, 0] = sign
            x[r, :, 11, :, 0] = 2.0 ** -10
            sign = np.ones((8, E))
        else:
            for g in rng.permutation(8)[:4]: x[r, g, 0, rng.integers(E), 0] = rng.choice([-1.0, 1.0]) * 2.0 ** 29
        least = -30.0 if o[r] == 2 else -23.0
        x[r, :, 8] = ((s[r, :, :, None] >> b) & 1) * np.exp2(b + least) * sign[:, :, None]
        x[r, :, 9] = ((s[r, :, :, None] >> (b + 4)) & 1) * np.exp2(b + 4 + least) * sign[:, :, None]
        k = 1.0 if o[r] == 0 else 2.0 ** -30
        for h in range(0, 128, 16):
            u[r, h, h, 0] = k
            u[r, h + 8, h] = k
            u[r, h + 9, h] = k
            u[r, h + 11, h, 0] = k
    return {"x": x.reshape(N, 128, 4 * E).astype(BF), "u": u.reshape(N, 128, 512), "v": d["v"], **weights(rng, layers(rng, [0, 8, 9, 10, 11, 12, 13, 14, 15]))}
def setup_inputs_huge(rng):
    d = numbers_of(rng)
    o = rng.permutation(N)
    c = rng.choice([-1.0, 1.0], (N, 8, 1, E, 1))
    u = d["u"].reshape(N, 128, 128, 4)
    u[:, :, ::16] = 0
    for r in range(N):
        a = (2.0 ** 30 * (1.0 - 0.1 * rng.random((128, 8, 4)))).astype(np.float32).astype(BF)
        if o[r] < N // 2:
            c[r] = c[r, :1].copy()
            u[r, :, ::16] = a
        else:
            c[r, rng.permutation(8)[:4]] = -1.0
            for g in range(8): u[r, 16 * g:16 * g + 16, 16 * g] = a[16 * g:16 * g + 16, g]
    x = c * (0.8 + 0.2 * rng.random((N, 8, 16, E, 4))) * 2.0 ** 30
    w = np.zeros((N, 128, 4, 128, 4), np.float32)
    i = np.arange(128)
    for b in range(4): w[:, i, b, i, b] = -2
    return {"x": x.astype(np.float32).reshape(N, 128, 4 * E).astype(BF), "u": u.reshape(N, 128, 512), "v": d["v"], **weights(rng, w.astype(BF))}
def setup_inputs_spread(rng):
    d = setup_inputs(rng)
    d["x"] = wide(rng, N, 128, 4 * E, cols=6)
    return d
def check_inputs(d):
    b = []
    for k in ("x", "u", "v"):
        a = np.abs(d[k].astype(np.float32))
        if not (np.isfinite(a).all() and ((a == 0) | (a >= 2.0 ** -30) & (a <= 2.0 ** 30)).all()): b.append("a value of " + k)
    none, least, most = [emit(mx_ref.quantize(np.full((128, 16), k, np.float32).astype(BF)))[1][0, 0] for k in (0.0, 2.0 ** -30, 2.0 ** 30)]
    for r in range(N):
        if ((d["wc"][r] == 0x7F) | (d["wc"][r] == 0xFF)).any(): b.append("wc: a code that is no number")
        s = mx_ref.live(d["ws"][r])
        if ((s != none) & ((s < least) | (s > most))).any(): b.append("ws: a scale out of range")
    return b
def reference(x, u, v, wc, ws):
    qu = [mx_ref.quantize(u[r]) for r in range(N)]
    lay = [pk(wc[r], ws[r]) for r in range(N)]
    now = [x[r] for r in range(N)]
    le = np.zeros((N, 8, E), np.float32)
    for t in range(R):
        made, sent = [], []
        for r in range(N):
            s = mx_ref.matmul(qu[r], mx_ref.quantize(now[r]))[::16] + np.float32(0.0)
            o = np.argsort(s[:, :C], axis=1, kind="stable")
            b = C + np.argsort(s[:, C:], axis=1, kind="stable")
            e = np.concatenate([o, b], axis=1)
            for g in range(8):
                k = np.searchsorted(s[g, o[g]], s[g, b[g]], side="right")
                p = np.maximum.accumulate(k - np.arange(K)) + np.arange(K)
                j = np.flatnonzero(p < C)
                e[g, p[j]] = b[g, j]
                e[g, C + j] = o[g, p[j]]
            le[r] = e
            z = gcols(now[r], e)
            q = mx_ref.quantize(z)
            m = tile([mx_ref.matmul(pick(lay[r], np.arange(128 * a, 128 * a + 128)), q) * np.float32(0.015625) + z[:, a::4].astype(np.float32) for a in range(4)]).reshape(8, 16, E, 4)
            made.append(m)
            sent.append(mx_ref.quantize(np.ascontiguousarray(m[7, :, C:].reshape(16, K // 8, 8, 4).transpose(2, 0, 1, 3)).reshape(128, -1)))
        now = []
        for r in range(N):
            came = decode(sent[(r - t - 1) % N]).astype(BF).reshape(8, 16, K // 8, 4).transpose(1, 2, 0, 3).reshape(1, 16, K, 4)
            wait = np.concatenate([came, made[r][:7, :, C:]])
            now.append(np.ascontiguousarray(np.concatenate([made[r][:, :, :C], wait], axis=2)).reshape(128, -1))
    y = np.zeros((N, 128, E), np.float32)
    oc, osc = np.zeros((N, 128, 4 * E), np.uint8), np.zeros((N, 16, E), np.uint8)
    for r in range(N):
        q = mx_ref.quantize(now[r])
        y[r] = mx_ref.matmul(mx_ref.quantize(v[r]), q)
        oc[r], osc[r] = emit(q)
    return {"y": y, "le": le, "oc": oc, "osc": osc}

@@ -1,0 +1,590 @@
+from concourse.mybir import dt, AluOpType, ActivationFunctionType
+
+C, K, E, R = 320, 64, 384, 3
+BIG = 1e29
+M = 16384.0
+F8, U8, U16, BF, F32, I32 = "float8_e4m3fn_x4", "uint8", "uint16", "bfloat16", "float32", "int32"
+
+
+def _sb(n, d):
+    return ("sbuf", [128, n], d)
+
+
+SCRATCH = {
+    "X": _sb(1792, BF), "Z": _sb(2048, BF), "Z64": _sb(1536, BF), "M64": _sb(1536, BF), "Xb2": _sb(256, BF),
+    "Mt": _sb(256, BF), "Bs": _sb(256, BF), "TT": _sb(64, BF), "TT2": _sb(32, BF), "Bt": _sb(512, BF),
+    "ub": _sb(512, BF), "vb": _sb(512, BF),
+    "qu": _sb(128, F8), "su": _sb(128, U8), "qus": _sb(128, F8), "sus": _sb(128, U8),
+    "qv": _sb(128, F8), "sv": _sb(128, U8), "qW": _sb(512, F8), "sW": _sb(512, U8),
+    "qx": _sb(448, F8), "sx": _sb(448, U8), "qz": _sb(448, F8), "sz": _sb(448, U8),
+    "CT": _sb(4096, BF), "qc": _sb(1024, F8), "sc": _sb(1024, U8),
+    "CK": _sb(1280, BF), "CKs": _sb(1280, BF), "qk": _sb(384, F8), "sk": _sb(384, U8),
+    "GI": _sb(512, BF), "GH": _sb(512, BF), "GT": _sb(512, BF), "qg": _sb(128, F8), "sg": _sb(128, U8),
+    "F0": _sb(512, BF), "F1": _sb(512, BF),
+    "qf0": _sb(128, F8), "sf0": _sb(128, U8), "qf1": _sb(128, F8), "sf1": _sb(128, U8),
+    "pk": _sb(192, F8), "ps": _sb(192, U8),
+    "Km": _sb(320, F32), "H": _sb(320, F32), "Kmw": _sb(64, F32), "Hw": _sb(64, F32),
+    "Ds": _sb(320, BF), "Dsg": _sb(1280, BF), "junk": _sb(3072, BF), "acc": _sb(20, F32),
+    "a1": _sb(20, F32), "a2": _sb(20, F32), "a4": _sb(20, F32),
+    "st": _sb(320, F32), "st4": _sb(320, F32), "O4": _sb(320, F32),
+    "Dr": _sb(264, BF), "Ar": _sb(264, BF), "Sr": _sb(264, BF), "accd": _sb(4, F32), "r1": _sb(4, F32),
+    "k4": _sb(64, F32), "ks4": _sb(64, F32), "B4": _sb(64, F32), "stb": _sb(64, F32),
+    "p4": _sb(64, F32), "f1": _sb(64, F32), "f2": _sb(64, F32), "f3": _sb(64, F32), "stp": _sb(64, F32),
+    "stl": _sb(64, F32), "LE": _sb(448, F32), "Lb": _sb(64, F32), "ysb": _sb(384, F32),
+    "oR": _sb(20, U16), "oZ": _sb(80, U16), "oW": _sb(4, U16), "oB": _sb(16, U16), "oP": _sb(16, U16),
+    "oL": _sb(4, U16), "oU": _sb(8, U16), "oS": _sb(16, U16), "oT": _sb(2, U16), "oD": _sb(8, U16),
+    "pI": _sb(8, I32), "pJ": _sb(8, I32), "PC": _sb(24, F32), "IU": _sb(640, F32), "IA": _sb(640, F32),
+    "IB": _sb(640, F32), "DD": _sb(640, F32), "Mn": _sb(320, F32), "Rst": _sb(320, F32), "Z16": _sb(320, BF),
+    "V4i": _sb(384, F32), "V4": _sb(384, F32), "IO": _sb(80, F32), "IP": _sb(32, F32),
+    "Ri": _sb(264, BF), "Rj": _sb(264, BF), "Fl": _sb(264, BF), "four": _sb(64, F32),
+}
+for _t in range(R):
+    SCRATCH["lq%d" % _t] = _sb(144, F8)
+    SCRATCH["ls%d" % _t] = _sb(144, U8)
+    SCRATCH["qb%d" % _t] = _sb(128, F8)
+    SCRATCH["sb%d" % _t] = _sb(128, U8)
+for _b in range(8):
+    SCRATCH["P%d" % _b] = ("psum", [128, 512], F32)
+
+NDMA = 28
+SEMAPHORES = ["eV", "eS", "eP", "eG", "sent", "arr0", "arr1", "arr2"] + ["d%d" % i for i in range(NDMA)]
+
+A = AluOpType
+AF = ActivationFunctionType
+S_FULL = (19, 18, 17)
+K_VEC = 12
+POST_S = 2
+NENG = 8
+TILE0 = (0, 320, 576, 768, 896)
+
+
+def _strip(s):
+    n = 20 - s
+    return n // 4, n % 4
+
+
+def rank_program(g, core, T, topo):
+    rank = T.rank_of(core)
+    if rank is None:
+        return
+    n_ranks = len(T.cores)
+    ops = []
+
+    def op(eng, fn, rd, wr, kind="c", info=None):
+        ops.append({"e": eng, "fn": fn, "rd": rd, "wr": wr, "k": kind, "info": info})
+
+    V, S, P = g.vector, g.scalar, g.tensor
+
+    def ts(out, in0, s1, s2, o0, o1, rd, wr):
+        if o1 is None:
+            op("V", lambda: V.tensor_scalar(out, in0, s1, None, o0), rd, wr)
+        else:
+            op("V", lambda: V.tensor_scalar(out, in0, s1, s2, o0, o1), rd, wr)
+
+    def tt(out, in0, in1, o, rd, wr):
+        op("V", lambda: V.tensor_tensor(out, in0, in1, o), rd, wr)
+
+    def cp(out, in_, rd, wr):
+        op("V", lambda: V.tensor_copy(out, in_), rd, wr)
+
+    def ms(ap, c, wr):
+        op("V", lambda: V.memset(ap, c), [], wr)
+
+    def scan(out, d0, d1, init, o0, o1, rd, wr):
+        op("V", lambda: V.tensor_tensor_scan(out, d0, d1, init, o0, o1), rd, wr)
+
+    def qz(q, s, in_, rd, wr):
+        op("V", lambda: V.quantize_mx(q, s, in_), rd, wr)
+
+    def tr(out, in_, rd, wr):
+        op("V", lambda: V.transpose(out, in_), rd, wr)
+
+    def act(out, in_, f, rd, wr, bias=None, scale=None, acc=None):
+        kw = {}
+        if bias is not None:
+            kw["bias"] = bias
+        if scale is not None:
+            kw["scale"] = scale
+        if acc is not None:
+            kw["accum_out"] = acc
+        op("S", lambda: S.activation(out, in_, f, **kw), rd, wr)
+
+    def mm(out, lq, ls, rq, rs, start, stop, rd, wr):
+        op("P", lambda: P.matmul_mx(out, lq, ls, rq, rs, start, stop), rd, wr)
+
+    def iota(out, pat, base, cm, wr, small=True):
+        if small:
+            op("G", lambda: g.iota(out, pat, base, cm, allow_small_or_imprecise_dtypes=True), [], wr)
+        else:
+            op("G", lambda: g.iota(out, pat, base, cm), [], wr)
+
+    def select(out, in_, pat, o, base, cm, rd, wr):
+        op("G", lambda: g.affine_select(out, in_, pat, o, 0.0, base, cm), rd, wr)
+
+    def dma(q, out, in_, rd, wr):
+        e = g.sync if q == "Y" else g.scalar
+        op(q, lambda: e.dma_start(out, in_), rd, wr, kind="d")
+
+    PC = T.PC
+
+    def pc(i):
+        return PC[:, i:i + 1]
+    Q_, R4, Q4, Q8, Q7, AA = range(6)
+    Q2, INV16, INV4, CQ, C1280, ZC, BOFF, INV64, CB, C320 = range(8, 18)
+    XW = ["Xws", "Xw0", "Xw1", "Xw2", "Xw3"]
+    XR = ["Xr0", "Xr1", "Xr2", "Xr3"]
+    ZT = ["C1", "C2", "C3", "C4", "CTz4"]
+    MA = ["Ma0", "Ma1", "Ma2", "Ma3"]
+
+    dma("S", T.ub[:], T.u[:], [], ["ub"])
+    dma("Y", T.X[:, 0:1280], T.x[:, 0:1280], [], XR)
+    dma("Y", T.X[:, 1280:1536], T.x[:, 1280:1536], ["Xr0"], XW)
+    dma("Y", T.qW[:].bitcast(dt.uint8), T.wc[:], [], ["qW"])
+    dma("Y", T.sW[:], T.ws[:], [], ["sW"])
+    dma("Y", T.vb[:], T.v[:], [], ["vb"])
+
+    ms(T.Z16[:], -1000.0, ["Z16"])
+    iota(T.pI[:], [[0, 8]], 0, 1, ["pI"], small=False)
+    iota(T.IO[:, 0:8], [[16, 8]], 0, 0, ["IOu"])
+    iota(T.IU[:, 0:320], [[0, 20], [1, 16]], 0, 0, ["IU16"])
+    iota(T.Z16[:, 0:320:16], [[16, 20]], -144, 0, ["Z16"])
+    iota(T.IU[:, 320:640], [[0, 80], [1, 4]], -2, 0, ["IU4"])
+    iota(T.acc[:], [[0, 20]], 0, 0, ["acc%d" % s for s in range(20)])
+    iota(T.GI[:], [[0, 512]], 1, 0, ["GI"])
+    select(T.GH[:], T.GI[:], [[-16, 8], [0, 64]], A.is_ge, 0, 1, ["GI"], ["GH"])
+    select(T.GT[:], T.GH[:], [[16, 8], [0, 64]], A.is_ge, 15, -1, ["GH"], ["GT"])
+    iota(T.V4i[:], [[4, 384]], 0, 0, ["V4i"])
+    iota(T.Ri[:], [[-16, 4], [1, 66]], 0, 0, ["Ri"])
+    iota(T.Dr[:, 64:264:66], [[32, 4]], 0, 0, ["Drc"])
+    iota(T.Dr[:, 65:264:66], [[0, 4]], 0, 0, ["Drd"])
+    iota(T.IO[:, 28:44], [[4, 8], [128, 2]], 0, 0, ["IOs"])
+    iota(T.IO[:, 44:46], [[32, 2]], 0, 0, ["IOt"])
+    iota(T.IO[:, 52:60], [[1, 2], [0, 4]], 0, 0, ["IOh"])
+    iota(T.IO[:, 60:68], [[0, 2], [2, 4]], -16, 0, ["IOd"])
+    iota(T.four[:], [[0, 64]], 4, 0, ["four"])
+    iota(T.Z[:, 0:256], [[0, 256]], 0, 0, ["Zz"])
+    iota(T.Bt[:], [[0, 512]], 0, 0, ["Bt", "Gser"])
+    for a in range(4):
+        for h, f in enumerate((T.F0, T.F1)):
+            select(f[32 * a:32 * a + 32, :], T.GI[32 * a:32 * a + 32, :], [[64, 4], [-1, 32], [-64, 4]], A.is_equal,
+                   -16 * h, 1, ["GI"], ["F%d%d" % (h, a), "Gser"])
+
+    for i, (sh, an) in enumerate(((0, 15), (0, 3), (2, 3), (3, 1), (0, 7), (5, 3))):
+        ts(T.pJ[:, i:i + 1], T.pI[:, i:i + 1], sh, an, A.logical_shift_right, A.bitwise_and, ["pI"], ["pJ%d" % i])
+    cp(T.oU[:], T.IO[:, 0:8], ["IOu"], ["oU"])
+    cp(PC[:, 0:6], T.pJ[:, 0:6], ["pJ%d" % i for i in range(6)], ["PC"])
+    ms(T.Rst[:], -BIG, ["Rst"])
+    ts(pc(Q2), pc(Q_), 2.0, None, A.add, None, ["PC"], ["q2"])
+    ms(T.CT[:, 4 * 896:4 * 1024], 0.0, ZT)
+    ms(T.Rst[:, 0:320:16], BIG, ["Rst"])
+    ms(T.X[:, 1536:1792], 0.0, ["Xz"])
+    act(T.IA[:, 0:320], T.IU[:, 0:320], AF.Abs, ["IU16", "PC"], ["IA16"], bias=pc(Q_), scale=-1.0)
+    act(T.Mn[:], T.IA[:, 0:320], AF.Identity, ["IA16"], ["Mn"], bias=-BIG, scale=2 * BIG)
+    act(T.IA[:, 0:320], T.IU[:, 0:320], AF.Relu, ["IU16", "q2"], ["IA16"], bias=pc(Q2), scale=-1.0)
+    act(T.IA[:, 320:640], T.IU[:, 320:640], AF.Relu, ["IU4", "PC"], ["IA4"], bias=pc(Q4), scale=-1.0)
+    act(T.IB[:], T.IA[:], AF.Relu, ["IA16", "IA4"], ["IB"], bias=2.0, scale=-1.0)
+    act(T.IA[:], T.IB[:], AF.Abs, ["IB"], ["IA16", "IA4"], bias=-(1.0 + 0.5 / M), scale=1.0)
+    act(T.DD[:], T.IA[:], AF.Identity, ["IA16", "IA4"], ["DD"], bias=M + 0.5, scale=-M)
+    for k in range(4):
+        a = TILE0[k + 1] - 64
+        ms(T.CT[:, 4 * a:4 * a + 256], 0.0, ["C%d" % s for s in range(21) if _strip(s)[0] == k])
+    zt = T.CT[:, 4 * 896:4 * 1024]
+    qz(T.qu[:], T.su[:], T.ub[:], ["ub"], ["qu"])
+    qz(T.qc[:, 896:1024], T.sc[:, 896:1024], zt, ZT, ["qc3", "qcz"])
+    cp(T.qus[:].bitcast(dt.uint32), T.qu[:].bitcast(dt.uint32).indirect(T.oU[:]), ["qu", "oU"], ["qus"])
+    cp(T.sus[:], T.su[:].indirect(T.oU[:]), ["qu", "oU"], ["sus"])
+    qz(T.qk[:, 256:384], T.sk[:, 256:384], zt, ZT, ["qk", "qkz"])
+    qz(T.pk[:, 64:192], T.ps[:, 64:192], zt, ZT, ["pk", "ps", "pkz"])
+    qz(T.lq0[:, 16:144], T.ls0[:, 16:144], zt, ZT, ["lz0"])
+
+    def consts_1():
+        for t in range(1, R):
+            qz(T["lq%d" % t][:, 16:144], T["ls%d" % t][:, 16:144], zt, ZT, ["lz%d" % t])
+
+    def consts_2():
+        qz(T.qg[:], T.sg[:], T.GT[:], ["GT"], ["qg"])
+
+    def consts_3():
+        ts(pc(INV16), pc(Q_), 15.0, 1.0 / M, A.is_equal, A.max, ["PC"], ["inv16"])
+        ts(pc(INV4), pc(Q4), 3.0, 1.0 / M, A.is_equal, A.max, ["PC"], ["inv4"])
+        ts(T.Rj[:], T.Ri[:], pc(Q_), 2.0, A.not_equal, A.mult, ["PC", "Ri"], ["Rj"])
+        act(pc(CQ), pc(Q_), AF.Identity, ["PC"], ["cq"], bias=159.02, scale=-1.0)
+        act(T.V4[:], T.V4i[:], AF.Identity, ["V4i", "PC"], ["V4"], bias=pc(R4), scale=1.0)
+        act(T.Fl[:], T.Rj[:], AF.Identity, ["Rj"], ["Fl"], bias=-1.0, scale=1.0)
+
+    def consts_4():
+        act(pc(C1280), pc(R4), AF.Identity, ["PC"], ["c1280"], bias=1280.0, scale=1.0)
+        act(pc(BOFF), pc(Q4), AF.Identity, ["PC"], ["boff"], bias=pc(R4), scale=32.0)
+        act(pc(ZC), pc(AA), AF.Identity, ["PC"], ["zc"], bias=pc(Q7), scale=-2.0)
+        act(T.IP[:, 8:16], T.IO[:, 60:68], AF.Identity, ["PC", "IOd"], ["IP1"], bias=pc(Q8), scale=1.0)
+
+    def consts_5():
+        act(pc(INV64), pc(INV16), AF.Copy, ["inv16"], ["inv64"], scale=0.25)
+        act(pc(CB), pc(R4), AF.Identity, ["PC"], ["cb"], bias=0.02, scale=-0.25)
+        act(pc(C320), pc(R4), AF.Identity, ["PC"], ["c320"], bias=320.0, scale=0.0)
+
+    first_fill = [
+        lambda: ts(T.oS[:], T.IO[:, 28:44], pc(BOFF), None, A.add, None, ["boff", "IOs"], ["oS"]),
+        lambda: ts(T.IP[:, 0:8], T.IO[:, 52:60], pc(ZC), None, A.is_equal, None, ["zc", "IOh"], ["IP0"]),
+        lambda: ts(T.oT[:], T.IO[:, 44:46], pc(Q_), 16.0, A.add, A.add, ["PC", "IOt"], ["oT"]),
+        lambda: tt(T.IP[:, 16:24], T.IP[:, 0:8], T.IP[:, 8:16], A.mult, ["IP0", "IP1"], ["IP2"]),
+        lambda: ts(T.oD[:], T.IP[:, 16:24], 16.0, None, A.add, None, ["IP2"], ["oD"]),
+    ]
+
+    def fill():
+        if first_fill:
+            first_fill.pop(0)()
+
+    def consts_6():
+        qz(T.qf0[:], T.sf0[:], T.F0[:], ["F00", "F01", "F02", "F03"], ["qf0"])
+        qz(T.qf1[:], T.sf1[:], T.F1[:], ["F10", "F11", "F12", "F13"], ["qf1"])
+
+    def q_rows():
+        qz(T.qx[:, 0:320], T.sx[:, 0:320], T.X[:, 0:1280], XR, ["qxr"])
+
+    def q_waits():
+        qz(T.qx[:, 320:448], T.sx[:, 320:448], T.X[:, 1280:1792], XW + ["Xz"], ["qxw"])
+
+    def pick_codes(t):
+        cp(T.pk[:, 0:128].bitcast(dt.uint32), T["lq%d" % t][:, 0:24].bitcast(dt.uint32).indirect(T.oD[:]),
+           ["land%d" % t, "lz%d" % t, "oD"], ["pk"])
+
+    def pick_scales(t):
+        act(T.ps[:, 0:128], T["ls%d" % t][:, 0:24].indirect(T.oD[:]), AF.Copy, ["land%d" % t, "lz%d" % t, "oD"], ["ps"])
+
+    def unpack_mm(bank):
+        o = T[bank][:, 0:128]
+        mm(o, T.qf0[:], T.sf0[:], T.pk[:, 0:128], T.ps[:, 0:128], True, False, ["qf0", "pk", "ps"], [bank])
+        mm(o, T.qf1[:], T.sf1[:], T.pk[:, 64:192], T.ps[:, 64:192], False, True, ["qf1", "pk", "ps", "pkz"], [bank])
+
+    def unpack_copy(b, on_vector=False):
+        if on_vector:
+            cp(T.X[0:16, 1280 + b:1536:4], T.P2[32 * b:32 * b + 16, 0:64], ["P2"], ["Xw%d" % b])
+        else:
+            act(T.X[0:16, 1280 + b:1536:4], T.P3[32 * b:32 * b + 16, 0:64], AF.Copy, ["P3"], ["Xw%d" % b])
+
+    def turn1():
+        for a in range(4):
+            tr(T.TT[32 * a:32 * a + 32, :], T.Bs[96:128, 64 * a:64 * a + 64], ["Bs"], ["TT%d" % a])
+        act(T.TT2[:], T.TT[:].indirect(T.oT[:]), AF.Copy, ["TT0", "TT1", "TT2", "TT3", "oT"], ["TU"])
+
+    def turn2():
+        tr(T.Bt[:, 0:32], T.TT2[:], ["TU"], ["Bt"])
+
+    def send(t):
+        qb, sb = T["qb%d" % t], T["sb%d" % t]
+        qz(qb[:], sb[:], T.Bt[:], ["Bt"], ["qb%d" % t])
+        dst = T.cores[(rank + t + 1) % n_ranks]
+        rid, pid, _ = topo.addr(dst)
+        m = sum(1 << e for e in topo.engines(core, dst)[0:NENG])
+        arr = T.sem["arr%d" % t]
+        op("G", lambda: g.remote_dma(T["lq%d" % t][:, 0:8].bitcast(dt.uint8), qb[:, 0:8].bitcast(dt.uint8), arr,
+                                     T.sem.sent, pid, rid, m), ["qb%d" % t], [], kind="r")
+        op("G", lambda: g.remote_dma(T["ls%d" % t][:, 0:8], sb[:, 0:8], arr, T.sem.sent, pid, rid, m),
+           ["qb%d" % t], [], kind="r")
+        op("X", None, [], ["land%d" % t], kind="x", info=("arr%d" % t, 2 * NENG))
+
+    def tail_post():
+        act(T.Mt[:], T.M64[:, 0:256], AF.Copy, MA, ["Mt"], scale=1.0 / 64)
+        dma("Y", T.X[16:128, 1280:1536], T.Mt[0:112, :], ["Mt"], ["Xws"])
+
+    def cview(s, n):
+        k, e = _strip(s)
+        a = 4 * TILE0[k] + e
+        return T.CT[:, a:4 * (TILE0[k] + n):4]
+
+    def kcol(s):
+        return T.H[:, 16 * s + 15:16 * s + 16]
+
+    q_rows()
+    for t in range(R):
+        last = t == R - 1
+        mm(T.P0[:, 0:320], T.qus[:], T.sus[:], T.qx[:, 0:320], T.sx[:, 0:320], True, True, ["qus", "sus", "qxr"], ["P0"])
+        mm(T.P1[:, 0:320], T.qus[:], T.sus[:], T.qx[:, 0:320], T.sx[:, 0:320], True, True, ["qus", "sus", "qxr"], ["P1"])
+        if t == 0:
+            consts_1()
+        else:
+            send(t - 1)
+            tail_post()
+            if t == 1:
+                consts_6()
+            else:
+                qz(T.qv[:], T.sv[:], T.vb[:], ["vb"], ["qv"])
+        h = 16 * min(S_FULL)
+        tt(T.Km[:, h:320], T.P0[:, h:320], T.Mn[:, h:320], A.max, ["P0", "Mn"], ["Km1"])
+        tt(T.Km[:, 0:h], T.P0[:, 0:h], T.Mn[:, 0:h], A.max, ["P0", "Mn"], ["Km"])
+        scan(T.H[:, h:320], T.Rst[:, h:320], T.Km[:, h:320], BIG, A.max, A.min, ["Rst", "Km1"], ["H1"])
+        scan(T.H[:, 0:h], T.Rst[:, 0:h], T.Km[:, 0:h], BIG, A.max, A.min, ["Rst", "Km"], ["H"])
+        jo = [0]
+        for i, s in enumerate(S_FULL):
+            d = T.Dsg[:, 320 * i:320 * i + 16 * s]
+            act(d, T.P1[:, 0:16 * s], AF.Sign, ["P1", "H1"], ["Dsg%d" % i], bias=kcol(s), scale=-1.0)
+        for i, s in enumerate(S_FULL):
+            d = T.Dsg[:, 320 * i:320 * i + 16 * s]
+            act(cview(s, 16 * s), d, AF.Relu, ["Dsg%d" % i], ["C%d" % s, "acc%d" % s], scale=-1.0, acc=T.acc[:, s:s + 1])
+
+        def strip(s):
+            if s in S_FULL:
+                return
+            ts(cview(s, 16 * s), T.P0[:, 0:16 * s], kcol(s), None, A.is_gt, None, ["P0", "H", "H1"], ["C%d" % s])
+            act(T.junk[:, jo[0]:jo[0] + 16 * s], cview(s, 16 * s), AF.Copy, ["C%d" % s], ["junk%d" % s, "acc%d" % s],
+                acc=T.acc[:, s:s + 1])
+            jo[0] += 16 * s
+
+        def q_tile(k, a, b, strips):
+            qz(T.qc[:, a:b], T.sc[:, a:b], T.CT[:, 4 * a:4 * b], ["C%d" % s for s in strips], ["qc%d" % k])
+
+        def sum_mm(k, n, rd):
+            a = TILE0[k]
+            mm(T.P2[:, 0:n], T.qg[:], T.sg[:], T.qc[:, a:a + n], T.sc[:, a:a + n], k == 0, k == 4, ["qg"] + rd, ["P2"])
+
+        for s in (19, 18, 17):
+            strip(s)
+        tt(cview(20, 320), T.H[:], T.P0[:, 0:320], A.is_le, ["H", "H1", "P0"], ["C20"])
+        strip(16)
+        scan(T.Ds[:], T.Z16[:], cview(20, 320), -1000.0, A.max, A.subtract, ["Z16", "C20"], ["Ds"])
+        for s in (15, 14, 13, 12):
+            strip(s)
+        if t == 0:
+            consts_2()
+        q_tile(0, 0, 320, (20, 19, 18, 17))
+        sum_mm(0, 320, ["qc0"])
+        q_tile(1, 320, 576, (16, 15, 14, 13))
+        sum_mm(1, 256, ["qc1"])
+        for s in (11, 10, 9, 8):
+            strip(s)
+        q_tile(2, 576, 768, (12, 11, 10, 9))
+        sum_mm(2, 192, ["qc2"])
+        for s in (7, 6, 5, 4, 3, 2, 1):
+            strip(s)
+        if t == 0:
+            q_waits()
+        q_tile(3, 768, 960, (8, 7, 6, 5, 4, 3, 2, 1))
+        sum_mm(3, 128, ["qc3"])
+        sum_mm(4, 128, ["qc3", "qcz"])
+        if t > 0:
+            pick_codes(t - 1)
+            pick_scales(t - 1)
+            unpack_mm("P3")
+            for b in range(4):
+                unpack_copy(b)
+        else:
+            consts_3()
+        scan(T.st[:], T.DD[:, 0:320], T.P2[:, 0:320], 0.0, A.mult, A.add, ["DD", "P2"], ["st"])
+        tt(T.a1[:], T.Ds[:, 15:320:16], T.acc[:], A.subtract, ["Ds"] + ["acc%d" % s for s in range(20)], ["a1"])
+        ts(T.a2[:], T.st[:, 15:320:16], pc(INV16), pc(CQ), A.mult, A.add, ["st", "inv16", "cq"], ["a2"])
+        tt(T.a4[:], T.a1[:], T.a2[:], A.add, ["a1", "a2"], ["a4"])
+        cp(T.oR[:], T.a4[:], ["a4"], ["oR"])
+        if t > 0:
+            q_waits()
+        else:
+            ms(T.Fl[:, 0:264:66], 0.0, ["Fl"])
+        mm(T.P4[:, 0:128], T.qus[:], T.sus[:], T.qx[:, 320:448], T.sx[:, 320:448], True, True, ["qus", "sus", "qxw"], ["P4"])
+        mm(T.P5[:, 0:128], T.qus[:], T.sus[:], T.qx[:, 320:448], T.sx[:, 320:448], True, True, ["qus", "sus", "qxw"], ["P5"])
+        for s in range(K_VEC, 20):
+            a = 256 * (s // 4) + s % 4
+            act(T.CKs[:, a:256 * (s // 4 + 1):4], T.P5[:, 0:64], AF.Sign, ["P5", "H", "H1"], ["CKs%d" % s],
+                bias=kcol(s), scale=-1.0)
+        act(T.CK[:, 64 * K_VEC:1280], T.CKs[:, 64 * K_VEC:1280], AF.Relu, ["CKs%d" % s for s in range(K_VEC, 20)], ["CKS"])
+        if t == 0:
+            consts_4()
+        cp(T.O4[:].indirect(T.oR[:]), T.V4[:, 0:320], ["oR", "V4"], ["O4"])
+        tt(T.Kmw[:], T.P4[:, 0:64], T.Mn[:, 0:64], A.max, ["P4", "Mn"], ["Kmw"])
+        scan(T.st4[:], T.DD[:, 320:640], T.O4[:], 0.0, A.mult, A.add, ["DD", "O4"], ["st4"])
+        scan(T.Hw[:], T.Rst[:, 0:64], T.Kmw[:], BIG, A.max, A.min, ["Rst", "Kmw"], ["Hw"])
+        ts(T.oZ[:], T.st4[:, 3:320:4], pc(INV4), 0.02, A.mult, A.add, ["st4", "inv4"], ["oZ"])
+        for s in range(4):
+            act(T.Dr[:, 66 * s:66 * s + 64], T.P5[:, 0:64], AF.Sign, ["P5", "Hw"], ["Dr%d" % s, "accd%d" % s],
+                bias=T.Hw[:, 16 * s + 15:16 * s + 16], scale=-1.0, acc=T.accd[:, s:s + 1])
+        act(T.Ar[:], T.Dr[:], AF.Abs, ["Dr0", "Dr1", "Dr2", "Dr3", "Drc", "Drd"], ["Ar"])
+        act(T.Z[:, 512:1792], T.X[:, 0:1280].indirect(T.oZ[:]), AF.Copy, XR + ["oZ"], ["Zr"])
+        for s in range(K_VEC):
+            a = 256 * (s // 4) + s % 4
+            ts(T.CK[:, a:256 * (s // 4 + 1):4], T.P4[:, 0:64], kcol(s), None, A.is_lt, None, ["P4", "H", "H1"], ["CK%d" % s])
+        qz(T.qk[:, 0:320], T.sk[:, 0:320], T.CK[:], ["CK%d" % s for s in range(K_VEC)] + ["CKS"], ["qk"])
+        for k in range(5):
+            mm(T.P6[:, 0:128], T.qg[:], T.sg[:], T.qk[:, 64 * k:64 * k + 128], T.sk[:, 64 * k:64 * k + 128],
+               k == 0, k == 4, ["qg", "qk", "qkz"], ["P6"])
+        scan(T.Sr[:], T.Fl[:], T.Ar[:], 0.0, A.mult, A.add, ["Fl", "Ar"], ["Sr"])
+        tt(T.r1[:], T.Sr[:, 65:264:66], T.accd[:], A.add, ["Sr", "accd0", "accd1", "accd2", "accd3"], ["r1"])
+        ts(T.oW[:], T.r1[:], 0.5, pc(Q_), A.mult, A.add, ["r1", "PC"], ["oW"])
+        ts(T.k4[:], T.P6[:, 0:64], -4.0, pc(C1280), A.mult, A.add, ["P6", "c1280"], ["k4"])
+        cp(T.B4[:].indirect(T.oW[:]), T.V4[:, 0:64], ["oW", "V4"], ["B4"])
+        cp(T.ks4[:].indirect(T.oW[:]), T.k4[:], ["oW", "k4"], ["ks4"])
+        scan(T.stb[:], T.DD[:, 320:384], T.B4[:], 0.0, A.mult, A.add, ["DD", "B4"], ["stb"])
+        scan(T.p4[:], T.four[:], T.ks4[:], -4.0, A.add, A.max, ["four", "ks4"], ["p4"])
+        ts(T.oB[:], T.stb[:, 3:64:4], pc(INV4), 0.02, A.mult, A.add, ["stb", "inv4"], ["oB"])
+        act(T.Z[:, 1792:2048], T.X[:, 1280:1536].indirect(T.oB[:]), AF.Copy, XW + ["oB"], ["Zb"])
+        ts(T.f1[:], T.p4[:], 1280.0, 256.0, A.is_ge, A.mult, ["p4"], ["f1"])
+        fill()
+        tt(T.f2[:], T.f1[:], T.p4[:], A.add, ["f1", "p4"], ["f2"])
+        fill()
+        tt(T.f3[:], T.f2[:], T.V4[:, 320:384], A.min, ["f2", "V4"], ["f3"])
+        fill()
+        scan(T.stp[:], T.DD[:, 320:384], T.f3[:], 0.0, A.mult, A.add, ["DD", "f3"], ["stp"])
+        fill()
+        cp(T.Xb2[:], T.Z[:, 1792:2048], ["Zb"], ["Xb2"])
+        ts(T.oP[:], T.stp[:, 3:64:4], pc(INV4), 0.02, A.mult, A.add, ["stp", "inv4"], ["oP"])
+        fill()
+        cp(T.Z[:, 256:384], T.Z[:, 512:2048].indirect(T.oP[:, 0:8]), ["Zr", "Zb", "oP"], ["Zt0"])
+        act(T.Z[:, 384:512], T.Z[:, 512:2048].indirect(T.oP[:, 8:16]), AF.Copy, ["Zr", "Zb", "oP"], ["Zt1"])
+        act(T.Z64[:, 0:256], T.Z[:, 256:512], AF.Copy, ["Zt0", "Zt1"], ["Ya"], scale=64.0)
+        qz(T.qz[:, 0:128], T.sz[:, 0:128], T.Z[:, 0:512], ["Zt0", "Zt1", "Zz"], ["qz1"])
+        for b in range(4):
+            w = slice(128 * b, 128 * b + 128)
+            mm(T["P%d" % b][:, 0:128], T.qW[:, w], T.sW[:, w], T.qz[:, 0:128], T.sz[:, 0:128], True, True,
+               ["qW", "sW", "qz1"], ["P%d" % b])
+
+        def place(a, b):
+            cp(T.Z[:, 512:2048].indirect(T.oP[:, a:b]), T.Xb2[:, 16 * a:16 * b], ["Xb2", "oP"], ["Zr", "Zb"])
+
+        def add1():
+            for b in range(4):
+                tt(T.M64[:, b:256:4], T["P%d" % b][:, 64:128], T.Z64[:, b:256:4], A.add, ["P%d" % b, "Ya"], ["Ma%d" % b])
+
+        def b_gather():
+            act(T.Bs[:], T.M64[:, 0:256].indirect(T.oS[:]), AF.Copy, MA + ["oS"], ["Bs"], scale=1.0 / 64)
+
+        def q_z():
+            qz(T.qz[:, 128:448], T.sz[:, 128:448], T.Z[:, 512:1792], ["Zr"], ["qz2"])
+            for b in range(4):
+                w = slice(128 * b, 128 * b + 128)
+                mm(T["P%d" % (4 + b)][:, 0:320], T.qW[:, w], T.sW[:, w], T.qz[:, 128:448], T.sz[:, 128:448], True, True,
+                   ["qW", "sW", "qz2"], ["P%d" % (4 + b)])
+
+        def pre(b):
+            act(T.Z64[:, 256 + b:1536:4], T.Z[:, 512 + b:1792:4], AF.Copy, ["Zr"], ["Y%d" % b], scale=64.0)
+
+        def add2(b):
+            tt(T.M64[:, 256 + b:1536:4], T["P%d" % (4 + b)][:, 0:320], T.Z64[:, 256 + b:1536:4], A.add,
+               ["P%d" % (4 + b), "Y%d" % b], ["Mb%d" % b])
+
+        def post(b):
+            if b < POST_S:
+                act(T.X[:, b:1280:4], T.M64[:, 256 + b:1536:4], AF.Copy, ["Mb%d" % b], ["Xr%d" % b], scale=1.0 / 64)
+            else:
+                ts(T.X[:, b:1280:4], T.M64[:, 256 + b:1536:4], 1.0 / 64, None, A.mult, None, ["Mb%d" % b], ["Xr%d" % b])
+
+        if last:
+            act(T.LE[:, 64:384], T.O4[:], AF.Copy, ["O4"], ["LEr"], scale=0.25)
+            scan(T.stl[:], T.DD[:, 0:64], T.f3[:], 0.0, A.mult, A.add, ["DD", "f3"], ["stl"])
+            add1()
+            b_gather()
+            place(0, 8)
+            turn1()
+            place(8, 16)
+            turn2()
+            send(t)
+            q_z()
+            pre(0)
+            tail_post()
+            ts(T.oL[:], T.stl[:, 15:64:16], pc(INV64), pc(CB), A.mult, A.add, ["stl", "inv64", "cb"], ["oL"])
+            for b in range(1, 4):
+                pre(b)
+            for b in range(4):
+                add2(b)
+            for b in range(4):
+                post(b)
+        else:
+            if t == 0:
+                consts_5()
+            place(0, 16)
+            q_z()
+            add1()
+            pre(0)
+            pre(1)
+            b_gather()
+            pre(2)
+            pre(3)
+            add2(0)
+            add2(1)
+            post(0)
+            turn1()
+            add2(2)
+            add2(3)
+            for b in range(1, 4):
+                post(b)
+            turn2()
+        q_rows()
+
+    dma("Y", T.oc[:, 0:1280], T.qx[:, 0:320].bitcast(dt.uint8), ["qxr"], [])
+    act(T.LE[:, 384:448], T.B4[:], AF.Identity, ["B4", "c320"], ["LEb"], bias=pc(C320), scale=0.25)
+    act(T.Lb[:], T.B4[:], AF.Identity, ["B4", "c320"], ["Lb"], bias=pc(C320), scale=0.25)
+    mm(T.P0[:, 0:320], T.qv[:], T.sv[:], T.qx[:, 0:320], T.sx[:, 0:320], True, True, ["qv", "qxr"], ["P0"])
+    act(T.ysb[:, 0:320], T.P0[:, 0:320], AF.Copy, ["P0"], ["y0"])
+    dma("Y", T.y[:, 0:320], T.ysb[:, 0:320], ["y0"], [])
+    pick_codes(R - 1)
+    pick_scales(R - 1)
+    unpack_mm("P3")
+    unpack_mm("P2")
+    cp(T.LE[:, 0:64], T.LE[:, 64:448].indirect(T.oL[:]), ["LEr", "LEb", "oL"], ["LEt"])
+    unpack_copy(0)
+    unpack_copy(1)
+    unpack_copy(2, True)
+    unpack_copy(3, True)
+    q_waits()
+    mm(T.P1[:, 0:128], T.qv[:], T.sv[:], T.qx[:, 320:448], T.sx[:, 320:448], True, True, ["qv", "qxw"], ["P1"])
+    cp(T.LE[:, 64:448].indirect(T.oL[:]), T.Lb[:], ["Lb", "oL"], ["LEr", "LEb"])
+    dma("Y", T.le[:, 320:384], T.LE[0:128:16, 0:64], ["LEt"], [])
+    dma("Y", T.oc[:, 1280:1536], T.qx[:, 320:384].bitcast(dt.uint8), ["qxw"], [])
+    for k in range(4):
+        dma("S", T.osc[4 * k:4 * k + 4, :], T.sx[32 * k:32 * k + 4, 0:384], ["qxr", "qxw"], [])
+    cp(T.ysb[:, 320:384], T.P1[:, 0:64], ["P1"], ["y1"])
+    dma("Y", T.y[:, 320:384], T.ysb[:, 320:384], ["y1"], [])
+    dma("Y", T.le[:, 0:320], T.LE[0:128:16, 64:384], ["LEr"], [])
+
+    writer, readers, deps = {}, {}, []
+    for i, o in enumerate(ops):
+        d = set()
+        for r in o["rd"]:
+            d.add(writer[r])
+        for w in o["wr"]:
+            if w in writer:
+                d.add(writer[w])
+            d.update(readers.get(w, []))
+        d.discard(i)
+        if o["e"] == "P":
+            d = set(j for j in d if ops[j]["e"] != "P")
+        deps.append(d)
+        for r in o["rd"]:
+            readers.setdefault(r, []).append(i)
+        for w in o["wr"]:
+            writer[w] = i
+            readers[w] = []
+    need = []
+    for i, o in enumerate(ops):
+        best = {}
+        for j in deps[i]:
+            key = ops[j]["e"] if ops[j]["k"] == "c" else j
+            best[key] = max(best.get(key, -1), j)
+        need.append(sorted(best.values()))
+    used = set(j for n in need for j in n)
+    queue = {"V": V, "S": S, "P": P, "G": g, "Y": g.sync}
+    token, count, waited, ndma = {}, {}, {}, [0]
+    for i, o in enumerate(ops):
+        if o["k"] == "x":
+            token[i] = o["info"]
+            count[o["info"][0]] = o["info"][1]
+            continue
+        q = queue[o["e"]]
+        for j in need[i]:
+            s, c = token[j]
+            if waited.get((o["e"], s), 0) < c:
+                q.wait_ge(T.sem[s], c)
+                waited[(o["e"], s)] = c
+        ins = o["fn"]()
+        if o["k"] == "d":
+            s = "d%d" % ndma[0]
+            ndma[0] += 1
+            ins.then_inc(T.sem[s], 16)
+            token[i] = (s, 16)
+            count[s] = 16
+        elif o["k"] == "c" and i in used:
+            s = "e" + o["e"]
+            count[s] = count.get(s, 0) + 1
+            ins.then_inc(T.sem[s], 1)
+            token[i] = (s, count[s])
+    count["sent"] = 2 * NENG * R
+    for s in sorted(count):
+        if max([waited.get((e, s), 0) for e in queue]) < count[s]:
+            g.wait_ge(T.sem[s], count[s])

@@ -3,6 +3,7 @@ from concourse.mybir import dt, AluOpType, ActivationFunctionType
 C, K, E, R = 320, 64, 384, 3
 BIG = 1e29
 M = 16384.0
+M4 = 8192.0
 F8, U8, U16, BF, F32, I32 = "float8_e4m3fn_x4", "uint8", "uint16", "bfloat16", "float32", "int32"
 
 
@@ -11,56 +12,101 @@ def _sb(n, d):
 
 
 SCRATCH = {
-    "X": _sb(1792, BF), "Z": _sb(2048, BF), "Z64": _sb(1536, BF), "M64": _sb(1536, BF), "Xb2": _sb(256, BF),
+    "X": _sb(1536, BF), "Z": _sb(1792, BF), "Z64": _sb(1536, BF), "M64": _sb(1536, BF),
     "Mt": _sb(256, BF), "Bs": _sb(256, BF), "TT": _sb(64, BF), "TT2": _sb(32, BF), "Bt": _sb(512, BF),
-    "ub": _sb(512, BF), "vb": _sb(512, BF),
+    "ub": _sb(512, BF), "vb": _sb(512, BF), "ZT": _sb(1024, BF),
     "qu": _sb(128, F8), "su": _sb(128, U8), "qus": _sb(128, F8), "sus": _sb(128, U8),
     "qv": _sb(128, F8), "sv": _sb(128, U8), "qW": _sb(512, F8), "sW": _sb(512, U8),
-    "qx": _sb(448, F8), "sx": _sb(448, U8), "qz": _sb(448, F8), "sz": _sb(448, U8),
-    "CT": _sb(4096, BF), "qc": _sb(1024, F8), "sc": _sb(1024, U8),
-    "CK": _sb(1280, BF), "CKs": _sb(1280, BF), "qk": _sb(384, F8), "sk": _sb(384, U8),
-    "GI": _sb(512, BF), "GH": _sb(512, BF), "GT": _sb(512, BF), "qg": _sb(128, F8), "sg": _sb(128, U8),
-    "F0": _sb(512, BF), "F1": _sb(512, BF),
-    "qf0": _sb(128, F8), "sf0": _sb(128, U8), "qf1": _sb(128, F8), "sf1": _sb(128, U8),
+    "qx": _sb(384, F8), "sx": _sb(384, U8), "qz": _sb(448, F8), "sz": _sb(448, U8),
+    "CT": _sb(5376, BF), "qc": _sb(1984, F8), "sc": _sb(1984, U8), "Dsg": _sb(6080, BF), "Dw": _sb(1024, BF),
+    "GI": _sb(512, BF), "GT": _sb(512, BF), "qg": _sb(128, F8), "sg": _sb(128, U8),
+    "J": _sb(512, BF), "JA": _sb(512, BF), "F": _sb(1024, BF), "qf": _sb(256, F8), "sf": _sb(256, U8),
     "pk": _sb(192, F8), "ps": _sb(192, U8),
     "Km": _sb(320, F32), "H": _sb(320, F32), "Kmw": _sb(64, F32), "Hw": _sb(64, F32),
-    "Ds": _sb(320, BF), "Dsg": _sb(1280, BF), "junk": _sb(3072, BF), "acc": _sb(20, F32),
-    "a1": _sb(20, F32), "a2": _sb(20, F32), "a4": _sb(20, F32),
-    "st": _sb(320, F32), "st4": _sb(320, F32), "O4": _sb(320, F32),
+    "Ds": _sb(320, BF), "acc": _sb(20, F32), "a1": _sb(20, F32), "a2": _sb(20, F32), "a4": _sb(20, F32),
+    "st": _sb(320, F32), "L": _sb(384, BF), "Lt": _sb(64, BF), "Bb": _sb(64, BF), "s4": _sb(320, BF), "s4t": _sb(64, BF),
     "Dr": _sb(264, BF), "Ar": _sb(264, BF), "Sr": _sb(264, BF), "accd": _sb(4, F32), "r1": _sb(4, F32),
-    "k4": _sb(64, F32), "ks4": _sb(64, F32), "B4": _sb(64, F32), "stb": _sb(64, F32),
-    "p4": _sb(64, F32), "f1": _sb(64, F32), "f2": _sb(64, F32), "f3": _sb(64, F32), "stp": _sb(64, F32),
-    "stl": _sb(64, F32), "LE": _sb(448, F32), "Lb": _sb(64, F32), "ysb": _sb(384, F32),
-    "oR": _sb(20, U16), "oZ": _sb(80, U16), "oW": _sb(4, U16), "oB": _sb(16, U16), "oP": _sb(16, U16),
-    "oL": _sb(4, U16), "oU": _sb(8, U16), "oS": _sb(16, U16), "oT": _sb(2, U16), "oD": _sb(8, U16),
-    "pI": _sb(8, I32), "pJ": _sb(8, I32), "PC": _sb(24, F32), "IU": _sb(640, F32), "IA": _sb(640, F32),
-    "IB": _sb(640, F32), "DD": _sb(640, F32), "Mn": _sb(320, F32), "Rst": _sb(320, F32), "Z16": _sb(320, BF),
-    "V4i": _sb(384, F32), "V4": _sb(384, F32), "IO": _sb(80, F32), "IP": _sb(32, F32),
-    "Ri": _sb(264, BF), "Rj": _sb(264, BF), "Fl": _sb(264, BF), "four": _sb(64, F32),
+    "kk": _sb(64, F32), "ks": _sb(64, F32), "pp": _sb(64, F32), "stl": _sb(64, F32),
+    "LE": _sb(384, F32), "ysb": _sb(384, F32),
+    "oR": _sb(20, U16), "oZ": _sb(80, U16), "oW": _sb(4, U16), "oT": _sb(16, U16), "oL": _sb(4, U16),
+    "oU": _sb(8, U16), "oS": _sb(16, U16), "oQ": _sb(2, U16), "oD": _sb(8, U16),
+    "pI": _sb(8, I32), "pJ": _sb(8, I32), "PC": _sb(32, F32), "IU": _sb(320, F32), "IA": _sb(320, F32),
+    "IB": _sb(320, F32), "IC": _sb(320, F32), "DD": _sb(320, F32), "Mn": _sb(320, F32), "Rst": _sb(320, BF),
+    "Z16": _sb(320, BF), "I4": _sb(320, BF), "D4": _sb(320, BF), "V16": _sb(384, BF), "IO": _sb(80, F32),
+    "IP": _sb(32, F32), "Ri": _sb(264, BF), "Rj": _sb(264, BF), "Fl": _sb(264, BF), "one": _sb(64, F32),
 }
 for _t in range(R):
-    SCRATCH["lq%d" % _t] = _sb(144, F8)
-    SCRATCH["ls%d" % _t] = _sb(144, U8)
+    SCRATCH["lq%d" % _t] = _sb(24, F8)
+    SCRATCH["ls%d" % _t] = _sb(24, U8)
     SCRATCH["qb%d" % _t] = _sb(128, F8)
     SCRATCH["sb%d" % _t] = _sb(128, U8)
 for _b in range(8):
     SCRATCH["P%d" % _b] = ("psum", [128, 512], F32)
 
-NDMA = 28
+NDMA = 48
 SEMAPHORES = ["eV", "eS", "eP", "eG", "sent", "arr0", "arr1", "arr2"] + ["d%d" % i for i in range(NDMA)]
 
 A = AluOpType
 AF = ActivationFunctionType
-S_FULL = (19, 18, 17)
-K_VEC = 12
-POST_S = 2
 NENG = 8
-TILE0 = (0, 320, 576, 768, 896)
+N_S = 6
+JOIN = (11, 15, 15)
+W_S = 0
+GATHER_BY = "VVSSS"
+CHUNKS = ((0, 320),)
+PRE_BY = ("VSSS", "VSSS")
+POST_BY = ("SSVV", "SSVV")
+J0 = (0, 64, 128, 192, 256)
+CT0 = (0, 320, 576, 768, 960)
+QC0 = (0, 1408, 1792, 512, 960)
+W0 = 1088
+FIX, WAKE, DMA, REMOTE, FIRST, GATHER, SCATTER, SLACK, AHEAD, PASSES = 48, 120, 2400, 3600, 1800, 1.56, 3.0, 150, 3.0, 4
+ORDER = []
 
 
-def _strip(s):
-    n = 20 - s
-    return n // 4, n % 4
+def list_order(eng, cost, before, way, ready):
+    n = len(eng)
+    later = [[] for _ in range(n)]
+    for i in range(n):
+        for j in before[i]:
+            later[j].append(i)
+    free, left, ready, order, end = {}, [len(d) for d in before], list(ready), [], [0.0] * n
+    pool = set(i for i in range(n) if not left[i])
+
+    def start(i):
+        return max(ready[i], free.get(eng[i], 0.0))
+    while pool:
+        first = min(pool, key=lambda i: (start(i), i))
+        e, now = eng[first], start(first)
+        i = max((i for i in pool if eng[i] == e and start(i) <= now + SLACK),
+                key=lambda i: (way[i] - AHEAD * (start(i) - now), -i))
+        end[i] = start(i) + cost[i]
+        if e != "X":
+            free[e] = end[i]
+        pool.remove(i)
+        order.append(i)
+        for k in later[i]:
+            ready[k] = max(ready[k], end[i] + before[k][i])
+            left[k] -= 1
+            if not left[k]:
+                pool.add(k)
+    return order, end
+
+
+def issue_order(eng, cost, tail, before):
+    n = len(eng)
+    after = [{} for _ in range(n)]
+    for i in range(n):
+        for j, lag in before[i].items():
+            after[j][i] = lag
+    back, best = [float(i) for i in range(n)], None
+    for _ in range(PASSES):
+        way = list_order(eng, cost, after, back, tail)[1]
+        order, back = list_order(eng, cost, before, way, [0.0] * n)
+        total = max(back[i] + tail[i] for i in range(n))
+        if best is None or total < best[0]:
+            best = (total, order)
+    return best[1]
 
 
 def rank_program(g, core, T, topo):
@@ -69,496 +115,435 @@ def rank_program(g, core, T, topo):
         return
     n_ranks = len(T.cores)
     ops = []
-
-    def op(eng, fn, rd, wr, kind="c", info=None):
-        ops.append({"e": eng, "fn": fn, "rd": rd, "wr": wr, "k": kind, "info": info})
-
     V, S, P = g.vector, g.scalar, g.tensor
 
-    def ts(out, in0, s1, s2, o0, o1, rd, wr):
+    def v(name, a=0, b=None, st=1, p=(0, 128), cast=None, by=None):
+        t = T[name]
+        if b is None:
+            b = t.shape[1]
+        ap = t[p[0]:p[1], a:b:st] if st > 1 else t[p[0]:p[1], a:b]
+        if cast is not None:
+            ap = ap.bitcast(cast)
+        m = ((1 << (b - a)) - 1) << a if st == 1 else sum(1 << i for i in range(a, b, st))
+        if SCRATCH[name][0] == "psum":
+            m, p = -1, (0, 128)
+        reg = [(name, m, p[0], p[1])]
+        n = len(range(a, b, st))
+        if by is not None:
+            ap = ap.indirect(by[0])
+            reg = reg + by[1]
+            n = 16 * by[2]
+        return (ap, reg, n, SCRATCH[name][2] == BF, by is not None)
+
+    def op(eng, fn, rd, wr, cycles, kind="c", info=None):
+        r, w = [], []
+        for x in rd:
+            if isinstance(x, tuple):
+                r += x[1]
+        for x in wr:
+            w.append(x[1][0])
+            r += x[1][1:]
+        ops.append({"e": eng, "fn": fn, "rd": r, "wr": w, "k": kind, "info": info, "c": cycles})
+
+    def a_(x):
+        return x[0] if isinstance(x, tuple) else x
+
+    def cyc(out, *ins, rate=None):
+        if out[4] or ins and ins[0][4]:
+            return FIX + out[2] * (SCATTER if out[4] else GATHER)
+        if rate is None:
+            rate = 0.5 if out[3] and all(x[3] for x in ins) else 1.0
+        return FIX + max(64, out[2] * rate)
+
+    def ts(out, in0, s1, s2, o0, o1=None):
         if o1 is None:
-            op("V", lambda: V.tensor_scalar(out, in0, s1, None, o0), rd, wr)
+            op("V", lambda: V.tensor_scalar(out[0], in0[0], a_(s1), None, o0), [in0, s1], [out], cyc(out, in0))
         else:
-            op("V", lambda: V.tensor_scalar(out, in0, s1, s2, o0, o1), rd, wr)
+            op("V", lambda: V.tensor_scalar(out[0], in0[0], a_(s1), a_(s2), o0, o1), [in0, s1, s2], [out], cyc(out, in0))
 
-    def tt(out, in0, in1, o, rd, wr):
-        op("V", lambda: V.tensor_tensor(out, in0, in1, o), rd, wr)
+    def tt(out, in0, in1, o):
+        op("V", lambda: V.tensor_tensor(out[0], in0[0], in1[0], o), [in0, in1], [out],
+           cyc(out, in0, rate=1.0 if in0[1][0][1] == -1 else 2.0))
 
-    def cp(out, in_, rd, wr):
-        op("V", lambda: V.tensor_copy(out, in_), rd, wr)
+    def cp(out, in_):
+        op("V", lambda: V.tensor_copy(out[0], in_[0]), [in_], [out], cyc(out, in_))
 
-    def ms(ap, c, wr):
-        op("V", lambda: V.memset(ap, c), [], wr)
+    def ms(out, c):
+        op("V", lambda: V.memset(out[0], c), [], [out], cyc(out))
 
-    def scan(out, d0, d1, init, o0, o1, rd, wr):
-        op("V", lambda: V.tensor_tensor_scan(out, d0, d1, init, o0, o1), rd, wr)
+    def scan(out, d0, d1, init, o0, o1):
+        op("V", lambda: V.tensor_tensor_scan(out[0], d0[0], d1[0], init, o0, o1), [d0, d1], [out], cyc(out, d0, d1))
 
-    def qz(q, s, in_, rd, wr):
-        op("V", lambda: V.quantize_mx(q, s, in_), rd, wr)
+    def qz(q, s, a, b, in_):
+        qq, ss = v(q, a, b), v(s, a, b)
+        op("V", lambda: V.quantize_mx(qq[0], ss[0], in_[0]), [in_], [qq, ss], FIX + 15 + 0.265 * in_[2])
 
-    def tr(out, in_, rd, wr):
-        op("V", lambda: V.transpose(out, in_), rd, wr)
+    def tr(out, in_):
+        op("V", lambda: V.transpose(out[0], in_[0]), [in_], [out], cyc(out, in_))
 
-    def act(out, in_, f, rd, wr, bias=None, scale=None, acc=None):
+    def act(out, in_, f, bias=None, scale=None, acc=None):
         kw = {}
         if bias is not None:
-            kw["bias"] = bias
+            kw["bias"] = a_(bias)
         if scale is not None:
-            kw["scale"] = scale
+            kw["scale"] = a_(scale)
         if acc is not None:
-            kw["accum_out"] = acc
-        op("S", lambda: S.activation(out, in_, f, **kw), rd, wr)
+            kw["accum_out"] = acc[0]
+        op("S", lambda: S.activation(out[0], in_[0], f, **kw), [in_, bias, scale], [out] + ([acc] if acc else []),
+           cyc(out, in_, rate=1.0) + (24 if acc else 0))
 
-    def mm(out, lq, ls, rq, rs, start, stop, rd, wr):
-        op("P", lambda: P.matmul_mx(out, lq, ls, rq, rs, start, stop), rd, wr)
-
-    def iota(out, pat, base, cm, wr, small=True):
-        if small:
-            op("G", lambda: g.iota(out, pat, base, cm, allow_small_or_imprecise_dtypes=True), [], wr)
+    def move(by, out, in_, scale=None):
+        if by == "S":
+            act(out, in_, AF.Copy, scale=scale)
+        elif scale is None:
+            cp(out, in_)
         else:
-            op("G", lambda: g.iota(out, pat, base, cm), [], wr)
+            ts(out, in_, scale, None, A.mult)
 
-    def select(out, in_, pat, o, base, cm, rd, wr):
-        op("G", lambda: g.affine_select(out, in_, pat, o, 0.0, base, cm), rd, wr)
+    def mm(bank, lq, ls, la, rq, rs, a, n, group=None):
+        o, w = T[bank][:, 0:n], [v(lq, la, la + 128), v(ls, la, la + 128), v(rq, a, a + n), v(rs, a, a + n)]
 
-    def dma(q, out, in_, rd, wr):
+        def fn():
+            start, stop = group is None or group[0]["fn"] is fn, group is None or group[-1]["fn"] is fn
+            return P.matmul_mx(o, w[0][0], w[1][0], w[2][0], w[3][0], start, stop)
+        op("P", fn, w, [v(bank)], FIX + n, info=group)
+
+    def iota(out, pat, base, cm=0, small=True):
+        if small:
+            op("G", lambda: g.iota(out[0], pat, base, cm, allow_small_or_imprecise_dtypes=True), [], [out], 160 + 2 * out[2])
+        else:
+            op("G", lambda: g.iota(out[0], pat, base, cm), [], [out], 160 + 2 * out[2])
+
+    def dma(q, out, in_, after=()):
         e = g.sync if q == "Y" else g.scalar
-        op(q, lambda: e.dma_start(out, in_), rd, wr, kind="d")
+        op(q, lambda: e.dma_start(a_(out), a_(in_)), [in_] + list(after), [out] if isinstance(out, tuple) else [], 70,
+           kind="d")
 
-    PC = T.PC
+    names = ("q", "r", "q8", "aa", "b2", "g", "p", "q2", "e15", "inv16", "m16", "cq", "cqm", "q4", "nq4", "q7", "t1", "t2",
+             "inv4", "c768", "boff", "zc", "a32", "n0", "n1", "c192", "c320")
 
-    def pc(i):
-        return PC[:, i:i + 1]
-    Q_, R4, Q4, Q8, Q7, AA = range(6)
-    Q2, INV16, INV4, CQ, C1280, ZC, BOFF, INV64, CB, C320 = range(8, 18)
-    XW = ["Xws", "Xw0", "Xw1", "Xw2", "Xw3"]
-    XR = ["Xr0", "Xr1", "Xr2", "Xr3"]
-    ZT = ["C1", "C2", "C3", "C4", "CTz4"]
-    MA = ["Ma0", "Ma1", "Ma2", "Ma3"]
+    def pc(name):
+        i = names.index(name)
+        return v("PC", i, i + 1)
 
-    dma("S", T.ub[:], T.u[:], [], ["ub"])
-    dma("Y", T.X[:, 0:1280], T.x[:, 0:1280], [], XR)
-    dma("Y", T.X[:, 1280:1536], T.x[:, 1280:1536], ["Xr0"], XW)
-    dma("Y", T.qW[:].bitcast(dt.uint8), T.wc[:], [], ["qW"])
-    dma("Y", T.sW[:], T.ws[:], [], ["sW"])
-    dma("Y", T.vb[:], T.v[:], [], ["vb"])
+    def col(name, src, scale, bias, f=AF.Identity):
+        act(pc(name), pc(src), f, bias=bias, scale=scale)
 
-    ms(T.Z16[:], -1000.0, ["Z16"])
-    iota(T.pI[:], [[0, 8]], 0, 1, ["pI"], small=False)
-    iota(T.IO[:, 0:8], [[16, 8]], 0, 0, ["IOu"])
-    iota(T.IU[:, 0:320], [[0, 20], [1, 16]], 0, 0, ["IU16"])
-    iota(T.Z16[:, 0:320:16], [[16, 20]], -144, 0, ["Z16"])
-    iota(T.IU[:, 320:640], [[0, 80], [1, 4]], -2, 0, ["IU4"])
-    iota(T.acc[:], [[0, 20]], 0, 0, ["acc%d" % s for s in range(20)])
-    iota(T.GI[:], [[0, 512]], 1, 0, ["GI"])
-    select(T.GH[:], T.GI[:], [[-16, 8], [0, 64]], A.is_ge, 0, 1, ["GI"], ["GH"])
-    select(T.GT[:], T.GH[:], [[16, 8], [0, 64]], A.is_ge, 15, -1, ["GH"], ["GT"])
-    iota(T.V4i[:], [[4, 384]], 0, 0, ["V4i"])
-    iota(T.Ri[:], [[-16, 4], [1, 66]], 0, 0, ["Ri"])
-    iota(T.Dr[:, 64:264:66], [[32, 4]], 0, 0, ["Drc"])
-    iota(T.Dr[:, 65:264:66], [[0, 4]], 0, 0, ["Drd"])
-    iota(T.IO[:, 28:44], [[4, 8], [128, 2]], 0, 0, ["IOs"])
-    iota(T.IO[:, 44:46], [[32, 2]], 0, 0, ["IOt"])
-    iota(T.IO[:, 52:60], [[1, 2], [0, 4]], 0, 0, ["IOh"])
-    iota(T.IO[:, 60:68], [[0, 2], [2, 4]], -16, 0, ["IOd"])
-    iota(T.four[:], [[0, 64]], 4, 0, ["four"])
-    iota(T.Z[:, 0:256], [[0, 256]], 0, 0, ["Zz"])
-    iota(T.Bt[:], [[0, 512]], 0, 0, ["Bt", "Gser"])
-    for a in range(4):
-        for h, f in enumerate((T.F0, T.F1)):
-            select(f[32 * a:32 * a + 32, :], T.GI[32 * a:32 * a + 32, :], [[64, 4], [-1, 32], [-64, 4]], A.is_equal,
-                   -16 * h, 1, ["GI"], ["F%d%d" % (h, a), "Gser"])
+    def cview(s, a, b):
+        k, e = (s + 1) // 4, (s + 1) % 4
+        w = CT0[k] - J0[k]
+        return v("CT", 4 * (w + a) + e, 4 * (w + b), 4)
 
-    for i, (sh, an) in enumerate(((0, 15), (0, 3), (2, 3), (3, 1), (0, 7), (5, 3))):
-        ts(T.pJ[:, i:i + 1], T.pI[:, i:i + 1], sh, an, A.logical_shift_right, A.bitwise_and, ["pI"], ["pJ%d" % i])
-    cp(T.oU[:], T.IO[:, 0:8], ["IOu"], ["oU"])
-    cp(PC[:, 0:6], T.pJ[:, 0:6], ["pJ%d" % i for i in range(6)], ["PC"])
-    ms(T.Rst[:], -BIG, ["Rst"])
-    ts(pc(Q2), pc(Q_), 2.0, None, A.add, None, ["PC"], ["q2"])
-    ms(T.CT[:, 4 * 896:4 * 1024], 0.0, ZT)
-    ms(T.Rst[:, 0:320:16], BIG, ["Rst"])
-    ms(T.X[:, 1536:1792], 0.0, ["Xz"])
-    act(T.IA[:, 0:320], T.IU[:, 0:320], AF.Abs, ["IU16", "PC"], ["IA16"], bias=pc(Q_), scale=-1.0)
-    act(T.Mn[:], T.IA[:, 0:320], AF.Identity, ["IA16"], ["Mn"], bias=-BIG, scale=2 * BIG)
-    act(T.IA[:, 0:320], T.IU[:, 0:320], AF.Relu, ["IU16", "q2"], ["IA16"], bias=pc(Q2), scale=-1.0)
-    act(T.IA[:, 320:640], T.IU[:, 320:640], AF.Relu, ["IU4", "PC"], ["IA4"], bias=pc(Q4), scale=-1.0)
-    act(T.IB[:], T.IA[:], AF.Relu, ["IA16", "IA4"], ["IB"], bias=2.0, scale=-1.0)
-    act(T.IA[:], T.IB[:], AF.Abs, ["IB"], ["IA16", "IA4"], bias=-(1.0 + 0.5 / M), scale=1.0)
-    act(T.DD[:], T.IA[:], AF.Identity, ["IA16", "IA4"], ["DD"], bias=M + 0.5, scale=-M)
-    for k in range(4):
-        a = TILE0[k + 1] - 64
-        ms(T.CT[:, 4 * a:4 * a + 256], 0.0, ["C%d" % s for s in range(21) if _strip(s)[0] == k])
-    zt = T.CT[:, 4 * 896:4 * 1024]
-    qz(T.qu[:], T.su[:], T.ub[:], ["ub"], ["qu"])
-    qz(T.qc[:, 896:1024], T.sc[:, 896:1024], zt, ZT, ["qc3", "qcz"])
-    cp(T.qus[:].bitcast(dt.uint32), T.qu[:].bitcast(dt.uint32).indirect(T.oU[:]), ["qu", "oU"], ["qus"])
-    cp(T.sus[:], T.su[:].indirect(T.oU[:]), ["qu", "oU"], ["sus"])
-    qz(T.qk[:, 256:384], T.sk[:, 256:384], zt, ZT, ["qk", "qkz"])
-    qz(T.pk[:, 64:192], T.ps[:, 64:192], zt, ZT, ["pk", "ps", "pkz"])
-    qz(T.lq0[:, 16:144], T.ls0[:, 16:144], zt, ZT, ["lz0"])
+    def kcol(s):
+        return v("H", 16 * s + 15, 16 * s + 16)
 
-    def consts_1():
-        for t in range(1, R):
-            qz(T["lq%d" % t][:, 16:144], T["ls%d" % t][:, 16:144], zt, ZT, ["lz%d" % t])
+    rows = v("X", 0, 4 * C)
+    dma("S", v("ub"), T.u[:])
+    dma("Y", rows, T.x[:, 0:4 * C])
+    dma("Y", v("X", 4 * C, 4 * E), T.x[:, 4 * C:4 * E], [rows])
+    dma("Y", v("qW", cast=dt.uint8), T.wc[:], [rows])
+    dma("Y", v("sW"), T.ws[:], [rows])
+    dma("Y", v("vb"), T.v[:], [rows])
 
-    def consts_2():
-        qz(T.qg[:], T.sg[:], T.GT[:], ["GT"], ["qg"])
-
-    def consts_3():
-        ts(pc(INV16), pc(Q_), 15.0, 1.0 / M, A.is_equal, A.max, ["PC"], ["inv16"])
-        ts(pc(INV4), pc(Q4), 3.0, 1.0 / M, A.is_equal, A.max, ["PC"], ["inv4"])
-        ts(T.Rj[:], T.Ri[:], pc(Q_), 2.0, A.not_equal, A.mult, ["PC", "Ri"], ["Rj"])
-        act(pc(CQ), pc(Q_), AF.Identity, ["PC"], ["cq"], bias=159.02, scale=-1.0)
-        act(T.V4[:], T.V4i[:], AF.Identity, ["V4i", "PC"], ["V4"], bias=pc(R4), scale=1.0)
-        act(T.Fl[:], T.Rj[:], AF.Identity, ["Rj"], ["Fl"], bias=-1.0, scale=1.0)
-
-    def consts_4():
-        act(pc(C1280), pc(R4), AF.Identity, ["PC"], ["c1280"], bias=1280.0, scale=1.0)
-        act(pc(BOFF), pc(Q4), AF.Identity, ["PC"], ["boff"], bias=pc(R4), scale=32.0)
-        act(pc(ZC), pc(AA), AF.Identity, ["PC"], ["zc"], bias=pc(Q7), scale=-2.0)
-        act(T.IP[:, 8:16], T.IO[:, 60:68], AF.Identity, ["PC", "IOd"], ["IP1"], bias=pc(Q8), scale=1.0)
-
-    def consts_5():
-        act(pc(INV64), pc(INV16), AF.Copy, ["inv16"], ["inv64"], scale=0.25)
-        act(pc(CB), pc(R4), AF.Identity, ["PC"], ["cb"], bias=0.02, scale=-0.25)
-        act(pc(C320), pc(R4), AF.Identity, ["PC"], ["c320"], bias=320.0, scale=0.0)
-
-    first_fill = [
-        lambda: ts(T.oS[:], T.IO[:, 28:44], pc(BOFF), None, A.add, None, ["boff", "IOs"], ["oS"]),
-        lambda: ts(T.IP[:, 0:8], T.IO[:, 52:60], pc(ZC), None, A.is_equal, None, ["zc", "IOh"], ["IP0"]),
-        lambda: ts(T.oT[:], T.IO[:, 44:46], pc(Q_), 16.0, A.add, A.add, ["PC", "IOt"], ["oT"]),
-        lambda: tt(T.IP[:, 16:24], T.IP[:, 0:8], T.IP[:, 8:16], A.mult, ["IP0", "IP1"], ["IP2"]),
-        lambda: ts(T.oD[:], T.IP[:, 16:24], 16.0, None, A.add, None, ["IP2"], ["oD"]),
-    ]
-
-    def fill():
-        if first_fill:
-            first_fill.pop(0)()
-
-    def consts_6():
-        qz(T.qf0[:], T.sf0[:], T.F0[:], ["F00", "F01", "F02", "F03"], ["qf0"])
-        qz(T.qf1[:], T.sf1[:], T.F1[:], ["F10", "F11", "F12", "F13"], ["qf1"])
+    iota(v("pI"), [[0, 8]], 0, 1, small=False)
+    iota(v("IU"), [[0, 20], [1, 16]], 0)
+    iota(v("IO", 0, 8), [[16, 8]], 0)
+    iota(v("GI"), [[1, 8], [0, 64]], 0)
+    ms(v("ZT"), 0.0)
+    for i, (sh, an) in enumerate(((0, 15), (0, 3), (3, 1), (5, 3), (2, 1), (4, 7))):
+        ts(v("pJ", i, i + 1), v("pI", i, i + 1), sh, an, A.logical_shift_right, A.bitwise_and)
+    cp(pc("q"), v("pJ", 0, 1))
+    cp(v("PC", 1, 6), v("pJ", 1, 6))
+    cp(v("oU"), v("IO", 0, 8))
+    ms(v("Rst"), BIG)
+    ms(v("Rst", 0, C, 16), -BIG)
+    ms(v("Z16"), -1000.0)
+    iota(v("Z16", 0, C, 16), [[16, 20]], -144)
+    iota(v("acc"), [[0, 20]], 0)
+    iota(v("Ri"), [[-16, 4], [1, 66]], 0)
+    iota(v("Dr", 64, 264, 66), [[32, 4]], 0)
+    iota(v("Dr", 65, 264, 66), [[0, 4]], 0)
+    iota(v("V16"), [[1, 384]], -192)
+    iota(v("one"), [[0, 64]], 1)
+    iota(v("I4"), [[0, 80], [1, 4]], 0)
+    iota(pc("p"), [[0, 1]], 0, 1)
+    iota(v("J"), [[64, 4], [1, 32], [-64, 4]], 0)
+    iota(v("IO", 28, 44), [[4, 8], [128, 2]], 0)
+    iota(v("IO", 44, 46), [[32, 2]], 0)
+    iota(v("IO", 52, 60), [[1, 2], [0, 4]], 0)
+    iota(v("IO", 60, 68), [[0, 2], [2, 4]], -16)
+    act(v("IC"), v("IU"), AF.Abs, bias=pc("q"), scale=-1.0)
+    act(v("Mn"), v("IC"), AF.Identity, bias=BIG, scale=-2 * BIG)
+    col("q2", "q", 1.0, 2.0)
+    act(v("IA"), v("IU"), AF.Relu, bias=pc("q2"), scale=-1.0)
+    act(v("IB"), v("IA"), AF.Relu, bias=2.0, scale=-1.0)
+    act(v("IA"), v("IB"), AF.Abs, bias=-(1.0 + 0.5 / M), scale=1.0)
+    act(v("DD"), v("IA"), AF.Identity, bias=M + 0.5, scale=-M)
+    col("e15", "q", 1.0, -14.0, AF.Relu)
+    col("cq", "q", 1.0, 144.15)
+    col("m16", "e15", 1.0 - M, M)
+    col("inv16", "e15", 1.0 - 1.0 / M, 1.0 / M)
+    act(pc("cqm"), pc("cq"), AF.Copy, scale=pc("m16"))
+    col("q4", "q8", 2.0, pc("b2"))
+    col("t1", "q8", M4 * M4 - 1.0, 1.0)
+    col("t2", "b2", (M4 - 1.0) * 4.0 / M4 ** 3, 4.0 / M4 ** 3)
+    act(pc("inv4"), pc("t1"), AF.Copy, scale=pc("t2"))
+    col("nq4", "q4", -1.0, -0.5)
+    col("c768", "r", 1.0, 768.0)
+    col("c192", "r", 0.0, 192.0)
+    col("c320", "r", 0.0, 320.0)
+    act(v("I4"), v("I4"), AF.Sign, bias=pc("nq4"), scale=1.0)
+    act(v("D4"), v("I4"), AF.Identity, bias=M4 / 2, scale=M4 / 2)
+    ts(v("Rj"), v("Ri"), pc("q"), 2.0, A.not_equal, A.mult)
+    act(v("Fl"), v("Rj"), AF.Identity, bias=-1.0, scale=1.0)
+    act(v("Fl", 0, 264, 66), v("Rj", 0, 264, 66), AF.Copy, scale=0.0)
+    zq = QC0[4] - J0[4]
+    qz("qc", "sc", zq, zq + 256, v("ZT"))
+    for k in range(5):
+        dma("Y", v("CT", 4 * CT0[k], 4 * CT0[k] + 192), v("ZT", 0, 192))
+    for q_, s_, a, n in [("qc", "sc", QC0[k] - n, n) for k, n in ((1, 128), (2, 128), (3, 192))] + [("pk", "ps", 128, 64)] + [
+            ("lq%d" % t, "ls%d" % t, 16, 8) for t in range(R)]:
+        dma("Y", v(q_, a, a + n, cast=dt.uint8), v("qc", zq, zq + n, cast=dt.uint8), [rows])
+        dma("Y", v(s_, a, a + n), v("sc", zq, zq + n), [rows])
+    dma("Y", v("L"), v("ZT", 0, E), [rows])
+    dma("Y", v("Z", 0, 256), v("ZT", 0, 256), [rows])
+    dma("Y", v("Bt"), v("ZT", 0, 512), [rows])
+    ts(v("GT"), v("GI"), pc("g"), None, A.is_equal)
+    qz("qg", "sg", 0, 128, v("GT"))
+    col("a32", "aa", 32.0, 0.0)
+    col("n0", "p", -1.0, pc("a32"))
+    col("n1", "n0", 1.0, 16.0)
+    for h in range(2):
+        act(v("JA"), v("J"), AF.Abs, bias=pc("n%d" % h), scale=1.0)
+        act(v("F", 512 * h, 512 * h + 512), v("JA"), AF.Relu, bias=1.0, scale=-1.0)
+    qz("qf", "sf", 0, 256, v("F"))
+    col("boff", "q4", 32.0, pc("r"))
+    col("q7", "q8", -8.0, pc("q"))
+    col("zc", "aa", -2.0, pc("q7"))
+    act(v("IP", 8, 16), v("IO", 60, 68), AF.Identity, bias=pc("q8"), scale=1.0)
+    ts(v("oS"), v("IO", 28, 44), pc("boff"), None, A.add)
+    ts(v("oQ"), v("IO", 44, 46), pc("q"), 16.0, A.add, A.add)
+    ts(v("IP", 0, 8), v("IO", 52, 60), pc("zc"), None, A.is_equal)
+    tt(v("IP", 16, 24), v("IP", 0, 8), v("IP", 8, 16), A.mult)
+    ts(v("oD"), v("IP", 16, 24), 16.0, None, A.add)
+    qz("qu", "su", 0, 128, v("ub"))
+    cp(v("qus", cast=dt.uint32), v("qu", cast=dt.uint32, by=v("oU")))
+    act(v("sus"), v("su", by=v("oU")), AF.Copy)
+    qz("qv", "sv", 0, 128, v("vb"))
 
     def q_rows():
-        qz(T.qx[:, 0:320], T.sx[:, 0:320], T.X[:, 0:1280], XR, ["qxr"])
+        qz("qx", "sx", 0, C, rows)
 
     def q_waits():
-        qz(T.qx[:, 320:448], T.sx[:, 320:448], T.X[:, 1280:1792], XW + ["Xz"], ["qxw"])
+        qz("qx", "sx", 256, E, v("X", 1024, 4 * E))
 
-    def pick_codes(t):
-        cp(T.pk[:, 0:128].bitcast(dt.uint32), T["lq%d" % t][:, 0:24].bitcast(dt.uint32).indirect(T.oD[:]),
-           ["land%d" % t, "lz%d" % t, "oD"], ["pk"])
-
-    def pick_scales(t):
-        act(T.ps[:, 0:128], T["ls%d" % t][:, 0:24].indirect(T.oD[:]), AF.Copy, ["land%d" % t, "lz%d" % t, "oD"], ["ps"])
-
-    def unpack_mm(bank):
-        o = T[bank][:, 0:128]
-        mm(o, T.qf0[:], T.sf0[:], T.pk[:, 0:128], T.ps[:, 0:128], True, False, ["qf0", "pk", "ps"], [bank])
-        mm(o, T.qf1[:], T.sf1[:], T.pk[:, 64:192], T.ps[:, 64:192], False, True, ["qf1", "pk", "ps", "pkz"], [bank])
-
-    def unpack_copy(b, on_vector=False):
-        if on_vector:
-            cp(T.X[0:16, 1280 + b:1536:4], T.P2[32 * b:32 * b + 16, 0:64], ["P2"], ["Xw%d" % b])
-        else:
-            act(T.X[0:16, 1280 + b:1536:4], T.P3[32 * b:32 * b + 16, 0:64], AF.Copy, ["P3"], ["Xw%d" % b])
-
-    def turn1():
-        for a in range(4):
-            tr(T.TT[32 * a:32 * a + 32, :], T.Bs[96:128, 64 * a:64 * a + 64], ["Bs"], ["TT%d" % a])
-        act(T.TT2[:], T.TT[:].indirect(T.oT[:]), AF.Copy, ["TT0", "TT1", "TT2", "TT3", "oT"], ["TU"])
-
-    def turn2():
-        tr(T.Bt[:, 0:32], T.TT2[:], ["TU"], ["Bt"])
+    def unpack(t, by):
+        cp(v("pk", 0, 128, cast=dt.uint32), v("lq%d" % t, cast=dt.uint32, by=v("oD")))
+        act(v("ps", 0, 128), v("ls%d" % t, by=v("oD")), AF.Copy)
+        bank = {"S": "P3", "V": "P2"}
+        for e in sorted(set(by)):
+            both = []
+            mm(bank[e], "qf", "sf", 0, "pk", "ps", 0, 128, both)
+            mm(bank[e], "qf", "sf", 128, "pk", "ps", 64, 128, both)
+        for b in range(4):
+            src = bank[by[b]]
+            move(by[b], v("X", 4 * C + b, 4 * E, 4, p=(0, 16)), (T[src][32 * b:32 * b + 16, 0:K],) + v(src, 0, K)[1:])
 
     def send(t):
-        qb, sb = T["qb%d" % t], T["sb%d" % t]
-        qz(qb[:], sb[:], T.Bt[:], ["Bt"], ["qb%d" % t])
+        qb, sb = "qb%d" % t, "sb%d" % t
+        qz(qb, sb, 0, 128, v("Bt"))
         dst = T.cores[(rank + t + 1) % n_ranks]
         rid, pid, _ = topo.addr(dst)
         m = sum(1 << e for e in topo.engines(core, dst)[0:NENG])
         arr = T.sem["arr%d" % t]
-        op("G", lambda: g.remote_dma(T["lq%d" % t][:, 0:8].bitcast(dt.uint8), qb[:, 0:8].bitcast(dt.uint8), arr,
-                                     T.sem.sent, pid, rid, m), ["qb%d" % t], [], kind="r")
-        op("G", lambda: g.remote_dma(T["ls%d" % t][:, 0:8], sb[:, 0:8], arr, T.sem.sent, pid, rid, m),
-           ["qb%d" % t], [], kind="r")
-        op("X", None, [], ["land%d" % t], kind="x", info=("arr%d" % t, 2 * NENG))
-
-    def tail_post():
-        act(T.Mt[:], T.M64[:, 0:256], AF.Copy, MA, ["Mt"], scale=1.0 / 64)
-        dma("Y", T.X[16:128, 1280:1536], T.Mt[0:112, :], ["Mt"], ["Xws"])
-
-    def cview(s, n):
-        k, e = _strip(s)
-        a = 4 * TILE0[k] + e
-        return T.CT[:, a:4 * (TILE0[k] + n):4]
-
-    def kcol(s):
-        return T.H[:, 16 * s + 15:16 * s + 16]
+        lq, ls = v("lq%d" % t, 0, 8, cast=dt.uint8), v("ls%d" % t, 0, 8)
+        cq, cs = v(qb, 0, 8, cast=dt.uint8), v(sb, 0, 8)
+        op("G", lambda: g.remote_dma(lq[0], cq[0], arr, T.sem.sent, pid, rid, m), [cq], [], 360, kind="r")
+        op("G", lambda: g.remote_dma(ls[0], cs[0], arr, T.sem.sent, pid, rid, m), [cs], [], 360, kind="r")
+        op("X", None, [cs], [lq, ls], REMOTE + (FIRST if t == 0 else 0), kind="x", info=("arr%d" % t, 2 * NENG))
 
     q_rows()
     for t in range(R):
-        last = t == R - 1
-        mm(T.P0[:, 0:320], T.qus[:], T.sus[:], T.qx[:, 0:320], T.sx[:, 0:320], True, True, ["qus", "sus", "qxr"], ["P0"])
-        mm(T.P1[:, 0:320], T.qus[:], T.sus[:], T.qx[:, 0:320], T.sx[:, 0:320], True, True, ["qus", "sus", "qxr"], ["P1"])
-        if t == 0:
-            consts_1()
-        else:
-            send(t - 1)
-            tail_post()
-            if t == 1:
-                consts_6()
+        mm("P0", "qus", "sus", 0, "qx", "sx", 0, C)
+        mm("P1", "qus", "sus", 0, "qx", "sx", 0, C)
+        for a, b in ((0, 48), (48, C)):
+            tt(v("Km", a, b), v("P0", a, b), v("Mn", a, b), A.min)
+            scan(v("H", a, b), v("Rst", a, b), v("Km", a, b), -BIG, A.min, A.max)
+        if t > 0:
+            unpack(t - 1, "SSSS")
+        q_waits()
+        mm("P4", "qus", "sus", 0, "qx", "sx", 192, 192)
+        mm("P5", "qus", "sus", 0, "qx", "sx", 256, 128)
+        tt(v("Kmw"), v("P4", 128, 192), v("Mn", 0, K), A.min)
+        scan(v("Hw"), v("Rst", 0, K), v("Kmw"), -BIG, A.min, A.max)
+        diag = v("CT", 0, 4 * C, 4)
+        tt(diag, v("P0", 0, C), v("H"), A.is_lt)
+        scan(v("Ds"), v("Z16"), diag, -1000.0, A.max, A.add)
+        for s in range(19):
+            a = 16 * s + 16
+            if s < N_S:
+                d = v("Dsg", C * s, C * s + C - a)
+                act(d, v("P1", a, C), AF.Sign, bias=kcol(s), scale=-1.0)
+                act(cview(s, a, C), d, AF.Relu, acc=v("acc", s, s + 1))
+                continue
+            if s < JOIN[t]:
+                ts(cview(s, a, C), v("P0", a, C), kcol(s), None, A.is_lt)
             else:
-                qz(T.qv[:], T.sv[:], T.vb[:], ["vb"], ["qv"])
-        h = 16 * min(S_FULL)
-        tt(T.Km[:, h:320], T.P0[:, h:320], T.Mn[:, h:320], A.max, ["P0", "Mn"], ["Km1"])
-        tt(T.Km[:, 0:h], T.P0[:, 0:h], T.Mn[:, 0:h], A.max, ["P0", "Mn"], ["Km"])
-        scan(T.H[:, h:320], T.Rst[:, h:320], T.Km[:, h:320], BIG, A.max, A.min, ["Rst", "Km1"], ["H1"])
-        scan(T.H[:, 0:h], T.Rst[:, 0:h], T.Km[:, 0:h], BIG, A.max, A.min, ["Rst", "Km"], ["H"])
-        jo = [0]
-        for i, s in enumerate(S_FULL):
-            d = T.Dsg[:, 320 * i:320 * i + 16 * s]
-            act(d, T.P1[:, 0:16 * s], AF.Sign, ["P1", "H1"], ["Dsg%d" % i], bias=kcol(s), scale=-1.0)
-        for i, s in enumerate(S_FULL):
-            d = T.Dsg[:, 320 * i:320 * i + 16 * s]
-            act(cview(s, 16 * s), d, AF.Relu, ["Dsg%d" % i], ["C%d" % s, "acc%d" % s], scale=-1.0, acc=T.acc[:, s:s + 1])
-
-        def strip(s):
-            if s in S_FULL:
-                return
-            ts(cview(s, 16 * s), T.P0[:, 0:16 * s], kcol(s), None, A.is_gt, None, ["P0", "H", "H1"], ["C%d" % s])
-            act(T.junk[:, jo[0]:jo[0] + 16 * s], cview(s, 16 * s), AF.Copy, ["C%d" % s], ["junk%d" % s, "acc%d" % s],
-                acc=T.acc[:, s:s + 1])
-            jo[0] += 16 * s
-
-        def q_tile(k, a, b, strips):
-            qz(T.qc[:, a:b], T.sc[:, a:b], T.CT[:, 4 * a:4 * b], ["C%d" % s for s in strips], ["qc%d" % k])
-
-        def sum_mm(k, n, rd):
-            a = TILE0[k]
-            mm(T.P2[:, 0:n], T.qg[:], T.sg[:], T.qc[:, a:a + n], T.sc[:, a:a + n], k == 0, k == 4, ["qg"] + rd, ["P2"])
-
-        for s in (19, 18, 17):
-            strip(s)
-        tt(cview(20, 320), T.H[:], T.P0[:, 0:320], A.is_le, ["H", "H1", "P0"], ["C20"])
-        strip(16)
-        scan(T.Ds[:], T.Z16[:], cview(20, 320), -1000.0, A.max, A.subtract, ["Z16", "C20"], ["Ds"])
-        for s in (15, 14, 13, 12):
-            strip(s)
-        if t == 0:
-            consts_2()
-        q_tile(0, 0, 320, (20, 19, 18, 17))
-        sum_mm(0, 320, ["qc0"])
-        q_tile(1, 320, 576, (16, 15, 14, 13))
-        sum_mm(1, 256, ["qc1"])
-        for s in (11, 10, 9, 8):
-            strip(s)
-        q_tile(2, 576, 768, (12, 11, 10, 9))
-        sum_mm(2, 192, ["qc2"])
-        for s in (7, 6, 5, 4, 3, 2, 1):
-            strip(s)
-        if t == 0:
-            q_waits()
-        q_tile(3, 768, 960, (8, 7, 6, 5, 4, 3, 2, 1))
-        sum_mm(3, 128, ["qc3"])
-        sum_mm(4, 128, ["qc3", "qcz"])
-        if t > 0:
-            pick_codes(t - 1)
-            pick_scales(t - 1)
-            unpack_mm("P3")
-            for b in range(4):
-                unpack_copy(b)
-        else:
-            consts_3()
-        scan(T.st[:], T.DD[:, 0:320], T.P2[:, 0:320], 0.0, A.mult, A.add, ["DD", "P2"], ["st"])
-        tt(T.a1[:], T.Ds[:, 15:320:16], T.acc[:], A.subtract, ["Ds"] + ["acc%d" % s for s in range(20)], ["a1"])
-        ts(T.a2[:], T.st[:, 15:320:16], pc(INV16), pc(CQ), A.mult, A.add, ["st", "inv16", "cq"], ["a2"])
-        tt(T.a4[:], T.a1[:], T.a2[:], A.add, ["a1", "a2"], ["a4"])
-        cp(T.oR[:], T.a4[:], ["a4"], ["oR"])
-        if t > 0:
-            q_waits()
-        else:
-            ms(T.Fl[:, 0:264:66], 0.0, ["Fl"])
-        mm(T.P4[:, 0:128], T.qus[:], T.sus[:], T.qx[:, 320:448], T.sx[:, 320:448], True, True, ["qus", "sus", "qxw"], ["P4"])
-        mm(T.P5[:, 0:128], T.qus[:], T.sus[:], T.qx[:, 320:448], T.sx[:, 320:448], True, True, ["qus", "sus", "qxw"], ["P5"])
-        for s in range(K_VEC, 20):
-            a = 256 * (s // 4) + s % 4
-            act(T.CKs[:, a:256 * (s // 4 + 1):4], T.P5[:, 0:64], AF.Sign, ["P5", "H", "H1"], ["CKs%d" % s],
-                bias=kcol(s), scale=-1.0)
-        act(T.CK[:, 64 * K_VEC:1280], T.CKs[:, 64 * K_VEC:1280], AF.Relu, ["CKs%d" % s for s in range(K_VEC, 20)], ["CKS"])
-        if t == 0:
-            consts_4()
-        cp(T.O4[:].indirect(T.oR[:]), T.V4[:, 0:320], ["oR", "V4"], ["O4"])
-        tt(T.Kmw[:], T.P4[:, 0:64], T.Mn[:, 0:64], A.max, ["P4", "Mn"], ["Kmw"])
-        scan(T.st4[:], T.DD[:, 320:640], T.O4[:], 0.0, A.mult, A.add, ["DD", "O4"], ["st4"])
-        scan(T.Hw[:], T.Rst[:, 0:64], T.Kmw[:], BIG, A.max, A.min, ["Rst", "Kmw"], ["Hw"])
-        ts(T.oZ[:], T.st4[:, 3:320:4], pc(INV4), 0.02, A.mult, A.add, ["st4", "inv4"], ["oZ"])
-        for s in range(4):
-            act(T.Dr[:, 66 * s:66 * s + 64], T.P5[:, 0:64], AF.Sign, ["P5", "Hw"], ["Dr%d" % s, "accd%d" % s],
-                bias=T.Hw[:, 16 * s + 15:16 * s + 16], scale=-1.0, acc=T.accd[:, s:s + 1])
-        act(T.Ar[:], T.Dr[:], AF.Abs, ["Dr0", "Dr1", "Dr2", "Dr3", "Drc", "Drd"], ["Ar"])
-        act(T.Z[:, 512:1792], T.X[:, 0:1280].indirect(T.oZ[:]), AF.Copy, XR + ["oZ"], ["Zr"])
-        for s in range(K_VEC):
-            a = 256 * (s // 4) + s % 4
-            ts(T.CK[:, a:256 * (s // 4 + 1):4], T.P4[:, 0:64], kcol(s), None, A.is_lt, None, ["P4", "H", "H1"], ["CK%d" % s])
-        qz(T.qk[:, 0:320], T.sk[:, 0:320], T.CK[:], ["CK%d" % s for s in range(K_VEC)] + ["CKS"], ["qk"])
+                ts(cview(s, a, E), v("P4", a - 192, E - 192), kcol(s), None, A.is_lt)
+            act(v("Dsg", C * s, C * s + C - a), cview(s, a, C), AF.Copy, acc=v("acc", s, s + 1))
+        alone = list(range(JOIN[t])) + [19]
+        nw = len(alone) // 4
+        for i, s in enumerate(alone):
+            k, e = i // 4, i % 4
+            if k < nw - W_S:
+                ts(v("CT", 4 * (W0 + K * k) + e, 4 * (W0 + K * k + K), 4), v("P4", 128, 192), kcol(s), None, A.is_lt)
+            else:
+                act(v("Dw", 256 * k + e, 256 * k + 256, 4), v("P5", K, 128), AF.Sign, bias=kcol(s), scale=-1.0)
+        for k in range(nw - W_S, nw):
+            act(v("CT", 4 * (W0 + K * k), 4 * (W0 + K * k + K)), v("Dw", 256 * k, 256 * k + 256), AF.Relu)
+        ranks, counts = [], []
         for k in range(5):
-            mm(T.P6[:, 0:128], T.qg[:], T.sg[:], T.qk[:, 64 * k:64 * k + 128], T.sk[:, 64 * k:64 * k + 128],
-               k == 0, k == 4, ["qg", "qk", "qkz"], ["P6"])
-        scan(T.Sr[:], T.Fl[:], T.Ar[:], 0.0, A.mult, A.add, ["Fl", "Ar"], ["Sr"])
-        tt(T.r1[:], T.Sr[:, 65:264:66], T.accd[:], A.add, ["Sr", "accd0", "accd1", "accd2", "accd3"], ["r1"])
-        ts(T.oW[:], T.r1[:], 0.5, pc(Q_), A.mult, A.add, ["r1", "PC"], ["oW"])
-        ts(T.k4[:], T.P6[:, 0:64], -4.0, pc(C1280), A.mult, A.add, ["P6", "c1280"], ["k4"])
-        cp(T.B4[:].indirect(T.oW[:]), T.V4[:, 0:64], ["oW", "V4"], ["B4"])
-        cp(T.ks4[:].indirect(T.oW[:]), T.k4[:], ["oW", "k4"], ["ks4"])
-        scan(T.stb[:], T.DD[:, 320:384], T.B4[:], 0.0, A.mult, A.add, ["DD", "B4"], ["stb"])
-        scan(T.p4[:], T.four[:], T.ks4[:], -4.0, A.add, A.max, ["four", "ks4"], ["p4"])
-        ts(T.oB[:], T.stb[:, 3:64:4], pc(INV4), 0.02, A.mult, A.add, ["stb", "inv4"], ["oB"])
-        act(T.Z[:, 1792:2048], T.X[:, 1280:1536].indirect(T.oB[:]), AF.Copy, XW + ["oB"], ["Zb"])
-        ts(T.f1[:], T.p4[:], 1280.0, 256.0, A.is_ge, A.mult, ["p4"], ["f1"])
-        fill()
-        tt(T.f2[:], T.f1[:], T.p4[:], A.add, ["f1", "p4"], ["f2"])
-        fill()
-        tt(T.f3[:], T.f2[:], T.V4[:, 320:384], A.min, ["f2", "V4"], ["f3"])
-        fill()
-        scan(T.stp[:], T.DD[:, 320:384], T.f3[:], 0.0, A.mult, A.add, ["DD", "f3"], ["stp"])
-        fill()
-        cp(T.Xb2[:], T.Z[:, 1792:2048], ["Zb"], ["Xb2"])
-        ts(T.oP[:], T.stp[:, 3:64:4], pc(INV4), 0.02, A.mult, A.add, ["stp", "inv4"], ["oP"])
-        fill()
-        cp(T.Z[:, 256:384], T.Z[:, 512:2048].indirect(T.oP[:, 0:8]), ["Zr", "Zb", "oP"], ["Zt0"])
-        act(T.Z[:, 384:512], T.Z[:, 512:2048].indirect(T.oP[:, 8:16]), AF.Copy, ["Zr", "Zb", "oP"], ["Zt1"])
-        act(T.Z64[:, 0:256], T.Z[:, 256:512], AF.Copy, ["Zt0", "Zt1"], ["Ya"], scale=64.0)
-        qz(T.qz[:, 0:128], T.sz[:, 0:128], T.Z[:, 0:512], ["Zt0", "Zt1", "Zz"], ["qz1"])
+            n = C - J0[k] + (K if 4 * k - 1 >= JOIN[t] else 0) + (K * nw if k == 4 else 0)
+            qz("qc", "sc", QC0[k], QC0[k] + n, v("CT", 4 * CT0[k], 4 * (CT0[k] + n)))
+            mm("P2", "qg", "sg", 0, "qc", "sc", QC0[k] - J0[k], C, ranks)
+            if 4 * k - 1 >= JOIN[t]:
+                mm("P6", "qg", "sg", 0, "qc", "sc", QC0[k] + C - J0[k], 128, counts)
+        for k in range(nw):
+            mm("P6", "qg", "sg", 0, "qc", "sc", W0 + K * k, 128, counts)
+        for s in range(4):
+            act(v("Dr", 66 * s, 66 * s + K), v("P5", K, 128), AF.Sign, bias=v("Hw", 16 * s + 15, 16 * s + 16), scale=-1.0,
+                acc=v("accd", s, s + 1))
+        act(v("Ar"), v("Dr"), AF.Abs)
+        scan(v("Sr"), v("Fl"), v("Ar"), 0.0, A.mult, A.add)
+        tt(v("r1"), v("Sr", 65, 264, 66), v("accd"), A.add)
+        ts(v("oW"), v("r1"), 0.5, pc("q"), A.mult, A.add)
+        cp(v("Bb", by=v("oW")), v("V16", C, E))
+        act(v("kk"), v("P6", 0, K), AF.Identity, bias=pc("c320"), scale=-1.0)
+        cp(v("ks", by=v("oW")), v("kk"))
+        scan(v("pp"), v("one"), v("ks"), -1.0, A.add, A.max)
+        scan(v("stl"), v("DD", 0, K), v("pp"), 0.0, A.mult, A.add)
+        ts(v("oL"), v("stl", 15, K, 16), pc("inv16"), -0.17, A.mult, A.add)
+        tt(v("a1"), v("Ds", 15, C, 16), v("acc"), A.add)
+        act(v("a2"), v("a1"), AF.Identity, bias=pc("cqm"), scale=pc("m16"))
+        scan(v("st"), v("DD"), v("P2", 0, C), 0.0, A.mult, A.add)
+        tt(v("a4"), v("a2"), v("st", 15, C, 16), A.subtract)
+        ts(v("oR"), v("a4"), pc("inv16"), None, A.mult)
+        cp(v("L", by=v("oL")), v("Bb"))
+        cp(v("L", 0, C, by=v("oR")), v("V16", 0, C))
+        cp(v("Lt"), v("L", by=v("oL")))
+        cp(v("L", by=v("oL")), v("Bb"))
+        scan(v("s4t"), v("D4", 0, K), v("Lt"), 0.0, A.mult, A.add)
+        ts(v("oT"), v("s4t", 3, K, 4), pc("inv4"), pc("c768"), A.mult, A.add)
+        scan(v("s4"), v("D4"), v("L", 0, C), 0.0, A.mult, A.add)
+        ts(v("oZ"), v("s4", 3, C, 4), pc("inv4"), pc("c768"), A.mult, A.add)
+        act(v("Z", 256, 512), v("X", by=v("oT")), AF.Copy)
+        for i, by in enumerate(GATHER_BY):
+            move(by, v("Z", 512 + 256 * i, 768 + 256 * i), v("X", by=v("oZ", 16 * i, 16 * i + 16)))
+        qz("qz", "sz", 0, 128, v("Z", 0, 512))
+        ts(v("Z64", 0, 256), v("Z", 256, 512), 64.0, None, A.mult)
         for b in range(4):
-            w = slice(128 * b, 128 * b + 128)
-            mm(T["P%d" % b][:, 0:128], T.qW[:, w], T.sW[:, w], T.qz[:, 0:128], T.sz[:, 0:128], True, True,
-               ["qW", "sW", "qz1"], ["P%d" % b])
-
-        def place(a, b):
-            cp(T.Z[:, 512:2048].indirect(T.oP[:, a:b]), T.Xb2[:, 16 * a:16 * b], ["Xb2", "oP"], ["Zr", "Zb"])
-
-        def add1():
+            mm("P%d" % b, "qW", "sW", 128 * b, "qz", "sz", 0, 128)
+            tt(v("M64", b, 256, 4), v("P%d" % b, K, 128), v("Z64", b, 256, 4), A.add)
+        act(v("Bs"), v("M64", 0, 256, by=v("oS")), AF.Copy, scale=1.0 / 64)
+        for a in range(4):
+            tr(v("TT", p=(32 * a, 32 * a + 32)), v("Bs", 64 * a, 64 * a + 64, p=(96, 128)))
+        act(v("TT2"), v("TT", by=v("oQ")), AF.Copy)
+        tr(v("Bt", 0, 32), v("TT2"))
+        send(t)
+        act(v("Mt"), v("M64", 0, 256), AF.Copy, scale=1.0 / 64)
+        dma("Y", v("X", 4 * C, 4 * E, p=(16, 128)), v("Mt", p=(0, 112)))
+        for i, (a, b_) in enumerate(CHUNKS):
+            qz("qz", "sz", 128 + a, 128 + b_, v("Z", 512 + 4 * a, 512 + 4 * b_))
+            if len(PRE_BY[i]) == 1:
+                move(PRE_BY[i], v("Z64", 256 + 4 * a, 256 + 4 * b_), v("Z", 512 + 4 * a, 512 + 4 * b_), 64.0)
             for b in range(4):
-                tt(T.M64[:, b:256:4], T["P%d" % b][:, 64:128], T.Z64[:, b:256:4], A.add, ["P%d" % b, "Ya"], ["Ma%d" % b])
-
-        def b_gather():
-            act(T.Bs[:], T.M64[:, 0:256].indirect(T.oS[:]), AF.Copy, MA + ["oS"], ["Bs"], scale=1.0 / 64)
-
-        def q_z():
-            qz(T.qz[:, 128:448], T.sz[:, 128:448], T.Z[:, 512:1792], ["Zr"], ["qz2"])
-            for b in range(4):
-                w = slice(128 * b, 128 * b + 128)
-                mm(T["P%d" % (4 + b)][:, 0:320], T.qW[:, w], T.sW[:, w], T.qz[:, 128:448], T.sz[:, 128:448], True, True,
-                   ["qW", "sW", "qz2"], ["P%d" % (4 + b)])
-
-        def pre(b):
-            act(T.Z64[:, 256 + b:1536:4], T.Z[:, 512 + b:1792:4], AF.Copy, ["Zr"], ["Y%d" % b], scale=64.0)
-
-        def add2(b):
-            tt(T.M64[:, 256 + b:1536:4], T["P%d" % (4 + b)][:, 0:320], T.Z64[:, 256 + b:1536:4], A.add,
-               ["P%d" % (4 + b), "Y%d" % b], ["Mb%d" % b])
-
-        def post(b):
-            if b < POST_S:
-                act(T.X[:, b:1280:4], T.M64[:, 256 + b:1536:4], AF.Copy, ["Mb%d" % b], ["Xr%d" % b], scale=1.0 / 64)
-            else:
-                ts(T.X[:, b:1280:4], T.M64[:, 256 + b:1536:4], 1.0 / 64, None, A.mult, None, ["Mb%d" % b], ["Xr%d" % b])
-
-        if last:
-            act(T.LE[:, 64:384], T.O4[:], AF.Copy, ["O4"], ["LEr"], scale=0.25)
-            scan(T.stl[:], T.DD[:, 0:64], T.f3[:], 0.0, A.mult, A.add, ["DD", "f3"], ["stl"])
-            add1()
-            b_gather()
-            place(0, 8)
-            turn1()
-            place(8, 16)
-            turn2()
-            send(t)
-            q_z()
-            pre(0)
-            tail_post()
-            ts(T.oL[:], T.stl[:, 15:64:16], pc(INV64), pc(CB), A.mult, A.add, ["stl", "inv64", "cb"], ["oL"])
-            for b in range(1, 4):
-                pre(b)
-            for b in range(4):
-                add2(b)
-            for b in range(4):
-                post(b)
-        else:
-            if t == 0:
-                consts_5()
-            place(0, 16)
-            q_z()
-            add1()
-            pre(0)
-            pre(1)
-            b_gather()
-            pre(2)
-            pre(3)
-            add2(0)
-            add2(1)
-            post(0)
-            turn1()
-            add2(2)
-            add2(3)
-            for b in range(1, 4):
-                post(b)
-            turn2()
+                bank = "P%d" % ((4 + 4 * i + b) % 8)
+                z64, m64 = v("Z64", 256 + 4 * a + b, 256 + 4 * b_, 4), v("M64", 256 + 4 * a + b, 256 + 4 * b_, 4)
+                mm(bank, "qW", "sW", 128 * b, "qz", "sz", 128 + a, b_ - a)
+                if len(PRE_BY[i]) == 4:
+                    move(PRE_BY[i][b], z64, v("Z", 512 + 4 * a + b, 512 + 4 * b_, 4), 64.0)
+                tt(m64, v(bank, 0, b_ - a), z64, A.add)
+                if len(POST_BY[i]) == 4:
+                    move(POST_BY[i][b], v("X", 4 * a + b, 4 * b_, 4), m64, 1.0 / 64)
+            if len(POST_BY[i]) == 1:
+                move(POST_BY[i], v("X", 4 * a, 4 * b_), v("M64", 256 + 4 * a, 256 + 4 * b_), 1.0 / 64)
         q_rows()
 
-    dma("Y", T.oc[:, 0:1280], T.qx[:, 0:320].bitcast(dt.uint8), ["qxr"], [])
-    act(T.LE[:, 384:448], T.B4[:], AF.Identity, ["B4", "c320"], ["LEb"], bias=pc(C320), scale=0.25)
-    act(T.Lb[:], T.B4[:], AF.Identity, ["B4", "c320"], ["Lb"], bias=pc(C320), scale=0.25)
-    mm(T.P0[:, 0:320], T.qv[:], T.sv[:], T.qx[:, 0:320], T.sx[:, 0:320], True, True, ["qv", "qxr"], ["P0"])
-    act(T.ysb[:, 0:320], T.P0[:, 0:320], AF.Copy, ["P0"], ["y0"])
-    dma("Y", T.y[:, 0:320], T.ysb[:, 0:320], ["y0"], [])
-    pick_codes(R - 1)
-    pick_scales(R - 1)
-    unpack_mm("P3")
-    unpack_mm("P2")
-    cp(T.LE[:, 0:64], T.LE[:, 64:448].indirect(T.oL[:]), ["LEr", "LEb", "oL"], ["LEt"])
-    unpack_copy(0)
-    unpack_copy(1)
-    unpack_copy(2, True)
-    unpack_copy(3, True)
+    dma("Y", T.oc[:, 0:1024], v("qx", 0, 256, cast=dt.uint8))
+    act(v("LE", 0, C), v("L", 0, C), AF.Identity, bias=pc("c192"), scale=1.0)
+    act(v("LE", C, E), v("Lt"), AF.Identity, bias=pc("c192"), scale=1.0)
+    dma("Y", T.le[:], (T.LE[0:128:16, :], v("LE")[1]))
+    mm("P0", "qv", "sv", 0, "qx", "sx", 0, 256)
+    act(v("ysb", 0, 256), v("P0", 0, 256), AF.Copy)
+    dma("Y", T.y[:, 0:256], v("ysb", 0, 256))
+    unpack(R - 1, "SSVV")
     q_waits()
-    mm(T.P1[:, 0:128], T.qv[:], T.sv[:], T.qx[:, 320:448], T.sx[:, 320:448], True, True, ["qv", "qxw"], ["P1"])
-    cp(T.LE[:, 64:448].indirect(T.oL[:]), T.Lb[:], ["Lb", "oL"], ["LEr", "LEb"])
-    dma("Y", T.le[:, 320:384], T.LE[0:128:16, 0:64], ["LEt"], [])
-    dma("Y", T.oc[:, 1280:1536], T.qx[:, 320:384].bitcast(dt.uint8), ["qxw"], [])
+    mm("P1", "qv", "sv", 0, "qx", "sx", 256, 128)
+    dma("Y", T.oc[:, 1024:1536], v("qx", 256, E, cast=dt.uint8))
     for k in range(4):
-        dma("S", T.osc[4 * k:4 * k + 4, :], T.sx[32 * k:32 * k + 4, 0:384], ["qxr", "qxw"], [])
-    cp(T.ysb[:, 320:384], T.P1[:, 0:64], ["P1"], ["y1"])
-    dma("Y", T.y[:, 320:384], T.ysb[:, 320:384], ["y1"], [])
-    dma("Y", T.le[:, 0:320], T.LE[0:128:16, 64:384], ["LEr"], [])
+        dma("S", T.osc[4 * k:4 * k + 4, :], v("sx", p=(32 * k, 32 * k + 4)))
+    cp(v("ysb", 256, E), v("P1", 0, 128))
+    dma("Y", T.y[:, 256:E], v("ysb", 256, E))
 
-    writer, readers, deps = {}, {}, []
+    def meets(x, y):
+        return x[1] & y[1] and x[2] < y[3] and y[2] < x[3]
+
+    def touched(o):
+        return [(x, False) for x in o["rd"]] + [(x, True) for x in o["wr"]]
+
+    if not ORDER:
+        seen, before = {}, []
+        for i, o in enumerate(ops):
+            d = {}
+            for reg, writes in touched(o):
+                for j, other, wrote in seen.get(reg[0], []):
+                    p = ops[j]
+                    same = p["e"] == o["e"] and p["k"] == "c" and o["k"] == "c"
+                    if same and o["info"] is not None and o["info"] is p["info"]:
+                        continue
+                    if (wrote or writes or reg[1] == -1 and not same) and meets(reg, other):
+                        lag = 0 if same and reg[1] == -1 else DMA if p["k"] == "d" else WAKE
+                        d[j] = max(d.get(j, 0), lag)
+            before.append(d)
+            for reg, writes in touched(o):
+                seen.setdefault(reg[0], []).append((i, reg, writes))
+        ORDER.extend(issue_order([o["e"] for o in ops], [o["c"] for o in ops],
+                                 [DMA if o["k"] == "d" else 0 for o in ops], before))
+    ops = [ops[i] for i in ORDER]
+
+    seen, need = {}, []
     for i, o in enumerate(ops):
-        d = set()
-        for r in o["rd"]:
-            d.add(writer[r])
-        for w in o["wr"]:
-            if w in writer:
-                d.add(writer[w])
-            d.update(readers.get(w, []))
-        d.discard(i)
-        if o["e"] == "P":
-            d = set(j for j in d if ops[j]["e"] != "P")
-        deps.append(d)
-        for r in o["rd"]:
-            readers.setdefault(r, []).append(i)
-        for w in o["wr"]:
-            writer[w] = i
-            readers[w] = []
-    need = []
-    for i, o in enumerate(ops):
+        if o["k"] == "x":
+            o["rd"] = []
+        elif o["info"] is not None:
+            o["info"].append(o)
         best = {}
-        for j in deps[i]:
+        for reg, writes in touched(o):
+            bank = reg[1] == -1
+            for j, other, wrote in seen.get(reg[0], []):
+                p = ops[j]
+                same = p["e"] == o["e"] and p["k"] == "c" and o["k"] == "c"
+                if same and bank:
+                    continue
+                if (wrote or writes or bank) and meets(reg, other):
+                    key = p["e"] if p["k"] == "c" else j
+                    best[key] = max(best.get(key, -1), j)
+        need.append(sorted(best.values(), reverse=True))
+        for reg, writes in touched(o):
+            seen.setdefault(reg[0], []).append((i, reg, writes))
+    known, after, waits = {}, {}, []
+    for i, o in enumerate(ops):
+        k, w = known.setdefault(o["e"], {}), []
+        for j in need[i]:
             key = ops[j]["e"] if ops[j]["k"] == "c" else j
-            best[key] = max(best.get(key, -1), j)
-        need.append(sorted(best.values()))
-    used = set(j for n in need for j in n)
+            if k.get(key, -1) < j:
+                w.append(j)
+                k[key] = j
+                for kk, jj in after[j].items():
+                    k[kk] = max(k.get(kk, -1), jj)
+        waits.append(w)
+        after[i] = dict(k) if o["k"] != "x" else {}
+    used = set(j for w in waits for j in w)
     queue = {"V": V, "S": S, "P": P, "G": g, "Y": g.sync}
     token, count, waited, ndma = {}, {}, {}, [0]
     for i, o in enumerate(ops):
@@ -567,11 +552,10 @@ def rank_program(g, core, T, topo):
             count[o["info"][0]] = o["info"][1]
             continue
         q = queue[o["e"]]
-        for j in need[i]:
+        for j in waits[i]:
             s, c = token[j]
-            if waited.get((o["e"], s), 0) < c:
-                q.wait_ge(T.sem[s], c)
-                waited[(o["e"], s)] = c
+            q.wait_ge(T.sem[s], c)
+            waited[s] = max(waited.get(s, 0), c)
         ins = o["fn"]()
         if o["k"] == "d":
             s = "d%d" % ndma[0]
@@ -586,5 +570,5 @@ def rank_program(g, core, T, topo):
             token[i] = (s, count[s])
     count["sent"] = 2 * NENG * R
     for s in sorted(count):
-        if max([waited.get((e, s), 0) for e in queue]) < count[s]:
+        if waited.get(s, 0) < count[s]:
             g.wait_ge(T.sem[s], count[s])

@@ -12,59 +12,77 @@ def _sb(n, d):
 
 
 SCRATCH = {
-    "X": _sb(1536, BF), "Z": _sb(1792, BF), "Z64": _sb(1536, BF), "M64": _sb(1536, BF),
+    "X": _sb(1536, BF), "Z": _sb(1824, BF), "Z64": _sb(1536, BF), "M64": _sb(1536, BF),
     "Mt": _sb(256, BF), "Bs": _sb(256, BF), "TT": _sb(64, BF), "TT2": _sb(32, BF), "Bt": _sb(512, BF),
-    "ub": _sb(512, BF), "vb": _sb(512, BF), "ZT": _sb(1024, BF),
+    "ub": _sb(512, BF), "vb": _sb(512, BF),
     "qu": _sb(128, F8), "su": _sb(128, U8), "qus": _sb(128, F8), "sus": _sb(128, U8),
     "qv": _sb(128, F8), "sv": _sb(128, U8), "qW": _sb(512, F8), "sW": _sb(512, U8),
-    "qx": _sb(384, F8), "sx": _sb(384, U8), "qz": _sb(448, F8), "sz": _sb(448, U8),
-    "CT": _sb(5376, BF), "qc": _sb(1984, F8), "sc": _sb(1984, U8), "Dsg": _sb(6080, BF), "Dw": _sb(1024, BF),
+    "qx": _sb(384, F8), "sx": _sb(384, U8),
+    "CT": _sb(6144, BF), "qc": _sb(2304, F8), "sc": _sb(2304, U8), "Dsg": _sb(6080, BF), "Dw": _sb(1280, BF),
     "GI": _sb(512, BF), "GT": _sb(512, BF), "qg": _sb(128, F8), "sg": _sb(128, U8),
-    "J": _sb(512, BF), "JA": _sb(512, BF), "F": _sb(1024, BF), "qf": _sb(256, F8), "sf": _sb(256, U8),
+    "J": _sb(512, F32), "JA": _sb(1024, BF), "F": _sb(1024, BF), "qf": _sb(256, F8), "sf": _sb(256, U8),
     "pk": _sb(192, F8), "ps": _sb(192, U8),
     "Km": _sb(320, F32), "H": _sb(320, F32), "Kmw": _sb(64, F32), "Hw": _sb(64, F32),
     "Ds": _sb(320, BF), "acc": _sb(20, F32), "a1": _sb(20, F32), "a2": _sb(20, F32), "a4": _sb(20, F32),
-    "st": _sb(320, F32), "L": _sb(384, BF), "Lt": _sb(64, BF), "Bb": _sb(64, BF), "s4": _sb(320, BF), "s4t": _sb(64, BF),
-    "Dr": _sb(264, BF), "Ar": _sb(264, BF), "Sr": _sb(264, BF), "accd": _sb(4, F32), "r1": _sb(4, F32),
+    "st": _sb(320, F32), "L": _sb(448, BF), "Bb": _sb(64, BF), "s4": _sb(384, BF),
+    "Dr": _sb(264, BF), "Ar": _sb(264, BF), "Sr": _sb(264, BF), "accd": _sb(4, F32),
     "kk": _sb(64, F32), "ks": _sb(64, F32), "pp": _sb(64, F32), "stl": _sb(64, F32),
-    "LE": _sb(384, F32), "ysb": _sb(384, F32),
-    "oR": _sb(20, U16), "oZ": _sb(80, U16), "oW": _sb(4, U16), "oT": _sb(16, U16), "oL": _sb(4, U16),
-    "oU": _sb(8, U16), "oS": _sb(16, U16), "oQ": _sb(2, U16), "oD": _sb(8, U16),
-    "pI": _sb(8, I32), "pJ": _sb(8, I32), "PC": _sb(32, F32), "IU": _sb(320, F32), "IA": _sb(320, F32),
+    "LE": _sb(384, F32), "ysb": _sb(384, F32), "sB": _sb(64, F32), "oB": _sb(4, U16), "BT": _sb(64, BF), "pT": _sb(64, F32),
+    "oR": _sb(20, U16), "oZ": _sb(96, U16), "oW": _sb(4, U16), "oL": _sb(4, U16), "oU": _sb(8, U16), "oC": _sb(32, U16),
+    "pI": _sb(4, I32), "pJ": _sb(4, I32), "PC": _sb(40, F32), "IU": _sb(320, F32), "IA": _sb(320, F32),
     "IB": _sb(320, F32), "IC": _sb(320, F32), "DD": _sb(320, F32), "Mn": _sb(320, F32), "Rst": _sb(320, BF),
-    "Z16": _sb(320, BF), "I4": _sb(320, BF), "D4": _sb(320, BF), "V16": _sb(384, BF), "IO": _sb(80, F32),
+    "Z16": _sb(320, BF), "I4": _sb(384, BF), "D4": _sb(384, BF), "V16": _sb(384, BF), "IO": _sb(80, F32),
     "IP": _sb(32, F32), "Ri": _sb(264, BF), "Rj": _sb(264, BF), "Fl": _sb(264, BF), "one": _sb(64, F32),
 }
 for _t in range(R):
-    SCRATCH["lq%d" % _t] = _sb(24, F8)
-    SCRATCH["ls%d" % _t] = _sb(24, U8)
+    SCRATCH["lq%d" % _t] = _sb(32, F8)
+    SCRATCH["ls%d" % _t] = _sb(32, U8)
+    SCRATCH["qz%d" % _t] = _sb(456, F8)
+    SCRATCH["sz%d" % _t] = _sb(456, U8)
     SCRATCH["qb%d" % _t] = _sb(128, F8)
     SCRATCH["sb%d" % _t] = _sb(128, U8)
 for _b in range(8):
     SCRATCH["P%d" % _b] = ("psum", [128, 512], F32)
 
-NDMA = 48
+NDMA = 72
 SEMAPHORES = ["eV", "eS", "eP", "eG", "sent", "arr0", "arr1", "arr2"] + ["d%d" % i for i in range(NDMA)]
 
 A = AluOpType
 AF = ActivationFunctionType
 NENG = 8
-N_S = 6
-JOIN = (11, 15, 15)
-W_S = 0
-GATHER_BY = "VVSSS"
-CHUNKS = ((0, 320),)
-PRE_BY = ("VSSS", "VSSS")
-POST_BY = ("SSVV", "SSVV")
+STRIP_BY = ("SSSVVVVVVVVVVVVVSSS",) * 3
+HI = (320, 192, 192)
+KEY_CUTS = (0, 32)
+W_CUTS = (256,)
+TURN_BY = "SV"
+SORT_BY = "V"
+GT_BY = "V"
+D4_BY = "V"
+CORNER_BY = "GGGG"
+ZERO_V = 0
+LAST_BY = "VVVV"
+COL_V = ("q", "q8", "q4", "c768", "boff", "c8", "z1", "zd")
+SHIFT_BY = "VVV"
+LIST_CUTS = ((0, 64, 192, 384),) * 3
+RANK_CUTS = ((0, 192, 320),) * 3
+TAIL_WITH = (False, False, False)
+B_WITH = (False, False, False)
+JOIN = (5, 5, 4)
+W_S = (1, 1, 1)
+GATHER_BY = ("SSVSSS",) * 3
+CHUNKS = (((192, 320), (0, 192)),) * 3
+PRE_BY = (("VSSS", "SSSS"),) * 3
+POST_BY = (("SSSS", "SSVV"),) * 3
 J0 = (0, 64, 128, 192, 256)
-CT0 = (0, 320, 576, 768, 960)
-QC0 = (0, 1408, 1792, 512, 960)
-W0 = 1088
-FIX, WAKE, DMA, REMOTE, FIRST, GATHER, SCATTER, SLACK, AHEAD, PASSES = 48, 120, 2400, 3600, 1800, 1.56, 3.0, 150, 3.0, 4
+CT0 = (0, 384, 704, 960, 1152)
+QC0 = (0, 1536, 1984, 576, 1024)
+FIX, WAKE, ISSUE, DMA, REMOTE, FIRST, GATHER, SCATTER, PASSES = 5, 270, 100, 1000, 1700, 1800, 1.56, 3.8, 3
+PE_FIX, WIDE = 50, {F8: 4, U8: 1, BF: 2, F32: 4}
+PATIENCE = ((120, 2.0), (150, 3.0), (250, 3.0), (300, 2.0), (400, 4.0), (600, 3.0))
 ORDER = []
 
 
-def list_order(eng, cost, before, way, ready):
+def list_order(eng, cost, before, way, ready, slack, ahead):
     n = len(eng)
     later = [[] for _ in range(n)]
     for i in range(n):
@@ -78,8 +96,8 @@ def list_order(eng, cost, before, way, ready):
     while pool:
         first = min(pool, key=lambda i: (start(i), i))
         e, now = eng[first], start(first)
-        i = max((i for i in pool if eng[i] == e and start(i) <= now + SLACK),
-                key=lambda i: (way[i] - AHEAD * (start(i) - now), -i))
+        i = max((i for i in pool if eng[i] == e and start(i) <= now + slack),
+                key=lambda i: (way[i] - ahead * (start(i) - now), -i))
         end[i] = start(i) + cost[i]
         if e != "X":
             free[e] = end[i]
@@ -99,13 +117,15 @@ def issue_order(eng, cost, tail, before):
     for i in range(n):
         for j, lag in before[i].items():
             after[j][i] = lag
-    back, best = [float(i) for i in range(n)], None
-    for _ in range(PASSES):
-        way = list_order(eng, cost, after, back, tail)[1]
-        order, back = list_order(eng, cost, before, way, [0.0] * n)
-        total = max(back[i] + tail[i] for i in range(n))
-        if best is None or total < best[0]:
-            best = (total, order)
+    best = None
+    for slack, ahead in PATIENCE:
+        back = [float(i) for i in range(n)]
+        for _ in range(PASSES):
+            way = list_order(eng, cost, after, back, tail, slack, ahead)[1]
+            order, back = list_order(eng, cost, before, way, [0.0] * n, slack, ahead)
+            total = max(back[i] + tail[i] for i in range(n))
+            if best is None or total < best[0]:
+                best = (total, order)
     return best[1]
 
 
@@ -206,7 +226,7 @@ def rank_program(g, core, T, topo):
         def fn():
             start, stop = group is None or group[0]["fn"] is fn, group is None or group[-1]["fn"] is fn
             return P.matmul_mx(o, w[0][0], w[1][0], w[2][0], w[3][0], start, stop)
-        op("P", fn, w, [v(bank)], FIX + n, info=group)
+        op("P", fn, w, [v(bank)], PE_FIX + n, info=group)
 
     def iota(out, pat, base, cm=0, small=True):
         if small:
@@ -216,18 +236,26 @@ def rank_program(g, core, T, topo):
 
     def dma(q, out, in_, after=()):
         e = g.sync if q == "Y" else g.scalar
-        op(q, lambda: e.dma_start(a_(out), a_(in_)), [in_] + list(after), [out] if isinstance(out, tuple) else [], 70,
-           kind="d")
+        side = out if isinstance(out, tuple) else in_
+        op(q, lambda: e.dma_start(a_(out), a_(in_)), [in_] + list(after), [out] if isinstance(out, tuple) else [],
+           ISSUE + 0.6 * side[2] * WIDE[SCRATCH[side[1][0][0]][2]], kind="d")
+        ops[-1]["lag"] = DMA
 
-    names = ("q", "r", "q8", "aa", "b2", "g", "p", "q2", "e15", "inv16", "m16", "cq", "cqm", "q4", "nq4", "q7", "t1", "t2",
-             "inv4", "c768", "boff", "zc", "a32", "n0", "n1", "c192", "c320")
+    def select(out, in_, pat, base, cm):
+        op("G", lambda: g.affine_select(out[0], in_[0], pat, A.is_ge, 0.0, base, cm), [in_], [out], 205 + 2 * out[2])
+
+    names = ("f4", "f8", "g", "f32", "p", "p768", "q", "q2", "cq", "inv16", "m16", "q8", "b2", "t1", "t2", "inv4", "q4",
+             "c768", "boff", "c8", "n0", "n1", "z1", "zd")
 
     def pc(name):
         i = names.index(name)
         return v("PC", i, i + 1)
 
-    def col(name, src, scale, bias, f=AF.Identity):
-        act(pc(name), pc(src), f, bias=bias, scale=scale)
+    def col(name, src, scale, bias):
+        if name in COL_V:
+            ts(pc(name), pc(src), scale, bias, A.mult, A.add)
+        else:
+            act(pc(name), pc(src), AF.Identity, bias=bias, scale=scale)
 
     def cview(s, a, b):
         k, e = (s + 1) // 4, (s + 1) % 4
@@ -245,33 +273,35 @@ def rank_program(g, core, T, topo):
     dma("Y", v("sW"), T.ws[:], [rows])
     dma("Y", v("vb"), T.v[:], [rows])
 
-    iota(v("pI"), [[0, 8]], 0, 1, small=False)
+    for i in range(4):
+        iota(v("pI", i, i + 1), [[0, 1]], 0, 8 >> i, small=False)
+    iota(pc("p"), [[0, 1]], 0, 1)
+    ts(v("pJ", 0, 4), v("pI", 0, 4), 5, None, A.logical_shift_right)
+    cp(v("PC", 0, 4), v("pJ", 0, 4))
+    col("q", "g", -16.0, pc("p"))
+    iota(pc("p768"), [[0, 1]], 768, 1)
+    col("c768", "f4", -4.0, pc("p768"))
+    col("q4", "g", -4.0, pc("f4"))
+    col("q8", "g", -2.0, pc("f8"))
+    col("b2", "f8", -2.0, pc("f4"))
     iota(v("IU"), [[0, 20], [1, 16]], 0)
     iota(v("IO", 0, 8), [[16, 8]], 0)
-    iota(v("GI"), [[1, 8], [0, 64]], 0)
-    ms(v("ZT"), 0.0)
-    for i, (sh, an) in enumerate(((0, 15), (0, 3), (3, 1), (5, 3), (2, 1), (4, 7))):
-        ts(v("pJ", i, i + 1), v("pI", i, i + 1), sh, an, A.logical_shift_right, A.bitwise_and)
-    cp(pc("q"), v("pJ", 0, 1))
-    cp(v("PC", 1, 6), v("pJ", 1, 6))
     cp(v("oU"), v("IO", 0, 8))
-    ms(v("Rst"), BIG)
-    ms(v("Rst", 0, C, 16), -BIG)
-    ms(v("Z16"), -1000.0)
-    iota(v("Z16", 0, C, 16), [[16, 20]], -144)
+    ms(v("Rst"), 0.0)
+    ms(v("Rst", 0, C, 16), -2 * BIG)
+    iota(v("Z16"), [[16, 20], [-32, 16]], -144)
     iota(v("acc"), [[0, 20]], 0)
     iota(v("Ri"), [[-16, 4], [1, 66]], 0)
     iota(v("Dr", 64, 264, 66), [[32, 4]], 0)
     iota(v("Dr", 65, 264, 66), [[0, 4]], 0)
     iota(v("V16"), [[1, 384]], -192)
     iota(v("one"), [[0, 64]], 1)
-    iota(v("I4"), [[0, 80], [1, 4]], 0)
-    iota(pc("p"), [[0, 1]], 0, 1)
-    iota(v("J"), [[64, 4], [1, 32], [-64, 4]], 0)
-    iota(v("IO", 28, 44), [[4, 8], [128, 2]], 0)
-    iota(v("IO", 44, 46), [[32, 2]], 0)
-    iota(v("IO", 52, 60), [[1, 2], [0, 4]], 0)
-    iota(v("IO", 60, 68), [[0, 2], [2, 4]], -16)
+    iota(v("I4"), [[0, 96], [1, 4]], 0)
+    iota(v("J"), [[64, 4], [1, 32], [-64, 4]], 0, -1)
+    iota(v("IO", 16, 32), [[4, 8], [128, 2]], -768)
+    iota(v("IO", 32, 36), [[2, 4]], 0, 8)
+    iota(v("IO", 36, 38), [[32, 2]], 16)
+    iota(v("IO", 38, 46), [[64, 2], [2, 4]], 0, -64)
     act(v("IC"), v("IU"), AF.Abs, bias=pc("q"), scale=-1.0)
     act(v("Mn"), v("IC"), AF.Identity, bias=BIG, scale=-2 * BIG)
     col("q2", "q", 1.0, 2.0)
@@ -279,53 +309,67 @@ def rank_program(g, core, T, topo):
     act(v("IB"), v("IA"), AF.Relu, bias=2.0, scale=-1.0)
     act(v("IA"), v("IB"), AF.Abs, bias=-(1.0 + 0.5 / M), scale=1.0)
     act(v("DD"), v("IA"), AF.Identity, bias=M + 0.5, scale=-M)
-    col("e15", "q", 1.0, -14.0, AF.Relu)
     col("cq", "q", 1.0, 144.15)
-    col("m16", "e15", 1.0 - M, M)
-    col("inv16", "e15", 1.0 - 1.0 / M, 1.0 / M)
-    act(pc("cqm"), pc("cq"), AF.Copy, scale=pc("m16"))
-    col("q4", "q8", 2.0, pc("b2"))
+    ts(pc("inv16"), pc("q"), 15.0, 1.0 / M, A.is_equal, A.max)
+    col("m16", "inv16", -M, M + 1.0)
     col("t1", "q8", M4 * M4 - 1.0, 1.0)
     col("t2", "b2", (M4 - 1.0) * 4.0 / M4 ** 3, 4.0 / M4 ** 3)
-    act(pc("inv4"), pc("t1"), AF.Copy, scale=pc("t2"))
-    col("nq4", "q4", -1.0, -0.5)
-    col("c768", "r", 1.0, 768.0)
-    col("c192", "r", 0.0, 192.0)
-    col("c320", "r", 0.0, 320.0)
-    act(v("I4"), v("I4"), AF.Sign, bias=pc("nq4"), scale=1.0)
-    act(v("D4"), v("I4"), AF.Identity, bias=M4 / 2, scale=M4 / 2)
+    col("inv4", "t1", pc("t2"), 0.0)
+    if D4_BY == "V":
+        ts(v("D4"), v("I4"), pc("q4"), M4, A.is_gt, A.mult)
+    else:
+        act(v("I4"), v("I4"), AF.Sign, bias=pc("q4"), scale=-1.0)
+        act(v("D4"), v("I4"), AF.Relu, scale=-M4)
     ts(v("Rj"), v("Ri"), pc("q"), 2.0, A.not_equal, A.mult)
     act(v("Fl"), v("Rj"), AF.Identity, bias=-1.0, scale=1.0)
     act(v("Fl", 0, 264, 66), v("Rj", 0, 264, 66), AF.Copy, scale=0.0)
     zq = QC0[4] - J0[4]
-    qz("qc", "sc", zq, zq + 256, v("ZT"))
-    for k in range(5):
-        dma("Y", v("CT", 4 * CT0[k], 4 * CT0[k] + 192), v("ZT", 0, 192))
-    for q_, s_, a, n in [("qc", "sc", QC0[k] - n, n) for k, n in ((1, 128), (2, 128), (3, 192))] + [("pk", "ps", 128, 64)] + [
-            ("lq%d" % t, "ls%d" % t, 16, 8) for t in range(R)]:
-        dma("Y", v(q_, a, a + n, cast=dt.uint8), v("qc", zq, zq + n, cast=dt.uint8), [rows])
-        dma("Y", v(s_, a, a + n), v("sc", zq, zq + n), [rows])
-    dma("Y", v("L"), v("ZT", 0, E), [rows])
-    dma("Y", v("Z", 0, 256), v("ZT", 0, 256), [rows])
-    dma("Y", v("Bt"), v("ZT", 0, 512), [rows])
-    ts(v("GT"), v("GI"), pc("g"), None, A.is_equal)
+    zt = v("CT", 4 * CT0[4], 4 * CT0[4] + 1024)
+    ms(zt, 0.0)
+    qz("qc", "sc", zq, zq + 256, zt)
+    for k in range(4):
+        corner = v("CT", 4 * CT0[k], 4 * CT0[k] + 192)
+        if CORNER_BY[k] == "V":
+            ms(corner, 0.0)
+        else:
+            iota(corner, [[0, 192]], 0)
+    for i, (a, n) in enumerate([(QC0[k] - n, n) for k, n in ((2, 128), (1, 128), (3, 192))] + [
+            (QC0[4] + 128 + K * j, K) for j in sorted(set(JOIN)) if j < 4] + [(QC0[2] + 256, K)] * (min(JOIN) < 3)):
+        if i < ZERO_V and n >= 128:
+            qz("qc", "sc", a, a + n, v("CT", 4 * CT0[4], 4 * (CT0[4] + n)))
+        else:
+            dma("Y", v("qc", a, a + n, cast=dt.uint8), v("qc", zq, zq + n, cast=dt.uint8), [rows])
+            dma("Y", v("sc", a, a + n), v("sc", zq, zq + n), [rows])
+    for q_, s_, a, n in [("pk", "ps", 128, K)] + [("lq%d" % t, "ls%d" % t, 16, 16) for t in range(R)]:
+        cp(v(q_, a, a + n, cast=dt.uint32), v("qc", zq, zq + 128, cast=dt.uint32, by=v("oU", 0, n // 16)))
+        act(v(s_, a, a + n), v("sc", zq, zq + 128, by=v("oU", 0, n // 16)), AF.Copy)
+    iota(v("Z", 0, 256), [[0, 256]], 0)
+    iota(v("Bt"), [[0, 512]], 0)
+    if GT_BY == "V":
+        iota(v("GI"), [[1, 8], [0, 64]], 0)
+        ts(v("GT"), v("GI"), pc("g"), None, A.is_equal)
+    else:
+        iota(v("GT"), [[0, 512]], 1)
+        select(v("GI"), v("GT"), [[-16, 8], [0, 64]], 0, 1)
+        select(v("GT"), v("GI"), [[16, 8], [0, 64]], 15, -1)
     qz("qg", "sg", 0, 128, v("GT"))
-    col("a32", "aa", 32.0, 0.0)
-    col("n0", "p", -1.0, pc("a32"))
-    col("n1", "n0", 1.0, 16.0)
     for h in range(2):
-        act(v("JA"), v("J"), AF.Abs, bias=pc("n%d" % h), scale=1.0)
-        act(v("F", 512 * h, 512 * h + 512), v("JA"), AF.Relu, bias=1.0, scale=-1.0)
+        col("n%d" % h, "f32", 32.0, 16.0 * h)
+        act(v("JA", 512 * h, 512 * h + 512), v("J"), AF.Abs, bias=pc("n%d" % h), scale=1.0)
+        act(v("F", 512 * h, 512 * h + 512), v("JA", 512 * h, 512 * h + 512), AF.Relu, bias=1.0, scale=-1.0)
     qz("qf", "sf", 0, 256, v("F"))
-    col("boff", "q4", 32.0, pc("r"))
-    col("q7", "q8", -8.0, pc("q"))
-    col("zc", "aa", -2.0, pc("q7"))
-    act(v("IP", 8, 16), v("IO", 60, 68), AF.Identity, bias=pc("q8"), scale=1.0)
-    ts(v("oS"), v("IO", 28, 44), pc("boff"), None, A.add)
-    ts(v("oQ"), v("IO", 44, 46), pc("q"), 16.0, A.add, A.add)
-    ts(v("IP", 0, 8), v("IO", 52, 60), pc("zc"), None, A.is_equal)
-    tt(v("IP", 16, 24), v("IP", 0, 8), v("IP", 8, 16), A.mult)
-    ts(v("oD"), v("IP", 16, 24), 16.0, None, A.add)
+    col("boff", "q4", 32.0, pc("c768"))
+    col("c8", "f8", -64.0, pc("q8"))
+    col("z1", "f8", 512.0, pc("q8"))
+    col("zd", "f32", 128.0, pc("z1"))
+    act(v("IP", 0, 16), v("IO", 16, 32), AF.Identity, bias=pc("boff"), scale=1.0)
+    act(v("IP", 16, 20), v("IO", 32, 36), AF.Identity, bias=pc("c8"), scale=1.0)
+    act(v("IP", 20, 22), v("IO", 36, 38), AF.Identity, bias=pc("q"), scale=1.0)
+    act(v("IO", 48, 56), v("IO", 38, 46), AF.Abs, bias=pc("zd"), scale=1.0)
+    act(v("IO", 56, 64), v("IO", 48, 56), AF.Relu, bias=16.0, scale=-1.0)
+    act(v("IP", 22, 30), v("IO", 56, 64), AF.Identity, bias=16.0, scale=-1.0)
+    cp(v("oC", 0, 30), v("IP", 0, 30))
+    o_s, o_8, o_q, o_d = v("oC", 0, 16), v("oC", 16, 20), v("oC", 20, 22), v("oC", 22, 30)
     qz("qu", "su", 0, 128, v("ub"))
     cp(v("qus", cast=dt.uint32), v("qu", cast=dt.uint32, by=v("oU")))
     act(v("sus"), v("su", by=v("oU")), AF.Copy)
@@ -338,8 +382,8 @@ def rank_program(g, core, T, topo):
         qz("qx", "sx", 256, E, v("X", 1024, 4 * E))
 
     def unpack(t, by):
-        cp(v("pk", 0, 128, cast=dt.uint32), v("lq%d" % t, cast=dt.uint32, by=v("oD")))
-        act(v("ps", 0, 128), v("ls%d" % t, by=v("oD")), AF.Copy)
+        cp(v("pk", 0, 128, cast=dt.uint32), v("lq%d" % t, cast=dt.uint32, by=o_d))
+        act(v("ps", 0, 128), v("ls%d" % t, by=o_d), AF.Copy)
         bank = {"S": "P3", "V": "P2"}
         for e in sorted(set(by)):
             both = []
@@ -349,139 +393,203 @@ def rank_program(g, core, T, topo):
             src = bank[by[b]]
             move(by[b], v("X", 4 * C + b, 4 * E, 4, p=(0, 16)), (T[src][32 * b:32 * b + 16, 0:K],) + v(src, 0, K)[1:])
 
-    def send(t):
-        qb, sb = "qb%d" % t, "sb%d" % t
-        qz(qb, sb, 0, 128, v("Bt"))
+    def send(t, qb, sb, a):
         dst = T.cores[(rank + t + 1) % n_ranks]
         rid, pid, _ = topo.addr(dst)
         m = sum(1 << e for e in topo.engines(core, dst)[0:NENG])
         arr = T.sem["arr%d" % t]
         lq, ls = v("lq%d" % t, 0, 8, cast=dt.uint8), v("ls%d" % t, 0, 8)
-        cq, cs = v(qb, 0, 8, cast=dt.uint8), v(sb, 0, 8)
+        cq, cs = v(qb, a, a + 8, cast=dt.uint8), v(sb, a, a + 8)
         op("G", lambda: g.remote_dma(lq[0], cq[0], arr, T.sem.sent, pid, rid, m), [cq], [], 360, kind="r")
         op("G", lambda: g.remote_dma(ls[0], cs[0], arr, T.sem.sent, pid, rid, m), [cs], [], 360, kind="r")
         op("X", None, [cs], [lq, ls], REMOTE + (FIRST if t == 0 else 0), kind="x", info=("arr%d" % t, 2 * NENG))
 
     q_rows()
     for t in range(R):
+        hi = HI[t]
+
+        def keys(by, s, a, b):
+            if 16 * s >= hi:
+                return v({"V": "P4", "S": "P5"}[by], a - hi, b - hi)
+            return v({"V": "P0", "S": "P1"}[by], a, b)
+
+        if hi < C:
+            mm("P4", "qus", "sus", 0, "qx", "sx", hi, C - hi)
+            mm("P5", "qus", "sus", 0, "qx", "sx", hi, C - hi)
         mm("P0", "qus", "sus", 0, "qx", "sx", 0, C)
         mm("P1", "qus", "sus", 0, "qx", "sx", 0, C)
-        for a, b in ((0, 48), (48, C)):
-            tt(v("Km", a, b), v("P0", a, b), v("Mn", a, b), A.min)
-            scan(v("H", a, b), v("Rst", a, b), v("Km", a, b), -BIG, A.min, A.max)
+        cuts = [x for x in KEY_CUTS if x < hi] + [hi] + ([C] if hi < C else [])
+        for a, b in reversed(list(zip(cuts, cuts[1:]))):
+            tt(v("Km", a, b), keys("V", a // 16, a, b), v("Mn", a, b), A.min)
+            scan(v("H", a, b), v("Rst", a, b), v("Km", a, b), 0.0, A.add, A.max)
+        for a, b in ((hi, C), (0, hi)) if hi < C else ((0, C),):
+            tt(v("CT", 4 * a, 4 * b, 4), keys("V", a // 16, a, b), v("H", a, b), A.is_lt)
+        scan(v("Ds"), v("Z16"), v("CT", 0, 4 * C, 4), -1000.0, A.max, A.add)
+        join = JOIN[t]
+        late = [s for s in range(19) if (s + 1) // 4 >= join and STRIP_BY[t][s] == "V"]
+        for s in range(19):
+            a = 16 * s + 16
+            d = v("Dsg", C * s, C * s + C - a)
+            if s in late:
+                continue
+            if STRIP_BY[t][s] == "S":
+                act(d, keys("S", s, a, C), AF.Sign, bias=kcol(s), scale=-1.0)
+                act(cview(s, a, C), d, AF.Relu, acc=v("acc", s, s + 1))
+            else:
+                ts(cview(s, a, C), keys("V", s, a, C), kcol(s), None, A.is_lt)
+                act(d, cview(s, a, C), AF.Copy, acc=v("acc", s, s + 1))
         if t > 0:
             unpack(t - 1, "SSSS")
         q_waits()
-        mm("P4", "qus", "sus", 0, "qx", "sx", 192, 192)
-        mm("P5", "qus", "sus", 0, "qx", "sx", 256, 128)
-        tt(v("Kmw"), v("P4", 128, 192), v("Mn", 0, K), A.min)
-        scan(v("Hw"), v("Rst", 0, K), v("Kmw"), -BIG, A.min, A.max)
-        diag = v("CT", 0, 4 * C, 4)
-        tt(diag, v("P0", 0, C), v("H"), A.is_lt)
-        scan(v("Ds"), v("Z16"), diag, -1000.0, A.max, A.add)
-        for s in range(19):
+        n = max(128, E - 16 * min(late + [19]) - 16)
+        mm("P6", "qus", "sus", 0, "qx", "sx", E - n, n)
+        mm("P7", "qus", "sus", 0, "qx", "sx", 256, 128)
+        waits_v, waits_s = v("P6", n - K, n), v("P7", K, 128)
+        tt(v("Kmw"), waits_v, v("Mn", 0, K), A.min)
+        scan(v("Hw"), v("Rst", 0, K), v("Kmw"), 0.0, A.add, A.max)
+        for s in late:
             a = 16 * s + 16
-            if s < N_S:
-                d = v("Dsg", C * s, C * s + C - a)
-                act(d, v("P1", a, C), AF.Sign, bias=kcol(s), scale=-1.0)
-                act(cview(s, a, C), d, AF.Relu, acc=v("acc", s, s + 1))
-                continue
-            if s < JOIN[t]:
-                ts(cview(s, a, C), v("P0", a, C), kcol(s), None, A.is_lt)
-            else:
-                ts(cview(s, a, E), v("P4", a - 192, E - 192), kcol(s), None, A.is_lt)
+            ts(cview(s, a, E), v("P6", a + n - E, n), kcol(s), None, A.is_lt)
             act(v("Dsg", C * s, C * s + C - a), cview(s, a, C), AF.Copy, acc=v("acc", s, s + 1))
-        alone = list(range(JOIN[t])) + [19]
-        nw = len(alone) // 4
-        for i, s in enumerate(alone):
-            k, e = i // 4, i % 4
-            if k < nw - W_S:
-                ts(v("CT", 4 * (W0 + K * k) + e, 4 * (W0 + K * k + K), 4), v("P4", 128, 192), kcol(s), None, A.is_lt)
+        w0 = 128 if join < 5 else K
+        for s in range(20):
+            k, e = (s + 1) % 20 // 4, (s + 1) % 4
+            w = CT0[4] + w0 + K * k if k < join else CT0[k] + C - J0[k]
+            if s in late:
+                continue
+            if k >= W_S[t]:
+                ts(v("CT", 4 * w + e, 4 * (w + K), 4), waits_v, kcol(s), None, A.is_lt)
             else:
-                act(v("Dw", 256 * k + e, 256 * k + 256, 4), v("P5", K, 128), AF.Sign, bias=kcol(s), scale=-1.0)
-        for k in range(nw - W_S, nw):
-            act(v("CT", 4 * (W0 + K * k), 4 * (W0 + K * k + K)), v("Dw", 256 * k, 256 * k + 256), AF.Relu)
+                act(v("Dw", 256 * k + e, 256 * k + 256, 4), waits_s, AF.Sign, bias=kcol(s), scale=-1.0)
+        for k in range(W_S[t]):
+            w = CT0[4] + w0 + K * k if k < join else CT0[k] + C - J0[k]
+            act(v("CT", 4 * w, 4 * (w + K)), v("Dw", 256 * k, 256 * k + 256), AF.Relu)
         ranks, counts = [], []
         for k in range(5):
-            n = C - J0[k] + (K if 4 * k - 1 >= JOIN[t] else 0) + (K * nw if k == 4 else 0)
-            qz("qc", "sc", QC0[k], QC0[k] + n, v("CT", 4 * CT0[k], 4 * (CT0[k] + n)))
-            mm("P2", "qg", "sg", 0, "qc", "sc", QC0[k] - J0[k], C, ranks)
-            if 4 * k - 1 >= JOIN[t]:
-                mm("P6", "qg", "sg", 0, "qc", "sc", QC0[k] + C - J0[k], 128, counts)
-        for k in range(nw):
-            mm("P6", "qg", "sg", 0, "qc", "sc", W0 + K * k, 128, counts)
+            n = C - J0[k] + (K if k >= join else 0) + (K * join if k == 4 else 0)
+            cuts = [0] + [x for x in W_CUTS if k == 4 and x <= n - 128] + [n]
+            for a, b in zip(cuts, cuts[1:]):
+                qz("qc", "sc", QC0[k] + a, QC0[k] + b, v("CT", 4 * (CT0[k] + a), 4 * (CT0[k] + b)))
+        parts = list(zip(RANK_CUTS[t], RANK_CUTS[t][1:]))
+        for i, (a, b) in enumerate(parts):
+            ranks = []
+            for k in range(5):
+                if J0[k] < b:
+                    mm("P%d" % (2 + i), "qg", "sg", 0, "qc", "sc", QC0[k] - J0[k] + a, b - a, ranks)
+        for k in range(5):
+            mm("P4", "qg", "sg", 0, "qc", "sc", QC0[k] + C - J0[k] if k >= join else QC0[4] + w0 + K * k, 128, counts)
         for s in range(4):
-            act(v("Dr", 66 * s, 66 * s + K), v("P5", K, 128), AF.Sign, bias=v("Hw", 16 * s + 15, 16 * s + 16), scale=-1.0,
+            act(v("Dr", 66 * s, 66 * s + K), waits_s, AF.Sign, bias=v("Hw", 16 * s + 15, 16 * s + 16), scale=-1.0,
                 acc=v("accd", s, s + 1))
         act(v("Ar"), v("Dr"), AF.Abs)
+        act(v("Ar", 65, 264, 66), v("accd"), AF.Copy)
         scan(v("Sr"), v("Fl"), v("Ar"), 0.0, A.mult, A.add)
-        tt(v("r1"), v("Sr", 65, 264, 66), v("accd"), A.add)
-        ts(v("oW"), v("r1"), 0.5, pc("q"), A.mult, A.add)
+        ts(v("oW"), v("Sr", 65, 264, 66), 0.5, pc("q"), A.mult, A.add)
         cp(v("Bb", by=v("oW")), v("V16", C, E))
-        act(v("kk"), v("P6", 0, K), AF.Identity, bias=pc("c320"), scale=-1.0)
-        cp(v("ks", by=v("oW")), v("kk"))
+        act(v("kk"), v("P4", 0, K), AF.Identity, bias=320.0, scale=-1.0)
+        if SORT_BY == "V":
+            cp(v("ks", by=v("oW")), v("kk"))
+        else:
+            scan(v("sB"), v("DD", 0, K), v("Bb"), 0.0, A.mult, A.add)
+            ts(v("oB"), v("sB", 15, K, 16), pc("inv16"), -128.09, A.mult, A.add)
+            act(v("ks"), v("kk", by=v("oB")), AF.Copy)
         scan(v("pp"), v("one"), v("ks"), -1.0, A.add, A.max)
-        scan(v("stl"), v("DD", 0, K), v("pp"), 0.0, A.mult, A.add)
+        move(TURN_BY[0], v("BT"), v("Bb", by=o_8))
+        move(TURN_BY[1], v("pT"), v("pp", by=o_8))
+        scan(v("stl"), v("DD", 0, K), v("pT"), 0.0, A.mult, A.add)
         ts(v("oL"), v("stl", 15, K, 16), pc("inv16"), -0.17, A.mult, A.add)
-        tt(v("a1"), v("Ds", 15, C, 16), v("acc"), A.add)
-        act(v("a2"), v("a1"), AF.Identity, bias=pc("cqm"), scale=pc("m16"))
-        scan(v("st"), v("DD"), v("P2", 0, C), 0.0, A.mult, A.add)
-        tt(v("a4"), v("a2"), v("st", 15, C, 16), A.subtract)
-        ts(v("oR"), v("a4"), pc("inv16"), None, A.mult)
-        cp(v("L", by=v("oL")), v("Bb"))
-        cp(v("L", 0, C, by=v("oR")), v("V16", 0, C))
-        cp(v("Lt"), v("L", by=v("oL")))
-        cp(v("L", by=v("oL")), v("Bb"))
-        scan(v("s4t"), v("D4", 0, K), v("Lt"), 0.0, A.mult, A.add)
-        ts(v("oT"), v("s4t", 3, K, 4), pc("inv4"), pc("c768"), A.mult, A.add)
-        scan(v("s4"), v("D4"), v("L", 0, C), 0.0, A.mult, A.add)
-        ts(v("oZ"), v("s4", 3, C, 4), pc("inv4"), pc("c768"), A.mult, A.add)
-        act(v("Z", 256, 512), v("X", by=v("oT")), AF.Copy)
-        for i, by in enumerate(GATHER_BY):
-            move(by, v("Z", 512 + 256 * i, 768 + 256 * i), v("X", by=v("oZ", 16 * i, 16 * i + 16)))
-        qz("qz", "sz", 0, 128, v("Z", 0, 512))
-        ts(v("Z64", 0, 256), v("Z", 256, 512), 64.0, None, A.mult)
-        for b in range(4):
-            mm("P%d" % b, "qW", "sW", 128 * b, "qz", "sz", 0, 128)
-            tt(v("M64", b, 256, 4), v("P%d" % b, K, 128), v("Z64", b, 256, 4), A.add)
-        act(v("Bs"), v("M64", 0, 256, by=v("oS")), AF.Copy, scale=1.0 / 64)
-        for a in range(4):
-            tr(v("TT", p=(32 * a, 32 * a + 32)), v("Bs", 64 * a, 64 * a + 64, p=(96, 128)))
-        act(v("TT2"), v("TT", by=v("oQ")), AF.Copy)
-        tr(v("Bt", 0, 32), v("TT2"))
-        send(t)
-        act(v("Mt"), v("M64", 0, 256), AF.Copy, scale=1.0 / 64)
-        dma("Y", v("X", 4 * C, 4 * E, p=(16, 128)), v("Mt", p=(0, 112)))
-        for i, (a, b_) in enumerate(CHUNKS):
-            qz("qz", "sz", 128 + a, 128 + b_, v("Z", 512 + 4 * a, 512 + 4 * b_))
-            if len(PRE_BY[i]) == 1:
-                move(PRE_BY[i], v("Z64", 256 + 4 * a, 256 + 4 * b_), v("Z", 512 + 4 * a, 512 + 4 * b_), 64.0)
+        for i, (a, b) in enumerate(parts):
+            x, y = a // 16, b // 16
+            tt(v("a1", x, y), v("Ds", a + 15, b, 16), v("acc", x, y), A.add)
+            act(v("a2", x, y), v("a1", x, y), AF.Copy, scale=pc("m16"))
+            scan(v("st", a, b), v("DD", a, b), v("P%d" % (2 + i), 0, b - a), 0.0, A.mult, A.add)
+            tt(v("a4", x, y), v("a2", x, y), v("st", a + 15, b, 16), A.subtract)
+            ts(v("oR", x, y), v("a4", x, y), pc("inv16"), pc("cq"), A.mult, A.add)
+        row = v("L", K, K + E, by=v("oL"))
+        iota(v("L", E, K + E), [[0, K]], 256)
+        for a, b in parts:
+            cp(v("L", K, E, by=v("oR", a // 16, b // 16)), v("V16", a, b))
+        tt(v("L", 0, K), row, v("BT"), A.min)
+        cp(row, v("BT"))
+        cuts = LIST_CUTS[t]
+        for a, b in zip(cuts, cuts[1:]):
+            scan(v("s4", a, b), v("D4", a, b), v("L", a, b), 0.0, A.mult, A.add)
+            ts(v("oZ", a // 4, b // 4), v("s4", a + 3, b, 4), pc("inv4"), pc("c768"), A.mult, A.add)
+        place, x = {}, K
+        for a, b in CHUNKS[t]:
+            for c in range(a, b, K):
+                place[c], x = x, x + K
+        for i, by in enumerate(GATHER_BY[t]):
+            x = place[K * i - K] if i else 0
+            move(by, v("Z", 256 + 4 * x, 512 + 4 * x), v("X", by=v("oZ", 16 * i, 16 * i + 16)))
+        qt, st_ = "qz%d" % t, "sz%d" % t
+
+        def layer(x0, x1, banks, pre_by, fill=0, more=0):
+            qz(qt, st_, K + x0 - fill, K + x1 + more, v("Z", 256 + 4 * (x0 - fill), 256 + 4 * (x1 + more)))
+            if len(pre_by) == 1:
+                move(pre_by, v("Z64", 4 * x0, 4 * x1), v("Z", 256 + 4 * x0, 256 + 4 * x1), 64.0)
             for b in range(4):
-                bank = "P%d" % ((4 + 4 * i + b) % 8)
-                z64, m64 = v("Z64", 256 + 4 * a + b, 256 + 4 * b_, 4), v("M64", 256 + 4 * a + b, 256 + 4 * b_, 4)
-                mm(bank, "qW", "sW", 128 * b, "qz", "sz", 128 + a, b_ - a)
-                if len(PRE_BY[i]) == 4:
-                    move(PRE_BY[i][b], z64, v("Z", 512 + 4 * a + b, 512 + 4 * b_, 4), 64.0)
-                tt(m64, v(bank, 0, b_ - a), z64, A.add)
-                if len(POST_BY[i]) == 4:
-                    move(POST_BY[i][b], v("X", 4 * a + b, 4 * b_, 4), m64, 1.0 / 64)
-            if len(POST_BY[i]) == 1:
-                move(POST_BY[i], v("X", 4 * a, 4 * b_), v("M64", 256 + 4 * a, 256 + 4 * b_), 1.0 / 64)
-        q_rows()
+                bank, z64 = "P%d" % (banks + b), v("Z64", 4 * x0 + b, 4 * x1, 4)
+                mm(bank, "qW", "sW", 128 * b, qt, st_, K + x0 - fill, x1 - x0 + fill)
+                if len(pre_by) == 4:
+                    move(pre_by[b], z64, v("Z", 256 + 4 * x0 + b, 256 + 4 * x1, 4), 64.0)
+                tt(v("M64", 4 * x0 + b, 4 * x1, 4), v(bank, fill, fill + x1 - x0), z64, A.add)
+
+        def descent(b_at):
+            if SHIFT_BY[t] == "D":
+                for a in range(8):
+                    dma("Y", v("TT2", p=(16 * a, 16 * a + 16)), v("M64", 32 * a, 32 * a + 32, p=(112, 128)))
+                act(b_at, v("TT2"), AF.Copy, scale=1.0 / 64)
+            else:
+                if SHIFT_BY[t] == "V":
+                    for a in range(4):
+                        tr(v("TT", p=(32 * a, 32 * a + 32)), v("M64", 64 * a, 64 * a + 64, p=(96, 128)))
+                else:
+                    tr(v("Bs", p=(96, 128)), v("M64", 0, 256, p=(96, 128)))
+                    for a in range(4):
+                        act(v("TT", p=(32 * a, 32 * a + 32)), v("Bs", 64 * a, 64 * a + 64, p=(96, 128)), AF.Copy)
+                act(v("TT2"), v("TT", by=o_q), AF.Copy, scale=1.0 / 64)
+                tr(b_at, v("TT2"))
+            act(v("Mt"), v("M64", 0, 256, by=o_s), AF.Copy, scale=1.0 / 64)
+            dma("Y", v("X", 4 * C, 4 * E, p=(16, 128)), v("Mt", p=(0, 112)))
+
+        b_at = v("Z", 256 + 4 * E, 288 + 4 * E) if B_WITH[t] else v("Bt", 0, 32)
+        if not TAIL_WITH[t]:
+            layer(0, K, 0, "V", fill=K)
+            descent(b_at)
+        for i, (a, b_) in enumerate(CHUNKS[t]):
+            x0, final = place[a], i == len(CHUNKS[t]) - 1
+            layer(0 if i == 0 and TAIL_WITH[t] else x0, x0 + b_ - a, 4 - 4 * i, PRE_BY[t][i],
+                  more=8 if final and B_WITH[t] else 0)
+            if i == 0 and TAIL_WITH[t]:
+                descent(b_at)
+            post_by = POST_BY[t][i]
+            for b in range(len(post_by)):
+                st = len(post_by)
+                move(post_by[b], v("X", 4 * a + b, 4 * b_, st), v("M64", 4 * x0 + b, 4 * (x0 + b_ - a), st), 1.0 / 64)
+            if t + 1 < R and HI[t + 1] < C:
+                qz("qx", "sx", a, b_, v("X", 4 * a, 4 * b_))
+        if B_WITH[t]:
+            send(t, qt, st_, K + E)
+        else:
+            qz("qb%d" % t, "sb%d" % t, 0, 128, v("Bt"))
+            send(t, "qb%d" % t, "sb%d" % t, 0)
+        if t + 1 == R or HI[t + 1] == C:
+            q_rows()
 
     dma("Y", T.oc[:, 0:1024], v("qx", 0, 256, cast=dt.uint8))
-    act(v("LE", 0, C), v("L", 0, C), AF.Identity, bias=pc("c192"), scale=1.0)
-    act(v("LE", C, E), v("Lt"), AF.Identity, bias=pc("c192"), scale=1.0)
-    dma("Y", T.le[:], (T.LE[0:128:16, :], v("LE")[1]))
+    act(v("LE", 0, C), v("L", K, E), AF.Identity, bias=192.0, scale=1.0)
+    act(v("LE", C, E), v("L", 0, K, by=o_8), AF.Identity, bias=192.0, scale=1.0)
+    dma("Y", T.le[:], (T.LE[0:128:16, :],) + v("LE")[1:])
     mm("P0", "qv", "sv", 0, "qx", "sx", 0, 256)
     act(v("ysb", 0, 256), v("P0", 0, 256), AF.Copy)
     dma("Y", T.y[:, 0:256], v("ysb", 0, 256))
-    unpack(R - 1, "SSVV")
+    unpack(R - 1, LAST_BY)
     q_waits()
     mm("P1", "qv", "sv", 0, "qx", "sx", 256, 128)
     dma("Y", T.oc[:, 1024:1536], v("qx", 256, E, cast=dt.uint8))
     for k in range(4):
-        dma("S", T.osc[4 * k:4 * k + 4, :], v("sx", p=(32 * k, 32 * k + 4)))
+        dma("YSSS"[k], T.osc[4 * k:4 * k + 4, :], v("sx", p=(32 * k, 32 * k + 4)))
     cp(v("ysb", 256, E), v("P1", 0, 128))
     dma("Y", T.y[:, 256:E], v("ysb", 256, E))
 
@@ -502,13 +610,13 @@ def rank_program(g, core, T, topo):
                     if same and o["info"] is not None and o["info"] is p["info"]:
                         continue
                     if (wrote or writes or reg[1] == -1 and not same) and meets(reg, other):
-                        lag = 0 if same and reg[1] == -1 else DMA if p["k"] == "d" else WAKE
+                        lag = 0 if same and reg[1] == -1 else p.get("lag", WAKE)
                         d[j] = max(d.get(j, 0), lag)
             before.append(d)
             for reg, writes in touched(o):
                 seen.setdefault(reg[0], []).append((i, reg, writes))
         ORDER.extend(issue_order([o["e"] for o in ops], [o["c"] for o in ops],
-                                 [DMA if o["k"] == "d" else 0 for o in ops], before))
+                                 [o.get("lag", 0) for o in ops], before))
     ops = [ops[i] for i in ORDER]
 
     seen, need = {}, []

@@ -12,73 +12,59 @@ def _sb(n, d):
 
 
 SCRATCH = {
-    "X": _sb(1536, BF), "Z": _sb(1824, BF), "Z64": _sb(1536, BF), "M64": _sb(1536, BF),
-    "Mt": _sb(256, BF), "Bs": _sb(256, BF), "TT": _sb(64, BF), "TT2": _sb(32, BF), "Bt": _sb(512, BF),
-    "ub": _sb(512, BF), "vb": _sb(512, BF),
+    "X": _sb(1536, BF), "Z": _sb(1792, BF), "Z64": _sb(1536, BF), "M64": _sb(1536, BF),
+    "Mt": _sb(256, BF), "TT": _sb(64, BF), "TT2": _sb(32, BF), "Bt": _sb(512, BF), "ub": _sb(512, BF), "vb": _sb(512, BF),
     "qu": _sb(128, F8), "su": _sb(128, U8), "qus": _sb(128, F8), "sus": _sb(128, U8),
     "qv": _sb(128, F8), "sv": _sb(128, U8), "qW": _sb(512, F8), "sW": _sb(512, U8),
-    "qx": _sb(384, F8), "sx": _sb(384, U8),
-    "CT": _sb(6144, BF), "qc": _sb(2304, F8), "sc": _sb(2304, U8), "Dsg": _sb(6080, BF), "Dw": _sb(1280, BF),
+    "qx": _sb(384, F8), "sx": _sb(384, U8), "qz": _sb(448, F8), "sz": _sb(448, U8),
+    "CT": _sb(6144, BF), "qc": _sb(2176, F8), "sc": _sb(2176, U8), "Dsg": _sb(6080, BF), "Dw": _sb(256, BF),
     "GI": _sb(512, BF), "GT": _sb(512, BF), "qg": _sb(128, F8), "sg": _sb(128, U8),
     "J": _sb(512, F32), "JA": _sb(1024, BF), "F": _sb(1024, BF), "qf": _sb(256, F8), "sf": _sb(256, U8),
-    "pk": _sb(192, F8), "ps": _sb(192, U8),
+    "pk": _sb(192, F8), "ps": _sb(192, U8), "qw": _sb(128, F8), "sw": _sb(128, U8),
     "Km": _sb(320, F32), "H": _sb(320, F32), "Kmw": _sb(64, F32), "Hw": _sb(64, F32),
     "Ds": _sb(320, BF), "acc": _sb(20, F32), "a1": _sb(20, F32), "a2": _sb(20, F32), "a4": _sb(20, F32),
-    "st": _sb(320, F32), "L": _sb(448, BF), "Bb": _sb(64, BF), "s4": _sb(384, BF),
-    "Dr": _sb(264, BF), "Ar": _sb(264, BF), "Sr": _sb(264, BF), "accd": _sb(4, F32),
-    "kk": _sb(64, F32), "ks": _sb(64, F32), "pp": _sb(64, F32), "stl": _sb(64, F32),
-    "LE": _sb(384, F32), "ysb": _sb(384, F32), "sB": _sb(64, F32), "oB": _sb(4, U16), "BT": _sb(64, BF), "pT": _sb(64, F32),
+    "st": _sb(320, F32), "L": _sb(448, BF), "L2": _sb(384, BF), "Bb": _sb(64, BF), "BT": _sb(64, BF),
+    "s2": _sb(320, BF), "s4": _sb(384, BF), "s5": _sb(96, BF), "Dr": _sb(256, BF), "Ar": _sb(260, F32), "Sr": _sb(260, F32),
+    "kk": _sb(64, F32), "ks": _sb(64, F32), "pp": _sb(64, F32), "pT": _sb(64, F32), "stl": _sb(64, F32),
+    "LE": _sb(384, F32), "ysb": _sb(384, F32),
     "oR": _sb(20, U16), "oZ": _sb(96, U16), "oW": _sb(4, U16), "oL": _sb(4, U16), "oU": _sb(8, U16), "oC": _sb(32, U16),
-    "pI": _sb(4, I32), "pJ": _sb(4, I32), "PC": _sb(40, F32), "IU": _sb(320, F32), "IA": _sb(320, F32),
+    "pI": _sb(4, I32), "pJ": _sb(4, I32), "PC": _sb(24, F32), "IU": _sb(320, F32), "IA": _sb(320, F32),
     "IB": _sb(320, F32), "IC": _sb(320, F32), "DD": _sb(320, F32), "Mn": _sb(320, F32), "Rst": _sb(320, BF),
-    "Z16": _sb(320, BF), "I4": _sb(384, BF), "D4": _sb(384, BF), "V16": _sb(384, BF), "IO": _sb(80, F32),
-    "IP": _sb(32, F32), "Ri": _sb(264, BF), "Rj": _sb(264, BF), "Fl": _sb(264, BF), "one": _sb(64, F32),
+    "Z16": _sb(320, BF), "I4": _sb(384, BF), "D4": _sb(384, BF), "V16": _sb(384, BF), "IO": _sb(64, F32),
+    "IP": _sb(32, F32), "Ri": _sb(260, BF), "Rj": _sb(260, BF), "Fl": _sb(260, BF), "one": _sb(64, F32),
 }
 for _t in range(R):
     SCRATCH["lq%d" % _t] = _sb(32, F8)
     SCRATCH["ls%d" % _t] = _sb(32, U8)
-    SCRATCH["qz%d" % _t] = _sb(456, F8)
-    SCRATCH["sz%d" % _t] = _sb(456, U8)
     SCRATCH["qb%d" % _t] = _sb(128, F8)
     SCRATCH["sb%d" % _t] = _sb(128, U8)
 for _b in range(8):
     SCRATCH["P%d" % _b] = ("psum", [128, 512], F32)
 
-NDMA = 72
+NDMA = 32
 SEMAPHORES = ["eV", "eS", "eP", "eG", "sent", "arr0", "arr1", "arr2"] + ["d%d" % i for i in range(NDMA)]
 
 A = AluOpType
 AF = ActivationFunctionType
 NENG = 8
-STRIP_BY = ("SSSVVVVVVVVVVVVVSSS",) * 3
-HI = (320, 192, 192)
-KEY_CUTS = (0, 32)
-W_CUTS = (256,)
-TURN_BY = "SV"
-SORT_BY = "V"
-GT_BY = "V"
-D4_BY = "V"
-CORNER_BY = "GGGG"
-ZERO_V = 0
-LAST_BY = "VVVV"
-COL_V = ("q", "q8", "q4", "c768", "boff", "c8", "z1", "zd")
-SHIFT_BY = "VVV"
-LIST_CUTS = ((0, 64, 192, 384),) * 3
-RANK_CUTS = ((0, 192, 320),) * 3
-TAIL_WITH = (False, False, False)
-B_WITH = (False, False, False)
-JOIN = (5, 5, 4)
-W_S = (1, 1, 1)
-GATHER_BY = ("SSVSSS",) * 3
-CHUNKS = (((192, 320), (0, 192)),) * 3
-PRE_BY = (("VSSS", "SSSS"),) * 3
-POST_BY = (("SSSS", "SSVV"),) * 3
+HI = 128
+STRIP_BY = "SSSVVVVVSSSSVVVVVVV"
+W_S = (0, 1, 1)
+UNPACK_BY = ("V", "V", "V")
+SORTED_BY = "V"
+TURN_BY = ("S", "S", "S")
+BESIDE = (False, True, False)
+LIST_CUTS = ((0, 64, 192, 384), (0, 64, 192, 384), (0, 64, 160, 256, 384))
+GATHER_BY = ("SSSVSSSSVVSS", "VSSVSSSVSSSS", "SVSSSSSSVVSV")
+RUNS = (((HI, C), (0, HI)), ((HI, C), (0, HI)), ((0, HI), (HI, C)))
+PRE_BY = (("SSSS", "V"), ("VSSS", "V"), ("SSSS", "VSSS"))
+POST_BY = (("S", "V"), ("SSSV", "SSSS"), ("SSVV", "SSVV"))
 J0 = (0, 64, 128, 192, 256)
 CT0 = (0, 384, 704, 960, 1152)
 QC0 = (0, 1536, 1984, 576, 1024)
-FIX, WAKE, ISSUE, DMA, REMOTE, FIRST, GATHER, SCATTER, PASSES = 5, 270, 100, 1000, 1700, 1800, 1.56, 3.8, 3
-PE_FIX, WIDE = 50, {F8: 4, U8: 1, BF: 2, F32: 4}
-PATIENCE = ((120, 2.0), (150, 3.0), (250, 3.0), (300, 2.0), (400, 4.0), (600, 3.0))
+FIX, FIX_BY, PE_FIX, SIGNAL, ISSUE, DMA, REMOTE = 4, 70, 40, 260, 200, 950, (3900, 2000, 1900)
+GATHER, SCATTER, WIDE, URGENT = 1.56, 3.8, {F8: 4, U8: 1, BF: 2, F32: 4}, (0, 0, 600)
+PATIENCE, PASSES = ((120, 2.0), (150, 3.0), (250, 3.0), (300, 2.0), (400, 4.0), (600, 3.0)), 4
 ORDER = []
 
 
@@ -111,7 +97,7 @@ def list_order(eng, cost, before, way, ready, slack, ahead):
     return order, end
 
 
-def issue_order(eng, cost, tail, before):
+def issue_order(eng, cost, tail, before, first):
     n = len(eng)
     after = [{} for _ in range(n)]
     for i in range(n):
@@ -121,7 +107,7 @@ def issue_order(eng, cost, tail, before):
     for slack, ahead in PATIENCE:
         back = [float(i) for i in range(n)]
         for _ in range(PASSES):
-            way = list_order(eng, cost, after, back, tail, slack, ahead)[1]
+            way = [w + x for w, x in zip(list_order(eng, cost, after, back, tail, slack, ahead)[1], first)]
             order, back = list_order(eng, cost, before, way, [0.0] * n, slack, ahead)
             total = max(back[i] + tail[i] for i in range(n))
             if best is None or total < best[0]:
@@ -170,7 +156,7 @@ def rank_program(g, core, T, topo):
 
     def cyc(out, *ins, rate=None):
         if out[4] or ins and ins[0][4]:
-            return FIX + out[2] * (SCATTER if out[4] else GATHER)
+            return FIX_BY + out[2] * (SCATTER if out[4] else GATHER)
         if rate is None:
             rate = 0.5 if out[3] and all(x[3] for x in ins) else 1.0
         return FIX + max(64, out[2] * rate)
@@ -210,7 +196,7 @@ def rank_program(g, core, T, topo):
         if acc is not None:
             kw["accum_out"] = acc[0]
         op("S", lambda: S.activation(out[0], in_[0], f, **kw), [in_, bias, scale], [out] + ([acc] if acc else []),
-           cyc(out, in_, rate=1.0) + (24 if acc else 0))
+           cyc(out, in_, rate=1.0) + (34 if acc else 10))
 
     def move(by, out, in_, scale=None):
         if by == "S":
@@ -241,9 +227,6 @@ def rank_program(g, core, T, topo):
            ISSUE + 0.6 * side[2] * WIDE[SCRATCH[side[1][0][0]][2]], kind="d")
         ops[-1]["lag"] = DMA
 
-    def select(out, in_, pat, base, cm):
-        op("G", lambda: g.affine_select(out[0], in_[0], pat, A.is_ge, 0.0, base, cm), [in_], [out], 205 + 2 * out[2])
-
     names = ("f4", "f8", "g", "f32", "p", "p768", "q", "q2", "cq", "inv16", "m16", "q8", "b2", "t1", "t2", "inv4", "q4",
              "c768", "boff", "c8", "n0", "n1", "z1", "zd")
 
@@ -252,10 +235,7 @@ def rank_program(g, core, T, topo):
         return v("PC", i, i + 1)
 
     def col(name, src, scale, bias):
-        if name in COL_V:
-            ts(pc(name), pc(src), scale, bias, A.mult, A.add)
-        else:
-            act(pc(name), pc(src), AF.Identity, bias=bias, scale=scale)
+        act(pc(name), pc(src), AF.Identity, bias=bias, scale=scale)
 
     def cview(s, a, b):
         k, e = (s + 1) // 4, (s + 1) % 4
@@ -265,9 +245,15 @@ def rank_program(g, core, T, topo):
     def kcol(s):
         return v("H", 16 * s + 15, 16 * s + 16)
 
+    def keys(by, s, a, b):
+        if 16 * s >= HI:
+            return v({"V": "P4", "S": "P5"}[by], a - HI, b - HI)
+        return v({"V": "P0", "S": "P1"}[by], a, b)
+
     rows = v("X", 0, 4 * C)
     dma("S", v("ub"), T.u[:])
-    dma("Y", rows, T.x[:, 0:4 * C])
+    for a, b in RUNS[0]:
+        dma("Y", v("X", 4 * a, 4 * b), T.x[:, 4 * a:4 * b])
     dma("Y", v("X", 4 * C, 4 * E), T.x[:, 4 * C:4 * E], [rows])
     dma("Y", v("qW", cast=dt.uint8), T.wc[:], [rows])
     dma("Y", v("sW"), T.ws[:], [rows])
@@ -291,9 +277,7 @@ def rank_program(g, core, T, topo):
     ms(v("Rst", 0, C, 16), -2 * BIG)
     iota(v("Z16"), [[16, 20], [-32, 16]], -144)
     iota(v("acc"), [[0, 20]], 0)
-    iota(v("Ri"), [[-16, 4], [1, 66]], 0)
-    iota(v("Dr", 64, 264, 66), [[32, 4]], 0)
-    iota(v("Dr", 65, 264, 66), [[0, 4]], 0)
+    iota(v("Ri"), [[-16, 4], [1, 65]], 0)
     iota(v("V16"), [[1, 384]], -192)
     iota(v("one"), [[0, 64]], 1)
     iota(v("I4"), [[0, 96], [1, 4]], 0)
@@ -315,43 +299,26 @@ def rank_program(g, core, T, topo):
     col("t1", "q8", M4 * M4 - 1.0, 1.0)
     col("t2", "b2", (M4 - 1.0) * 4.0 / M4 ** 3, 4.0 / M4 ** 3)
     col("inv4", "t1", pc("t2"), 0.0)
-    if D4_BY == "V":
-        ts(v("D4"), v("I4"), pc("q4"), M4, A.is_gt, A.mult)
-    else:
-        act(v("I4"), v("I4"), AF.Sign, bias=pc("q4"), scale=-1.0)
-        act(v("D4"), v("I4"), AF.Relu, scale=-M4)
+    ts(v("D4"), v("I4"), pc("q4"), M4, A.is_gt, A.mult)
     ts(v("Rj"), v("Ri"), pc("q"), 2.0, A.not_equal, A.mult)
     act(v("Fl"), v("Rj"), AF.Identity, bias=-1.0, scale=1.0)
-    act(v("Fl", 0, 264, 66), v("Rj", 0, 264, 66), AF.Copy, scale=0.0)
+    act(v("Fl", 0, 260, 65), v("Rj", 0, 260, 65), AF.Copy, scale=0.0)
     zq = QC0[4] - J0[4]
     zt = v("CT", 4 * CT0[4], 4 * CT0[4] + 1024)
     ms(zt, 0.0)
     qz("qc", "sc", zq, zq + 256, zt)
     for k in range(4):
-        corner = v("CT", 4 * CT0[k], 4 * CT0[k] + 192)
-        if CORNER_BY[k] == "V":
-            ms(corner, 0.0)
-        else:
-            iota(corner, [[0, 192]], 0)
-    for i, (a, n) in enumerate([(QC0[k] - n, n) for k, n in ((2, 128), (1, 128), (3, 192))] + [
-            (QC0[4] + 128 + K * j, K) for j in sorted(set(JOIN)) if j < 4] + [(QC0[2] + 256, K)] * (min(JOIN) < 3)):
-        if i < ZERO_V and n >= 128:
-            qz("qc", "sc", a, a + n, v("CT", 4 * CT0[4], 4 * (CT0[4] + n)))
-        else:
-            dma("Y", v("qc", a, a + n, cast=dt.uint8), v("qc", zq, zq + n, cast=dt.uint8), [rows])
-            dma("Y", v("sc", a, a + n), v("sc", zq, zq + n), [rows])
+        iota(v("CT", 4 * CT0[k], 4 * CT0[k] + 192), [[0, 192]], 0)
+    for k, n in ((2, 128), (1, 128), (3, 192)):
+        dma("Y", v("qc", QC0[k] - n, QC0[k], cast=dt.uint8), v("qc", zq, zq + n, cast=dt.uint8), [rows])
+        dma("Y", v("sc", QC0[k] - n, QC0[k]), v("sc", zq, zq + n), [rows])
     for q_, s_, a, n in [("pk", "ps", 128, K)] + [("lq%d" % t, "ls%d" % t, 16, 16) for t in range(R)]:
         cp(v(q_, a, a + n, cast=dt.uint32), v("qc", zq, zq + 128, cast=dt.uint32, by=v("oU", 0, n // 16)))
         act(v(s_, a, a + n), v("sc", zq, zq + 128, by=v("oU", 0, n // 16)), AF.Copy)
     iota(v("Z", 0, 256), [[0, 256]], 0)
     iota(v("Bt"), [[0, 512]], 0)
-    if GT_BY == "V":
-        iota(v("GI"), [[1, 8], [0, 64]], 0)
-        ts(v("GT"), v("GI"), pc("g"), None, A.is_equal)
-    else:
-        iota(v("GT"), [[0, 512]], 1)
-        select(v("GI"), v("GT"), [[-16, 8], [0, 64]], 0, 1)
-        select(v("GT"), v("GI"), [[16, 8], [0, 64]], 15, -1)
+    iota(v("GI"), [[1, 8], [0, 64]], 0)
+    ts(v("GT"), v("GI"), pc("g"), None, A.is_equal)
     qz("qg", "sg", 0, 128, v("GT"))
     for h in range(2):
         col("n%d" % h, "f32", 32.0, 16.0 * h)
@@ -375,127 +342,104 @@ def rank_program(g, core, T, topo):
     act(v("sus"), v("su", by=v("oU")), AF.Copy)
     qz("qv", "sv", 0, 128, v("vb"))
 
-    def q_rows():
-        qz("qx", "sx", 0, C, rows)
-
     def q_waits():
         qz("qx", "sx", 256, E, v("X", 1024, 4 * E))
 
-    def unpack(t, by):
+    def unpack(t):
         cp(v("pk", 0, 128, cast=dt.uint32), v("lq%d" % t, cast=dt.uint32, by=o_d))
         act(v("ps", 0, 128), v("ls%d" % t, by=o_d), AF.Copy)
-        bank = {"S": "P3", "V": "P2"}
-        for e in sorted(set(by)):
-            both = []
-            mm(bank[e], "qf", "sf", 0, "pk", "ps", 0, 128, both)
-            mm(bank[e], "qf", "sf", 128, "pk", "ps", 64, 128, both)
+        both = []
+        mm("P3", "qf", "sf", 0, "pk", "ps", 0, 128, both)
+        mm("P3", "qf", "sf", 128, "pk", "ps", 64, 128, both)
         for b in range(4):
-            src = bank[by[b]]
-            move(by[b], v("X", 4 * C + b, 4 * E, 4, p=(0, 16)), (T[src][32 * b:32 * b + 16, 0:K],) + v(src, 0, K)[1:])
+            move(UNPACK_BY[t], v("X", 4 * C + b, 4 * E, 4, p=(0, 16)), (T.P3[32 * b:32 * b + 16, 0:K],) + v("P3", 0, K)[1:])
 
-    def send(t, qb, sb, a):
+    def send(t):
+        qz("qb%d" % t, "sb%d" % t, 0, 128, v("Bt"))
         dst = T.cores[(rank + t + 1) % n_ranks]
         rid, pid, _ = topo.addr(dst)
         m = sum(1 << e for e in topo.engines(core, dst)[0:NENG])
         arr = T.sem["arr%d" % t]
         lq, ls = v("lq%d" % t, 0, 8, cast=dt.uint8), v("ls%d" % t, 0, 8)
-        cq, cs = v(qb, a, a + 8, cast=dt.uint8), v(sb, a, a + 8)
+        cq, cs = v("qb%d" % t, 0, 8, cast=dt.uint8), v("sb%d" % t, 0, 8)
         op("G", lambda: g.remote_dma(lq[0], cq[0], arr, T.sem.sent, pid, rid, m), [cq], [], 360, kind="r")
         op("G", lambda: g.remote_dma(ls[0], cs[0], arr, T.sem.sent, pid, rid, m), [cs], [], 360, kind="r")
-        op("X", None, [cs], [lq, ls], REMOTE + (FIRST if t == 0 else 0), kind="x", info=("arr%d" % t, 2 * NENG))
+        op("X", None, [cs], [lq, ls], REMOTE[t], kind="x", info=("arr%d" % t, 2 * NENG))
 
-    q_rows()
+    def layer(x0, x1, banks, pre_by, fill=0):
+        qz("qz", "sz", K + x0 - fill, K + x1, v("Z", 256 + 4 * (x0 - fill), 256 + 4 * x1))
+        if len(pre_by) == 1:
+            move(pre_by, v("Z64", 4 * x0, 4 * x1), v("Z", 256 + 4 * x0, 256 + 4 * x1), 64.0)
+        for b in range(4):
+            bank, z64 = "P%d" % (banks + b), v("Z64", 4 * x0 + b, 4 * x1, 4)
+            mm(bank, "qW", "sW", 128 * b, "qz", "sz", K + x0 - fill, x1 - x0 + fill)
+            if len(pre_by) == 4:
+                move(pre_by[b], z64, v("Z", 256 + 4 * x0 + b, 256 + 4 * x1, 4), 64.0)
+            tt(v("M64", 4 * x0 + b, 4 * x1, 4), v(bank, fill, fill + x1 - x0), z64, A.add)
+
+    for a, b in RUNS[0]:
+        qz("qx", "sx", a, b, v("X", 4 * a, 4 * b))
     for t in range(R):
-        hi = HI[t]
-
-        def keys(by, s, a, b):
-            if 16 * s >= hi:
-                return v({"V": "P4", "S": "P5"}[by], a - hi, b - hi)
-            return v({"V": "P0", "S": "P1"}[by], a, b)
-
-        if hi < C:
-            mm("P4", "qus", "sus", 0, "qx", "sx", hi, C - hi)
-            mm("P5", "qus", "sus", 0, "qx", "sx", hi, C - hi)
-        mm("P0", "qus", "sus", 0, "qx", "sx", 0, C)
-        mm("P1", "qus", "sus", 0, "qx", "sx", 0, C)
-        cuts = [x for x in KEY_CUTS if x < hi] + [hi] + ([C] if hi < C else [])
-        for a, b in reversed(list(zip(cuts, cuts[1:]))):
-            tt(v("Km", a, b), keys("V", a // 16, a, b), v("Mn", a, b), A.min)
+        for bank, a, n in (("P4", HI, C - HI), ("P5", HI, C - HI), ("P6", 0, HI), ("P0", 0, C), ("P1", 0, C)):
+            mm(bank, "qus", "sus", 0, "qx", "sx", a, n)
+        for a, b in ((HI, C), (K, HI), (0, K)):
+            tt(v("Km", a, b), v("P6", a, b) if a < HI else keys("V", a // 16, a, b), v("Mn", a, b), A.min)
             scan(v("H", a, b), v("Rst", a, b), v("Km", a, b), 0.0, A.add, A.max)
-        for a, b in ((hi, C), (0, hi)) if hi < C else ((0, C),):
+        for a, b in ((HI, C), (0, HI)):
             tt(v("CT", 4 * a, 4 * b, 4), keys("V", a // 16, a, b), v("H", a, b), A.is_lt)
         scan(v("Ds"), v("Z16"), v("CT", 0, 4 * C, 4), -1000.0, A.max, A.add)
-        join = JOIN[t]
-        late = [s for s in range(19) if (s + 1) // 4 >= join and STRIP_BY[t][s] == "V"]
-        for s in range(19):
+        for s in range(15):
             a = 16 * s + 16
             d = v("Dsg", C * s, C * s + C - a)
-            if s in late:
-                continue
-            if STRIP_BY[t][s] == "S":
+            if STRIP_BY[s] == "S":
                 act(d, keys("S", s, a, C), AF.Sign, bias=kcol(s), scale=-1.0)
                 act(cview(s, a, C), d, AF.Relu, acc=v("acc", s, s + 1))
             else:
                 ts(cview(s, a, C), keys("V", s, a, C), kcol(s), None, A.is_lt)
                 act(d, cview(s, a, C), AF.Copy, acc=v("acc", s, s + 1))
         if t > 0:
-            unpack(t - 1, "SSSS")
+            unpack(t - 1)
         q_waits()
-        n = max(128, E - 16 * min(late + [19]) - 16)
-        mm("P6", "qus", "sus", 0, "qx", "sx", E - n, n)
+        mm("P6", "qus", "sus", 0, "qx", "sx", 256, 128)
         mm("P7", "qus", "sus", 0, "qx", "sx", 256, 128)
-        waits_v, waits_s = v("P6", n - K, n), v("P7", K, 128)
+        waits_v, waits_s = v("P6", K, 128), v("P7", K, 128)
         tt(v("Kmw"), waits_v, v("Mn", 0, K), A.min)
         scan(v("Hw"), v("Rst", 0, K), v("Kmw"), 0.0, A.add, A.max)
-        for s in late:
+        for s in range(15, 19):
             a = 16 * s + 16
-            ts(cview(s, a, E), v("P6", a + n - E, n), kcol(s), None, A.is_lt)
+            ts(cview(s, a, E), v("P6", a - 256, 128), kcol(s), None, A.is_lt)
             act(v("Dsg", C * s, C * s + C - a), cview(s, a, C), AF.Copy, acc=v("acc", s, s + 1))
-        w0 = 128 if join < 5 else K
-        for s in range(20):
+        for s in list(range(15)) + [19]:
             k, e = (s + 1) % 20 // 4, (s + 1) % 4
-            w = CT0[4] + w0 + K * k if k < join else CT0[k] + C - J0[k]
-            if s in late:
-                continue
+            w = CT0[4] + 128 + K * k
             if k >= W_S[t]:
                 ts(v("CT", 4 * w + e, 4 * (w + K), 4), waits_v, kcol(s), None, A.is_lt)
             else:
-                act(v("Dw", 256 * k + e, 256 * k + 256, 4), waits_s, AF.Sign, bias=kcol(s), scale=-1.0)
-        for k in range(W_S[t]):
-            w = CT0[4] + w0 + K * k if k < join else CT0[k] + C - J0[k]
-            act(v("CT", 4 * w, 4 * (w + K)), v("Dw", 256 * k, 256 * k + 256), AF.Relu)
-        ranks, counts = [], []
-        for k in range(5):
-            n = C - J0[k] + (K if k >= join else 0) + (K * join if k == 4 else 0)
-            cuts = [0] + [x for x in W_CUTS if k == 4 and x <= n - 128] + [n]
-            for a, b in zip(cuts, cuts[1:]):
-                qz("qc", "sc", QC0[k] + a, QC0[k] + b, v("CT", 4 * (CT0[k] + a), 4 * (CT0[k] + b)))
-        parts = list(zip(RANK_CUTS[t], RANK_CUTS[t][1:]))
+                act(v("Dw", e, 256, 4), waits_s, AF.Sign, bias=kcol(s), scale=-1.0)
+        if W_S[t]:
+            act(v("CT", 4 * (CT0[4] + 128), 4 * (CT0[4] + 192)), v("Dw"), AF.Relu)
+        for k, a, b in [(k, 0, C - J0[k]) for k in range(4)] + [(4, 0, 128), (4, 128, E)]:
+            qz("qc", "sc", QC0[k] + a, QC0[k] + b, v("CT", 4 * (CT0[k] + a), 4 * (CT0[k] + b)))
+        parts, counts = ((0, HI), (HI, C)), []
         for i, (a, b) in enumerate(parts):
             ranks = []
             for k in range(5):
                 if J0[k] < b:
                     mm("P%d" % (2 + i), "qg", "sg", 0, "qc", "sc", QC0[k] - J0[k] + a, b - a, ranks)
         for k in range(5):
-            mm("P4", "qg", "sg", 0, "qc", "sc", QC0[k] + C - J0[k] if k >= join else QC0[4] + w0 + K * k, 128, counts)
+            mm("P4", "qg", "sg", 0, "qc", "sc", QC0[4] + (K if k == 4 else 128 + K * k), 128, counts)
         for s in range(4):
-            act(v("Dr", 66 * s, 66 * s + K), waits_s, AF.Sign, bias=v("Hw", 16 * s + 15, 16 * s + 16), scale=-1.0,
-                acc=v("accd", s, s + 1))
-        act(v("Ar"), v("Dr"), AF.Abs)
-        act(v("Ar", 65, 264, 66), v("accd"), AF.Copy)
+            key = v("Hw", 16 * s + 15, 16 * s + 16)
+            act(v("Dr", K * s, K * s + K), waits_s, AF.Sign, bias=key, scale=-1.0, acc=v("Ar", 65 * s + K, 65 * s + 65))
+            ts(v("Ar", 65 * s, 65 * s + K), waits_v, key, -1.0, A.is_equal, A.mult)
         scan(v("Sr"), v("Fl"), v("Ar"), 0.0, A.mult, A.add)
-        ts(v("oW"), v("Sr", 65, 264, 66), 0.5, pc("q"), A.mult, A.add)
+        ts(v("oW"), v("Sr", K, 260, 65), 0.5, 32.0, A.mult, A.add)
         cp(v("Bb", by=v("oW")), v("V16", C, E))
         act(v("kk"), v("P4", 0, K), AF.Identity, bias=320.0, scale=-1.0)
-        if SORT_BY == "V":
-            cp(v("ks", by=v("oW")), v("kk"))
-        else:
-            scan(v("sB"), v("DD", 0, K), v("Bb"), 0.0, A.mult, A.add)
-            ts(v("oB"), v("sB", 15, K, 16), pc("inv16"), -128.09, A.mult, A.add)
-            act(v("ks"), v("kk", by=v("oB")), AF.Copy)
+        cp(v("ks", by=v("oW")), v("kk"))
         scan(v("pp"), v("one"), v("ks"), -1.0, A.add, A.max)
-        move(TURN_BY[0], v("BT"), v("Bb", by=o_8))
-        move(TURN_BY[1], v("pT"), v("pp", by=o_8))
+        move(SORTED_BY, v("BT"), v("Bb", by=o_8))
+        act(v("pT"), v("pp", by=o_8), AF.Copy)
         scan(v("stl"), v("DD", 0, K), v("pT"), 0.0, A.mult, A.add)
         ts(v("oL"), v("stl", 15, K, 16), pc("inv16"), -0.17, A.mult, A.add)
         for i, (a, b) in enumerate(parts):
@@ -505,93 +449,72 @@ def rank_program(g, core, T, topo):
             scan(v("st", a, b), v("DD", a, b), v("P%d" % (2 + i), 0, b - a), 0.0, A.mult, A.add)
             tt(v("a4", x, y), v("a2", x, y), v("st", a + 15, b, 16), A.subtract)
             ts(v("oR", x, y), v("a4", x, y), pc("inv16"), pc("cq"), A.mult, A.add)
-        row = v("L", K, K + E, by=v("oL"))
+        if BESIDE[t]:
+            iota(v("L2"), [[0, E]], -200)
+            cp(v("L2", by=v("oL")), v("BT"))
+            scan(v("s2"), v("D4", 0, C), v("L2", 0, C), 0.0, A.mult, A.add)
         iota(v("L", E, K + E), [[0, K]], 256)
         for a, b in parts:
             cp(v("L", K, E, by=v("oR", a // 16, b // 16)), v("V16", a, b))
-        tt(v("L", 0, K), row, v("BT"), A.min)
-        cp(row, v("BT"))
-        cuts = LIST_CUTS[t]
-        for a, b in zip(cuts, cuts[1:]):
+        tt(v("L", 0, K), v("L", K, K + E, by=v("oL")), v("BT"), A.min)
+        if not BESIDE[t]:
+            cp(v("L", K, K + E, by=v("oL")), v("BT"))
+        for a, b in zip(LIST_CUTS[t], LIST_CUTS[t][1:]):
             scan(v("s4", a, b), v("D4", a, b), v("L", a, b), 0.0, A.mult, A.add)
-            ts(v("oZ", a // 4, b // 4), v("s4", a + 3, b, 4), pc("inv4"), pc("c768"), A.mult, A.add)
+            pick = v("s4", a + 3, b, 4)
+            if a >= K and BESIDE[t]:
+                pick = v("s5", a // 4, b // 4)
+                tt(pick, v("s4", a + 3, b, 4), v("s2", a - K + 3, b - K, 4), A.max)
+            ts(v("oZ", a // 4, b // 4), pick, pc("inv4"), pc("c768"), A.mult, A.add)
         place, x = {}, K
-        for a, b in CHUNKS[t]:
-            for c in range(a, b, K):
-                place[c], x = x, x + K
+        for a, b in RUNS[t]:
+            for c in range(a, b, 32):
+                place[c], x = x, x + 32
         for i, by in enumerate(GATHER_BY[t]):
-            x = place[K * i - K] if i else 0
-            move(by, v("Z", 256 + 4 * x, 512 + 4 * x), v("X", by=v("oZ", 16 * i, 16 * i + 16)))
-        qt, st_ = "qz%d" % t, "sz%d" % t
-
-        def layer(x0, x1, banks, pre_by, fill=0, more=0):
-            qz(qt, st_, K + x0 - fill, K + x1 + more, v("Z", 256 + 4 * (x0 - fill), 256 + 4 * (x1 + more)))
-            if len(pre_by) == 1:
-                move(pre_by, v("Z64", 4 * x0, 4 * x1), v("Z", 256 + 4 * x0, 256 + 4 * x1), 64.0)
-            for b in range(4):
-                bank, z64 = "P%d" % (banks + b), v("Z64", 4 * x0 + b, 4 * x1, 4)
-                mm(bank, "qW", "sW", 128 * b, qt, st_, K + x0 - fill, x1 - x0 + fill)
-                if len(pre_by) == 4:
-                    move(pre_by[b], z64, v("Z", 256 + 4 * x0 + b, 256 + 4 * x1, 4), 64.0)
-                tt(v("M64", 4 * x0 + b, 4 * x1, 4), v(bank, fill, fill + x1 - x0), z64, A.add)
-
-        def descent(b_at):
-            if SHIFT_BY[t] == "D":
-                for a in range(8):
-                    dma("Y", v("TT2", p=(16 * a, 16 * a + 16)), v("M64", 32 * a, 32 * a + 32, p=(112, 128)))
-                act(b_at, v("TT2"), AF.Copy, scale=1.0 / 64)
-            else:
-                if SHIFT_BY[t] == "V":
-                    for a in range(4):
-                        tr(v("TT", p=(32 * a, 32 * a + 32)), v("M64", 64 * a, 64 * a + 64, p=(96, 128)))
-                else:
-                    tr(v("Bs", p=(96, 128)), v("M64", 0, 256, p=(96, 128)))
-                    for a in range(4):
-                        act(v("TT", p=(32 * a, 32 * a + 32)), v("Bs", 64 * a, 64 * a + 64, p=(96, 128)), AF.Copy)
-                act(v("TT2"), v("TT", by=o_q), AF.Copy, scale=1.0 / 64)
-                tr(b_at, v("TT2"))
-            act(v("Mt"), v("M64", 0, 256, by=o_s), AF.Copy, scale=1.0 / 64)
-            dma("Y", v("X", 4 * C, 4 * E, p=(16, 128)), v("Mt", p=(0, 112)))
-
-        b_at = v("Z", 256 + 4 * E, 288 + 4 * E) if B_WITH[t] else v("Bt", 0, 32)
-        if not TAIL_WITH[t]:
-            layer(0, K, 0, "V", fill=K)
-            descent(b_at)
-        for i, (a, b_) in enumerate(CHUNKS[t]):
-            x0, final = place[a], i == len(CHUNKS[t]) - 1
-            layer(0 if i == 0 and TAIL_WITH[t] else x0, x0 + b_ - a, 4 - 4 * i, PRE_BY[t][i],
-                  more=8 if final and B_WITH[t] else 0)
-            if i == 0 and TAIL_WITH[t]:
-                descent(b_at)
-            post_by = POST_BY[t][i]
+            x, n = place[32 * i - K] if i > 1 else 32 * i, 2 if GATHER_BY[t][i ^ 1] == by else 1
+            if n == 1 or i % 2 == 0:
+                move(by, v("Z", 256 + 4 * x, 256 + 4 * x + 128 * n), v("X", by=v("oZ", 8 * i, 8 * (i + n))))
+        way_to_b = len(ops)
+        layer(0, K, 0, "V", fill=K)
+        for a in range(4):
+            tr(v("TT", p=(32 * a, 32 * a + 32)), v("M64", 64 * a, 64 * a + 64, p=(96, 128)))
+        move(TURN_BY[t], v("TT2"), v("TT", by=o_q), 1.0 / 64)
+        tr(v("Bt", 0, 32), v("TT2"))
+        for o in ops[way_to_b:]:
+            o["first"] = URGENT[t]
+        move("S", v("Mt"), v("M64", 0, 256, by=o_s), 1.0 / 64)
+        dma("Y", v("X", 4 * C, 4 * E, p=(16, 128)), v("Mt", p=(0, 112)))
+        for i, (a, b_) in enumerate(RUNS[t]):
+            x0, post_by = place[a], POST_BY[t][i]
+            layer(x0, x0 + b_ - a, 4 - 4 * i, PRE_BY[t][i])
             for b in range(len(post_by)):
                 st = len(post_by)
                 move(post_by[b], v("X", 4 * a + b, 4 * b_, st), v("M64", 4 * x0 + b, 4 * (x0 + b_ - a), st), 1.0 / 64)
-            if t + 1 < R and HI[t + 1] < C:
+            if t + 1 < R:
                 qz("qx", "sx", a, b_, v("X", 4 * a, 4 * b_))
-        if B_WITH[t]:
-            send(t, qt, st_, K + E)
-        else:
-            qz("qb%d" % t, "sb%d" % t, 0, 128, v("Bt"))
-            send(t, "qb%d" % t, "sb%d" % t, 0)
-        if t + 1 == R or HI[t + 1] == C:
-            q_rows()
+        send(t)
+        for o in ops[-4:]:
+            o["first"] = URGENT[t]
 
-    dma("Y", T.oc[:, 0:1024], v("qx", 0, 256, cast=dt.uint8))
+    qz("qx", "sx", 0, C, rows)
+    dma("Y", T.oc[:, 0:4 * C], v("qx", 0, C, cast=dt.uint8))
+    for k in range(4):
+        dma("Y", T.osc[4 * k:4 * k + 4, 0:C], v("sx", 0, C, p=(32 * k, 32 * k + 4)))
     act(v("LE", 0, C), v("L", K, E), AF.Identity, bias=192.0, scale=1.0)
     act(v("LE", C, E), v("L", 0, K, by=o_8), AF.Identity, bias=192.0, scale=1.0)
     dma("Y", T.le[:], (T.LE[0:128:16, :],) + v("LE")[1:])
-    mm("P0", "qv", "sv", 0, "qx", "sx", 0, 256)
-    act(v("ysb", 0, 256), v("P0", 0, 256), AF.Copy)
-    dma("Y", T.y[:, 0:256], v("ysb", 0, 256))
-    unpack(R - 1, LAST_BY)
-    q_waits()
-    mm("P1", "qv", "sv", 0, "qx", "sx", 256, 128)
-    dma("Y", T.oc[:, 1024:1536], v("qx", 256, E, cast=dt.uint8))
+    mm("P0", "qv", "sv", 0, "qx", "sx", 0, C)
+    act(v("ysb", 0, C), v("P0", 0, C), AF.Copy)
+    dma("Y", T.y[:, 0:C], v("ysb", 0, C))
+    unpack(R - 1)
+    qz("qw", "sw", 0, 128, v("X", 1024, 4 * E))
+    mm("P1", "qv", "sv", 0, "qw", "sw", 0, 128)
+    dma("S", T.oc[:, 4 * C:4 * E], v("qw", K, 128, cast=dt.uint8))
     for k in range(4):
-        dma("YSSS"[k], T.osc[4 * k:4 * k + 4, :], v("sx", p=(32 * k, 32 * k + 4)))
-    cp(v("ysb", 256, E), v("P1", 0, 128))
-    dma("Y", T.y[:, 256:E], v("ysb", 256, E))
+        dma("YYSS"[k], T.osc[4 * k:4 * k + 4, C:E], v("sw", K, 128, p=(32 * k, 32 * k + 4)))
+    cp(v("ysb", C, E), v("P1", K, 128))
+    dma("Y", T.y[:, C:E], v("ysb", C, E))
+
 
     def meets(x, y):
         return x[1] & y[1] and x[2] < y[3] and y[2] < x[3]
@@ -610,13 +533,13 @@ def rank_program(g, core, T, topo):
                     if same and o["info"] is not None and o["info"] is p["info"]:
                         continue
                     if (wrote or writes or reg[1] == -1 and not same) and meets(reg, other):
-                        lag = 0 if same and reg[1] == -1 else p.get("lag", WAKE)
+                        lag = 0 if same and reg[1] == -1 else p.get("lag", SIGNAL)
                         d[j] = max(d.get(j, 0), lag)
             before.append(d)
             for reg, writes in touched(o):
                 seen.setdefault(reg[0], []).append((i, reg, writes))
         ORDER.extend(issue_order([o["e"] for o in ops], [o["c"] for o in ops],
-                                 [o.get("lag", 0) for o in ops], before))
+                                 [o.get("lag", 0) for o in ops], before, [o.get("first", 0) for o in ops]))
     ops = [ops[i] for i in ORDER]
 
     seen, need = {}, []

from concourse.mybir import dt, AluOpType, ActivationFunctionType

C, K, E, R = 320, 64, 384, 3
BIG = 1e29
M = 16384.0
M4 = 8192.0
F8, U8, U16, BF, F32, I32 = "float8_e4m3fn_x4", "uint8", "uint16", "bfloat16", "float32", "int32"


def _sb(n, d):
    return ("sbuf", [128, n], d)


SCRATCH = {
    "X": _sb(1536, BF), "Z": _sb(1792, BF), "Z64": _sb(1536, BF), "M64": _sb(1536, BF),
    "Mt": _sb(256, BF), "TT": _sb(64, BF), "TT2": _sb(32, BF), "Bt": _sb(512, BF), "ub": _sb(512, BF), "vb": _sb(512, BF),
    "qu": _sb(128, F8), "su": _sb(128, U8), "qus": _sb(128, F8), "sus": _sb(128, U8),
    "qv": _sb(128, F8), "sv": _sb(128, U8), "qW": _sb(512, F8), "sW": _sb(512, U8),
    "qx": _sb(384, F8), "sx": _sb(384, U8), "qz": _sb(448, F8), "sz": _sb(448, U8),
    "CT": _sb(6144, BF), "qc": _sb(2176, F8), "sc": _sb(2176, U8), "Dsg": _sb(6080, BF), "Dw": _sb(256, BF),
    "GI": _sb(512, BF), "GT": _sb(512, BF), "qg": _sb(128, F8), "sg": _sb(128, U8),
    "J": _sb(512, F32), "JA": _sb(1024, BF), "F": _sb(1024, BF), "qf": _sb(256, F8), "sf": _sb(256, U8),
    "pk": _sb(192, F8), "ps": _sb(192, U8), "qw": _sb(128, F8), "sw": _sb(128, U8),
    "Km": _sb(320, F32), "H": _sb(320, F32), "Kmw": _sb(64, F32), "Hw": _sb(64, F32),
    "Ds": _sb(320, BF), "acc": _sb(20, F32), "a1": _sb(20, F32), "a2": _sb(20, F32), "a4": _sb(20, F32),
    "st": _sb(320, F32), "L": _sb(448, BF), "L2": _sb(384, BF), "Bb": _sb(64, BF), "BT": _sb(64, BF),
    "s2": _sb(320, BF), "s4": _sb(384, BF), "s5": _sb(96, BF), "Dr": _sb(256, BF), "Ar": _sb(260, F32), "Sr": _sb(260, F32),
    "kk": _sb(64, F32), "ks": _sb(64, F32), "pp": _sb(64, F32), "pT": _sb(64, F32), "stl": _sb(64, F32),
    "LE": _sb(384, F32), "ysb": _sb(384, F32),
    "oR": _sb(20, U16), "oZ": _sb(96, U16), "oW": _sb(4, U16), "oL": _sb(4, U16), "oU": _sb(8, U16), "oC": _sb(32, U16),
    "pI": _sb(4, I32), "pJ": _sb(4, I32), "PC": _sb(24, F32), "IU": _sb(320, F32), "IA": _sb(320, F32),
    "IB": _sb(320, F32), "IC": _sb(320, F32), "DD": _sb(320, F32), "Mn": _sb(320, F32), "Rst": _sb(320, BF),
    "Z16": _sb(320, BF), "I4": _sb(384, BF), "D4": _sb(384, BF), "V16": _sb(384, BF), "IO": _sb(64, F32),
    "IP": _sb(32, F32), "Ri": _sb(260, BF), "Rj": _sb(260, BF), "Fl": _sb(260, BF), "one": _sb(64, F32),
}
for _t in range(R):
    SCRATCH["lq%d" % _t] = _sb(32, F8)
    SCRATCH["ls%d" % _t] = _sb(32, U8)
    SCRATCH["qb%d" % _t] = _sb(128, F8)
    SCRATCH["sb%d" % _t] = _sb(128, U8)
for _b in range(8):
    SCRATCH["P%d" % _b] = ("psum", [128, 512], F32)

NDMA = 32
SEMAPHORES = ["eV", "eS", "eP", "eG", "sent", "arr0", "arr1", "arr2"] + ["d%d" % i for i in range(NDMA)]

A = AluOpType
AF = ActivationFunctionType
NENG = 8
HI = 128
STRIP_BY = "SSSVVVVVSSSSVVVVVVV"
W_S = (0, 1, 1)
UNPACK_BY = ("V", "V", "V")
SORTED_BY = "V"
TURN_BY = ("S", "S", "S")
BESIDE = (False, True, False)
LIST_CUTS = ((0, 64, 192, 384), (0, 64, 192, 384), (0, 64, 160, 256, 384))
GATHER_BY = ("SSSVSSSSVVSS", "VSSVSSSVSSSS", "SVSSSSSSVVSV")
RUNS = (((HI, C), (0, HI)), ((HI, C), (0, HI)), ((0, HI), (HI, C)))
PRE_BY = (("SSSS", "V"), ("VSSS", "V"), ("SSSS", "VSSS"))
POST_BY = (("S", "V"), ("SSSV", "SSSS"), ("SSVV", "SSVV"))
J0 = (0, 64, 128, 192, 256)
CT0 = (0, 384, 704, 960, 1152)
QC0 = (0, 1536, 1984, 576, 1024)
FIX, FIX_BY, PE_FIX, SIGNAL, ISSUE, DMA, REMOTE = 4, 70, 40, 260, 200, 950, (3900, 2000, 1900)
GATHER, SCATTER, WIDE, URGENT = 1.56, 3.8, {F8: 4, U8: 1, BF: 2, F32: 4}, (0, 0, 600)
PATIENCE, PASSES = ((120, 2.0), (150, 3.0), (250, 3.0), (300, 2.0), (400, 4.0), (600, 3.0)), 4
ORDER = []


def list_order(eng, cost, before, way, ready, slack, ahead):
    n = len(eng)
    later = [[] for _ in range(n)]
    for i in range(n):
        for j in before[i]:
            later[j].append(i)
    free, left, ready, order, end = {}, [len(d) for d in before], list(ready), [], [0.0] * n
    pool = set(i for i in range(n) if not left[i])

    def start(i):
        return max(ready[i], free.get(eng[i], 0.0))
    while pool:
        first = min(pool, key=lambda i: (start(i), i))
        e, now = eng[first], start(first)
        i = max((i for i in pool if eng[i] == e and start(i) <= now + slack),
                key=lambda i: (way[i] - ahead * (start(i) - now), -i))
        end[i] = start(i) + cost[i]
        if e != "X":
            free[e] = end[i]
        pool.remove(i)
        order.append(i)
        for k in later[i]:
            ready[k] = max(ready[k], end[i] + before[k][i])
            left[k] -= 1
            if not left[k]:
                pool.add(k)
    return order, end


def issue_order(eng, cost, tail, before, first):
    n = len(eng)
    after = [{} for _ in range(n)]
    for i in range(n):
        for j, lag in before[i].items():
            after[j][i] = lag
    best = None
    for slack, ahead in PATIENCE:
        back = [float(i) for i in range(n)]
        for _ in range(PASSES):
            way = [w + x for w, x in zip(list_order(eng, cost, after, back, tail, slack, ahead)[1], first)]
            order, back = list_order(eng, cost, before, way, [0.0] * n, slack, ahead)
            total = max(back[i] + tail[i] for i in range(n))
            if best is None or total < best[0]:
                best = (total, order)
    return best[1]


def rank_program(g, core, T, topo):
    rank = T.rank_of(core)
    if rank is None:
        return
    n_ranks = len(T.cores)
    ops = []
    V, S, P = g.vector, g.scalar, g.tensor

    def v(name, a=0, b=None, st=1, p=(0, 128), cast=None, by=None):
        t = T[name]
        if b is None:
            b = t.shape[1]
        ap = t[p[0]:p[1], a:b:st] if st > 1 else t[p[0]:p[1], a:b]
        if cast is not None:
            ap = ap.bitcast(cast)
        m = ((1 << (b - a)) - 1) << a if st == 1 else sum(1 << i for i in range(a, b, st))
        if SCRATCH[name][0] == "psum":
            m, p = -1, (0, 128)
        reg = [(name, m, p[0], p[1])]
        n = len(range(a, b, st))
        if by is not None:
            ap = ap.indirect(by[0])
            reg = reg + by[1]
            n = 16 * by[2]
        return (ap, reg, n, SCRATCH[name][2] == BF, by is not None)

    def op(eng, fn, rd, wr, cycles, kind="c", info=None):
        r, w = [], []
        for x in rd:
            if isinstance(x, tuple):
                r += x[1]
        for x in wr:
            w.append(x[1][0])
            r += x[1][1:]
        ops.append({"e": eng, "fn": fn, "rd": r, "wr": w, "k": kind, "info": info, "c": cycles})

    def a_(x):
        return x[0] if isinstance(x, tuple) else x

    def cyc(out, *ins, rate=None):
        if out[4] or ins and ins[0][4]:
            return FIX_BY + out[2] * (SCATTER if out[4] else GATHER)
        if rate is None:
            rate = 0.5 if out[3] and all(x[3] for x in ins) else 1.0
        return FIX + max(64, out[2] * rate)

    def ts(out, in0, s1, s2, o0, o1=None):
        if o1 is None:
            op("V", lambda: V.tensor_scalar(out[0], in0[0], a_(s1), None, o0), [in0, s1], [out], cyc(out, in0))
        else:
            op("V", lambda: V.tensor_scalar(out[0], in0[0], a_(s1), a_(s2), o0, o1), [in0, s1, s2], [out], cyc(out, in0))

    def tt(out, in0, in1, o):
        op("V", lambda: V.tensor_tensor(out[0], in0[0], in1[0], o), [in0, in1], [out],
           cyc(out, in0, rate=1.0 if in0[1][0][1] == -1 else 2.0))

    def cp(out, in_):
        op("V", lambda: V.tensor_copy(out[0], in_[0]), [in_], [out], cyc(out, in_))

    def ms(out, c):
        op("V", lambda: V.memset(out[0], c), [], [out], cyc(out))

    def scan(out, d0, d1, init, o0, o1):
        op("V", lambda: V.tensor_tensor_scan(out[0], d0[0], d1[0], init, o0, o1), [d0, d1], [out], cyc(out, d0, d1))

    def qz(q, s, a, b, in_):
        qq, ss = v(q, a, b), v(s, a, b)
        op("V", lambda: V.quantize_mx(qq[0], ss[0], in_[0]), [in_], [qq, ss], FIX + 15 + 0.265 * in_[2])

    def tr(out, in_):
        op("V", lambda: V.transpose(out[0], in_[0]), [in_], [out], cyc(out, in_))

    def act(out, in_, f, bias=None, scale=None, acc=None):
        kw = {}
        if bias is not None:
            kw["bias"] = a_(bias)
        if scale is not None:
            kw["scale"] = a_(scale)
        if acc is not None:
            kw["accum_out"] = acc[0]
        op("S", lambda: S.activation(out[0], in_[0], f, **kw), [in_, bias, scale], [out] + ([acc] if acc else []),
           cyc(out, in_, rate=1.0) + (34 if acc else 10))

    def move(by, out, in_, scale=None):
        if by == "S":
            act(out, in_, AF.Copy, scale=scale)
        elif scale is None:
            cp(out, in_)
        else:
            ts(out, in_, scale, None, A.mult)

    def mm(bank, lq, ls, la, rq, rs, a, n, group=None):
        o, w = T[bank][:, 0:n], [v(lq, la, la + 128), v(ls, la, la + 128), v(rq, a, a + n), v(rs, a, a + n)]

        def fn():
            start, stop = group is None or group[0]["fn"] is fn, group is None or group[-1]["fn"] is fn
            return P.matmul_mx(o, w[0][0], w[1][0], w[2][0], w[3][0], start, stop)
        op("P", fn, w, [v(bank)], PE_FIX + n, info=group)

    def iota(out, pat, base, cm=0, small=True):
        if small:
            op("G", lambda: g.iota(out[0], pat, base, cm, allow_small_or_imprecise_dtypes=True), [], [out], 160 + 2 * out[2])
        else:
            op("G", lambda: g.iota(out[0], pat, base, cm), [], [out], 160 + 2 * out[2])

    def dma(q, out, in_, after=()):
        e = g.sync if q == "Y" else g.scalar
        side = out if isinstance(out, tuple) else in_
        op(q, lambda: e.dma_start(a_(out), a_(in_)), [in_] + list(after), [out] if isinstance(out, tuple) else [],
           ISSUE + 0.6 * side[2] * WIDE[SCRATCH[side[1][0][0]][2]], kind="d")
        ops[-1]["lag"] = DMA

    names = ("f4", "f8", "g", "f32", "p", "p768", "q", "q2", "cq", "inv16", "m16", "q8", "b2", "t1", "t2", "inv4", "q4",
             "c768", "boff", "c8", "n0", "n1", "z1", "zd")

    def pc(name):
        i = names.index(name)
        return v("PC", i, i + 1)

    def col(name, src, scale, bias):
        act(pc(name), pc(src), AF.Identity, bias=bias, scale=scale)

    def cview(s, a, b):
        k, e = (s + 1) // 4, (s + 1) % 4
        w = CT0[k] - J0[k]
        return v("CT", 4 * (w + a) + e, 4 * (w + b), 4)

    def kcol(s):
        return v("H", 16 * s + 15, 16 * s + 16)

    def keys(by, s, a, b):
        if 16 * s >= HI:
            return v({"V": "P4", "S": "P5"}[by], a - HI, b - HI)
        return v({"V": "P0", "S": "P1"}[by], a, b)

    rows = v("X", 0, 4 * C)
    dma("S", v("ub"), T.u[:])
    for a, b in RUNS[0]:
        dma("Y", v("X", 4 * a, 4 * b), T.x[:, 4 * a:4 * b])
    dma("Y", v("X", 4 * C, 4 * E), T.x[:, 4 * C:4 * E], [rows])
    dma("Y", v("qW", cast=dt.uint8), T.wc[:], [rows])
    dma("Y", v("sW"), T.ws[:], [rows])
    dma("Y", v("vb"), T.v[:], [rows])

    for i in range(4):
        iota(v("pI", i, i + 1), [[0, 1]], 0, 8 >> i, small=False)
    iota(pc("p"), [[0, 1]], 0, 1)
    ts(v("pJ", 0, 4), v("pI", 0, 4), 5, None, A.logical_shift_right)
    cp(v("PC", 0, 4), v("pJ", 0, 4))
    col("q", "g", -16.0, pc("p"))
    iota(pc("p768"), [[0, 1]], 768, 1)
    col("c768", "f4", -4.0, pc("p768"))
    col("q4", "g", -4.0, pc("f4"))
    col("q8", "g", -2.0, pc("f8"))
    col("b2", "f8", -2.0, pc("f4"))
    iota(v("IU"), [[0, 20], [1, 16]], 0)
    iota(v("IO", 0, 8), [[16, 8]], 0)
    cp(v("oU"), v("IO", 0, 8))
    ms(v("Rst"), 0.0)
    ms(v("Rst", 0, C, 16), -2 * BIG)
    iota(v("Z16"), [[16, 20], [-32, 16]], -144)
    iota(v("acc"), [[0, 20]], 0)
    iota(v("Ri"), [[-16, 4], [1, 65]], 0)
    iota(v("V16"), [[1, 384]], -192)
    iota(v("one"), [[0, 64]], 1)
    iota(v("I4"), [[0, 96], [1, 4]], 0)
    iota(v("J"), [[64, 4], [1, 32], [-64, 4]], 0, -1)
    iota(v("IO", 16, 32), [[4, 8], [128, 2]], -768)
    iota(v("IO", 32, 36), [[2, 4]], 0, 8)
    iota(v("IO", 36, 38), [[32, 2]], 16)
    iota(v("IO", 38, 46), [[64, 2], [2, 4]], 0, -64)
    act(v("IC"), v("IU"), AF.Abs, bias=pc("q"), scale=-1.0)
    act(v("Mn"), v("IC"), AF.Identity, bias=BIG, scale=-2 * BIG)
    col("q2", "q", 1.0, 2.0)
    act(v("IA"), v("IU"), AF.Relu, bias=pc("q2"), scale=-1.0)
    act(v("IB"), v("IA"), AF.Relu, bias=2.0, scale=-1.0)
    act(v("IA"), v("IB"), AF.Abs, bias=-(1.0 + 0.5 / M), scale=1.0)
    act(v("DD"), v("IA"), AF.Identity, bias=M + 0.5, scale=-M)
    col("cq", "q", 1.0, 144.15)
    ts(pc("inv16"), pc("q"), 15.0, 1.0 / M, A.is_equal, A.max)
    col("m16", "inv16", -M, M + 1.0)
    col("t1", "q8", M4 * M4 - 1.0, 1.0)
    col("t2", "b2", (M4 - 1.0) * 4.0 / M4 ** 3, 4.0 / M4 ** 3)
    col("inv4", "t1", pc("t2"), 0.0)
    ts(v("D4"), v("I4"), pc("q4"), M4, A.is_gt, A.mult)
    ts(v("Rj"), v("Ri"), pc("q"), 2.0, A.not_equal, A.mult)
    act(v("Fl"), v("Rj"), AF.Identity, bias=-1.0, scale=1.0)
    act(v("Fl", 0, 260, 65), v("Rj", 0, 260, 65), AF.Copy, scale=0.0)
    zq = QC0[4] - J0[4]
    zt = v("CT", 4 * CT0[4], 4 * CT0[4] + 1024)
    ms(zt, 0.0)
    qz("qc", "sc", zq, zq + 256, zt)
    for k in range(4):
        iota(v("CT", 4 * CT0[k], 4 * CT0[k] + 192), [[0, 192]], 0)
    for k, n in ((2, 128), (1, 128), (3, 192)):
        dma("Y", v("qc", QC0[k] - n, QC0[k], cast=dt.uint8), v("qc", zq, zq + n, cast=dt.uint8), [rows])
        dma("Y", v("sc", QC0[k] - n, QC0[k]), v("sc", zq, zq + n), [rows])
    for q_, s_, a, n in [("pk", "ps", 128, K)] + [("lq%d" % t, "ls%d" % t, 16, 16) for t in range(R)]:
        cp(v(q_, a, a + n, cast=dt.uint32), v("qc", zq, zq + 128, cast=dt.uint32, by=v("oU", 0, n // 16)))
        act(v(s_, a, a + n), v("sc", zq, zq + 128, by=v("oU", 0, n // 16)), AF.Copy)
    iota(v("Z", 0, 256), [[0, 256]], 0)
    iota(v("Bt"), [[0, 512]], 0)
    iota(v("GI"), [[1, 8], [0, 64]], 0)
    ts(v("GT"), v("GI"), pc("g"), None, A.is_equal)
    qz("qg", "sg", 0, 128, v("GT"))
    for h in range(2):
        col("n%d" % h, "f32", 32.0, 16.0 * h)
        act(v("JA", 512 * h, 512 * h + 512), v("J"), AF.Abs, bias=pc("n%d" % h), scale=1.0)
        act(v("F", 512 * h, 512 * h + 512), v("JA", 512 * h, 512 * h + 512), AF.Relu, bias=1.0, scale=-1.0)
    qz("qf", "sf", 0, 256, v("F"))
    col("boff", "q4", 32.0, pc("c768"))
    col("c8", "f8", -64.0, pc("q8"))
    col("z1", "f8", 512.0, pc("q8"))
    col("zd", "f32", 128.0, pc("z1"))
    act(v("IP", 0, 16), v("IO", 16, 32), AF.Identity, bias=pc("boff"), scale=1.0)
    act(v("IP", 16, 20), v("IO", 32, 36), AF.Identity, bias=pc("c8"), scale=1.0)
    act(v("IP", 20, 22), v("IO", 36, 38), AF.Identity, bias=pc("q"), scale=1.0)
    act(v("IO", 48, 56), v("IO", 38, 46), AF.Abs, bias=pc("zd"), scale=1.0)
    act(v("IO", 56, 64), v("IO", 48, 56), AF.Relu, bias=16.0, scale=-1.0)
    act(v("IP", 22, 30), v("IO", 56, 64), AF.Identity, bias=16.0, scale=-1.0)
    cp(v("oC", 0, 30), v("IP", 0, 30))
    o_s, o_8, o_q, o_d = v("oC", 0, 16), v("oC", 16, 20), v("oC", 20, 22), v("oC", 22, 30)
    qz("qu", "su", 0, 128, v("ub"))
    cp(v("qus", cast=dt.uint32), v("qu", cast=dt.uint32, by=v("oU")))
    act(v("sus"), v("su", by=v("oU")), AF.Copy)
    qz("qv", "sv", 0, 128, v("vb"))

    def q_waits():
        qz("qx", "sx", 256, E, v("X", 1024, 4 * E))

    def unpack(t):
        cp(v("pk", 0, 128, cast=dt.uint32), v("lq%d" % t, cast=dt.uint32, by=o_d))
        act(v("ps", 0, 128), v("ls%d" % t, by=o_d), AF.Copy)
        both = []
        mm("P3", "qf", "sf", 0, "pk", "ps", 0, 128, both)
        mm("P3", "qf", "sf", 128, "pk", "ps", 64, 128, both)
        for b in range(4):
            move(UNPACK_BY[t], v("X", 4 * C + b, 4 * E, 4, p=(0, 16)), (T.P3[32 * b:32 * b + 16, 0:K],) + v("P3", 0, K)[1:])

    def send(t):
        qz("qb%d" % t, "sb%d" % t, 0, 128, v("Bt"))
        dst = T.cores[(rank + t + 1) % n_ranks]
        rid, pid, _ = topo.addr(dst)
        m = sum(1 << e for e in topo.engines(core, dst)[0:NENG])
        arr = T.sem["arr%d" % t]
        lq, ls = v("lq%d" % t, 0, 8, cast=dt.uint8), v("ls%d" % t, 0, 8)
        cq, cs = v("qb%d" % t, 0, 8, cast=dt.uint8), v("sb%d" % t, 0, 8)
        op("G", lambda: g.remote_dma(lq[0], cq[0], arr, T.sem.sent, pid, rid, m), [cq], [], 360, kind="r")
        op("G", lambda: g.remote_dma(ls[0], cs[0], arr, T.sem.sent, pid, rid, m), [cs], [], 360, kind="r")
        op("X", None, [cs], [lq, ls], REMOTE[t], kind="x", info=("arr%d" % t, 2 * NENG))

    def layer(x0, x1, banks, pre_by, fill=0):
        qz("qz", "sz", K + x0 - fill, K + x1, v("Z", 256 + 4 * (x0 - fill), 256 + 4 * x1))
        if len(pre_by) == 1:
            move(pre_by, v("Z64", 4 * x0, 4 * x1), v("Z", 256 + 4 * x0, 256 + 4 * x1), 64.0)
        for b in range(4):
            bank, z64 = "P%d" % (banks + b), v("Z64", 4 * x0 + b, 4 * x1, 4)
            mm(bank, "qW", "sW", 128 * b, "qz", "sz", K + x0 - fill, x1 - x0 + fill)
            if len(pre_by) == 4:
                move(pre_by[b], z64, v("Z", 256 + 4 * x0 + b, 256 + 4 * x1, 4), 64.0)
            tt(v("M64", 4 * x0 + b, 4 * x1, 4), v(bank, fill, fill + x1 - x0), z64, A.add)

    for a, b in RUNS[0]:
        qz("qx", "sx", a, b, v("X", 4 * a, 4 * b))
    for t in range(R):
        for bank, a, n in (("P4", HI, C - HI), ("P5", HI, C - HI), ("P6", 0, HI), ("P0", 0, C), ("P1", 0, C)):
            mm(bank, "qus", "sus", 0, "qx", "sx", a, n)
        for a, b in ((HI, C), (K, HI), (0, K)):
            tt(v("Km", a, b), v("P6", a, b) if a < HI else keys("V", a // 16, a, b), v("Mn", a, b), A.min)
            scan(v("H", a, b), v("Rst", a, b), v("Km", a, b), 0.0, A.add, A.max)
        for a, b in ((HI, C), (0, HI)):
            tt(v("CT", 4 * a, 4 * b, 4), keys("V", a // 16, a, b), v("H", a, b), A.is_lt)
        scan(v("Ds"), v("Z16"), v("CT", 0, 4 * C, 4), -1000.0, A.max, A.add)
        for s in range(15):
            a = 16 * s + 16
            d = v("Dsg", C * s, C * s + C - a)
            if STRIP_BY[s] == "S":
                act(d, keys("S", s, a, C), AF.Sign, bias=kcol(s), scale=-1.0)
                act(cview(s, a, C), d, AF.Relu, acc=v("acc", s, s + 1))
            else:
                ts(cview(s, a, C), keys("V", s, a, C), kcol(s), None, A.is_lt)
                act(d, cview(s, a, C), AF.Copy, acc=v("acc", s, s + 1))
        if t > 0:
            unpack(t - 1)
        q_waits()
        mm("P6", "qus", "sus", 0, "qx", "sx", 256, 128)
        mm("P7", "qus", "sus", 0, "qx", "sx", 256, 128)
        waits_v, waits_s = v("P6", K, 128), v("P7", K, 128)
        tt(v("Kmw"), waits_v, v("Mn", 0, K), A.min)
        scan(v("Hw"), v("Rst", 0, K), v("Kmw"), 0.0, A.add, A.max)
        for s in range(15, 19):
            a = 16 * s + 16
            ts(cview(s, a, E), v("P6", a - 256, 128), kcol(s), None, A.is_lt)
            act(v("Dsg", C * s, C * s + C - a), cview(s, a, C), AF.Copy, acc=v("acc", s, s + 1))
        for s in list(range(15)) + [19]:
            k, e = (s + 1) % 20 // 4, (s + 1) % 4
            w = CT0[4] + 128 + K * k
            if k >= W_S[t]:
                ts(v("CT", 4 * w + e, 4 * (w + K), 4), waits_v, kcol(s), None, A.is_lt)
            else:
                act(v("Dw", e, 256, 4), waits_s, AF.Sign, bias=kcol(s), scale=-1.0)
        if W_S[t]:
            act(v("CT", 4 * (CT0[4] + 128), 4 * (CT0[4] + 192)), v("Dw"), AF.Relu)
        for k, a, b in [(k, 0, C - J0[k]) for k in range(4)] + [(4, 0, 128), (4, 128, E)]:
            qz("qc", "sc", QC0[k] + a, QC0[k] + b, v("CT", 4 * (CT0[k] + a), 4 * (CT0[k] + b)))
        parts, counts = ((0, HI), (HI, C)), []
        for i, (a, b) in enumerate(parts):
            ranks = []
            for k in range(5):
                if J0[k] < b:
                    mm("P%d" % (2 + i), "qg", "sg", 0, "qc", "sc", QC0[k] - J0[k] + a, b - a, ranks)
        for k in range(5):
            mm("P4", "qg", "sg", 0, "qc", "sc", QC0[4] + (K if k == 4 else 128 + K * k), 128, counts)
        for s in range(4):
            key = v("Hw", 16 * s + 15, 16 * s + 16)
            act(v("Dr", K * s, K * s + K), waits_s, AF.Sign, bias=key, scale=-1.0, acc=v("Ar", 65 * s + K, 65 * s + 65))
            ts(v("Ar", 65 * s, 65 * s + K), waits_v, key, -1.0, A.is_equal, A.mult)
        scan(v("Sr"), v("Fl"), v("Ar"), 0.0, A.mult, A.add)
        ts(v("oW"), v("Sr", K, 260, 65), 0.5, 32.0, A.mult, A.add)
        cp(v("Bb", by=v("oW")), v("V16", C, E))
        act(v("kk"), v("P4", 0, K), AF.Identity, bias=320.0, scale=-1.0)
        cp(v("ks", by=v("oW")), v("kk"))
        scan(v("pp"), v("one"), v("ks"), -1.0, A.add, A.max)
        move(SORTED_BY, v("BT"), v("Bb", by=o_8))
        act(v("pT"), v("pp", by=o_8), AF.Copy)
        scan(v("stl"), v("DD", 0, K), v("pT"), 0.0, A.mult, A.add)
        ts(v("oL"), v("stl", 15, K, 16), pc("inv16"), -0.17, A.mult, A.add)
        for i, (a, b) in enumerate(parts):
            x, y = a // 16, b // 16
            tt(v("a1", x, y), v("Ds", a + 15, b, 16), v("acc", x, y), A.add)
            act(v("a2", x, y), v("a1", x, y), AF.Copy, scale=pc("m16"))
            scan(v("st", a, b), v("DD", a, b), v("P%d" % (2 + i), 0, b - a), 0.0, A.mult, A.add)
            tt(v("a4", x, y), v("a2", x, y), v("st", a + 15, b, 16), A.subtract)
            ts(v("oR", x, y), v("a4", x, y), pc("inv16"), pc("cq"), A.mult, A.add)
        if BESIDE[t]:
            iota(v("L2"), [[0, E]], -200)
            cp(v("L2", by=v("oL")), v("BT"))
            scan(v("s2"), v("D4", 0, C), v("L2", 0, C), 0.0, A.mult, A.add)
        iota(v("L", E, K + E), [[0, K]], 256)
        for a, b in parts:
            cp(v("L", K, E, by=v("oR", a // 16, b // 16)), v("V16", a, b))
        tt(v("L", 0, K), v("L", K, K + E, by=v("oL")), v("BT"), A.min)
        if not BESIDE[t]:
            cp(v("L", K, K + E, by=v("oL")), v("BT"))
        for a, b in zip(LIST_CUTS[t], LIST_CUTS[t][1:]):
            scan(v("s4", a, b), v("D4", a, b), v("L", a, b), 0.0, A.mult, A.add)
            pick = v("s4", a + 3, b, 4)
            if a >= K and BESIDE[t]:
                pick = v("s5", a // 4, b // 4)
                tt(pick, v("s4", a + 3, b, 4), v("s2", a - K + 3, b - K, 4), A.max)
            ts(v("oZ", a // 4, b // 4), pick, pc("inv4"), pc("c768"), A.mult, A.add)
        place, x = {}, K
        for a, b in RUNS[t]:
            for c in range(a, b, 32):
                place[c], x = x, x + 32
        for i, by in enumerate(GATHER_BY[t]):
            x, n = place[32 * i - K] if i > 1 else 32 * i, 2 if GATHER_BY[t][i ^ 1] == by else 1
            if n == 1 or i % 2 == 0:
                move(by, v("Z", 256 + 4 * x, 256 + 4 * x + 128 * n), v("X", by=v("oZ", 8 * i, 8 * (i + n))))
        way_to_b = len(ops)
        layer(0, K, 0, "V", fill=K)
        for a in range(4):
            tr(v("TT", p=(32 * a, 32 * a + 32)), v("M64", 64 * a, 64 * a + 64, p=(96, 128)))
        move(TURN_BY[t], v("TT2"), v("TT", by=o_q), 1.0 / 64)
        tr(v("Bt", 0, 32), v("TT2"))
        for o in ops[way_to_b:]:
            o["first"] = URGENT[t]
        move("S", v("Mt"), v("M64", 0, 256, by=o_s), 1.0 / 64)
        dma("Y", v("X", 4 * C, 4 * E, p=(16, 128)), v("Mt", p=(0, 112)))
        for i, (a, b_) in enumerate(RUNS[t]):
            x0, post_by = place[a], POST_BY[t][i]
            layer(x0, x0 + b_ - a, 4 - 4 * i, PRE_BY[t][i])
            for b in range(len(post_by)):
                st = len(post_by)
                move(post_by[b], v("X", 4 * a + b, 4 * b_, st), v("M64", 4 * x0 + b, 4 * (x0 + b_ - a), st), 1.0 / 64)
            if t + 1 < R:
                qz("qx", "sx", a, b_, v("X", 4 * a, 4 * b_))
        send(t)
        for o in ops[-4:]:
            o["first"] = URGENT[t]

    qz("qx", "sx", 0, C, rows)
    dma("Y", T.oc[:, 0:4 * C], v("qx", 0, C, cast=dt.uint8))
    for k in range(4):
        dma("Y", T.osc[4 * k:4 * k + 4, 0:C], v("sx", 0, C, p=(32 * k, 32 * k + 4)))
    act(v("LE", 0, C), v("L", K, E), AF.Identity, bias=192.0, scale=1.0)
    act(v("LE", C, E), v("L", 0, K, by=o_8), AF.Identity, bias=192.0, scale=1.0)
    dma("Y", T.le[:], (T.LE[0:128:16, :],) + v("LE")[1:])
    mm("P0", "qv", "sv", 0, "qx", "sx", 0, C)
    act(v("ysb", 0, C), v("P0", 0, C), AF.Copy)
    dma("Y", T.y[:, 0:C], v("ysb", 0, C))
    unpack(R - 1)
    qz("qw", "sw", 0, 128, v("X", 1024, 4 * E))
    mm("P1", "qv", "sv", 0, "qw", "sw", 0, 128)
    dma("S", T.oc[:, 4 * C:4 * E], v("qw", K, 128, cast=dt.uint8))
    for k in range(4):
        dma("YYSS"[k], T.osc[4 * k:4 * k + 4, C:E], v("sw", K, 128, p=(32 * k, 32 * k + 4)))
    cp(v("ysb", C, E), v("P1", K, 128))
    dma("Y", T.y[:, C:E], v("ysb", C, E))


    def meets(x, y):
        return x[1] & y[1] and x[2] < y[3] and y[2] < x[3]

    def touched(o):
        return [(x, False) for x in o["rd"]] + [(x, True) for x in o["wr"]]

    if not ORDER:
        seen, before = {}, []
        for i, o in enumerate(ops):
            d = {}
            for reg, writes in touched(o):
                for j, other, wrote in seen.get(reg[0], []):
                    p = ops[j]
                    same = p["e"] == o["e"] and p["k"] == "c" and o["k"] == "c"
                    if same and o["info"] is not None and o["info"] is p["info"]:
                        continue
                    if (wrote or writes or reg[1] == -1 and not same) and meets(reg, other):
                        lag = 0 if same and reg[1] == -1 else p.get("lag", SIGNAL)
                        d[j] = max(d.get(j, 0), lag)
            before.append(d)
            for reg, writes in touched(o):
                seen.setdefault(reg[0], []).append((i, reg, writes))
        ORDER.extend(issue_order([o["e"] for o in ops], [o["c"] for o in ops],
                                 [o.get("lag", 0) for o in ops], before, [o.get("first", 0) for o in ops]))
    ops = [ops[i] for i in ORDER]

    seen, need = {}, []
    for i, o in enumerate(ops):
        if o["k"] == "x":
            o["rd"] = []
        elif o["info"] is not None:
            o["info"].append(o)
        best = {}
        for reg, writes in touched(o):
            bank = reg[1] == -1
            for j, other, wrote in seen.get(reg[0], []):
                p = ops[j]
                same = p["e"] == o["e"] and p["k"] == "c" and o["k"] == "c"
                if same and bank:
                    continue
                if (wrote or writes or bank) and meets(reg, other):
                    key = p["e"] if p["k"] == "c" else j
                    best[key] = max(best.get(key, -1), j)
        need.append(sorted(best.values(), reverse=True))
        for reg, writes in touched(o):
            seen.setdefault(reg[0], []).append((i, reg, writes))
    known, after, waits = {}, {}, []
    for i, o in enumerate(ops):
        k, w = known.setdefault(o["e"], {}), []
        for j in need[i]:
            key = ops[j]["e"] if ops[j]["k"] == "c" else j
            if k.get(key, -1) < j:
                w.append(j)
                k[key] = j
                for kk, jj in after[j].items():
                    k[kk] = max(k.get(kk, -1), jj)
        waits.append(w)
        after[i] = dict(k) if o["k"] != "x" else {}
    used = set(j for w in waits for j in w)
    queue = {"V": V, "S": S, "P": P, "G": g, "Y": g.sync}
    token, count, waited, ndma = {}, {}, {}, [0]
    for i, o in enumerate(ops):
        if o["k"] == "x":
            token[i] = o["info"]
            count[o["info"][0]] = o["info"][1]
            continue
        q = queue[o["e"]]
        for j in waits[i]:
            s, c = token[j]
            q.wait_ge(T.sem[s], c)
            waited[s] = max(waited.get(s, 0), c)
        ins = o["fn"]()
        if o["k"] == "d":
            s = "d%d" % ndma[0]
            ndma[0] += 1
            ins.then_inc(T.sem[s], 16)
            token[i] = (s, 16)
            count[s] = 16
        elif o["k"] == "c" and i in used:
            s = "e" + o["e"]
            count[s] = count.get(s, 0) + 1
            ins.then_inc(T.sem[s], 1)
            token[i] = (s, count[s])
    count["sent"] = 2 * NENG * R
    for s in sorted(count):
        if waited.get(s, 0) < count[s]:
            g.wait_ge(T.sem[s], count[s])
